import numpy as np
import ml_dtypes


def mxq(x, axis, fmt="e4m3"):
    dtype, down = {"e4m3": (ml_dtypes.float8_e4m3fn, 7), "e5m2": (ml_dtypes.float8_e5m2, 14)}[fmt]
    v = np.moveaxis(np.asarray(x, np.float32).astype(ml_dtypes.bfloat16).astype(np.float64), axis, -1)
    blocks = v.reshape(v.shape[:-1] + (-1, 32))
    amax = np.abs(blocks).max(-1, keepdims=True)
    byte = np.maximum(np.where(amax > 0, np.frexp(amax)[1] - 1 + 127, 0) - down, 1)
    scale = np.exp2(byte - 127.0)
    codes = (blocks / scale).astype(np.float32).astype(dtype).astype(np.float64)
    return np.moveaxis((codes * scale).reshape(v.shape), -1, axis)


WIDE = False


def mx_kscale(k):
    if not WIDE:
        return np.ones(k)
    levels = np.array([10, -10, 5, -5, 0])
    if k % 512:
        return np.exp2(np.random.permutation(np.resize(levels, k // 32))).repeat(32)
    a = np.empty((k // 512, 16))
    for p in range(k // 512):
        a[p, :8] = np.random.permutation(np.resize(levels, 8))
        for g in range(8):
            far = levels[np.abs(levels - a[p, g]) >= 10]
            a[p, g + 8] = far[np.random.randint(len(far))]
    return np.exp2(a.ravel()).repeat(32)


def f64(x):
    return np.asarray(x).astype(np.float64)


def striped(idx):
    return np.tile(idx.reshape(-1, 16).T, (8, 1)).astype(np.uint16)


def unstriped(offs):
    return offs[:16].T.reshape(-1).astype(np.int64)


def pack_weight(w):
    k, n = w.shape
    w = f64(np.asarray(w, np.float32).astype(ml_dtypes.bfloat16)).reshape(k // 32, 32, n)
    amax = np.abs(w).max(1)
    byte = np.clip(np.where(amax > 0, np.frexp(amax)[1] - 1 + 127 - 7, 1), 1, 254)
    scaled = (w * np.exp2(127.0 - byte)[:, None, :]).reshape(k, n).astype(np.float32)
    words = np.ascontiguousarray(scaled.reshape(k // 512, 128, 4, n).transpose(0, 1, 3, 2)).astype(ml_dtypes.float8_e4m3fn).view(np.uint8)
    return words, np.ascontiguousarray(byte.astype(np.uint8).reshape(k // 512, 16, n))


def unpack_weight(words, scales):
    g, p, n, _ = words.shape
    vals = np.ascontiguousarray(words).view(ml_dtypes.float8_e4m3fn).astype(np.float64) * np.repeat(np.exp2(scales.astype(np.float64) - 127.0), 8, axis=1)[..., None]
    return vals.transpose(0, 1, 3, 2).reshape(g * 512, n)


E2M1 = np.array([0.0, 0.5, 1.0, 1.5, 2.0, 3.0, 4.0, 6.0, -0.0, -0.5, -1.0, -1.5, -2.0, -3.0, -4.0, -6.0])


def pack_fp4(w):
    k, n = w.shape
    w = f64(np.asarray(w, np.float32).astype(ml_dtypes.bfloat16)).reshape(k // 32, 32, n)
    amax = np.abs(w).max(1)
    mant, ex = np.frexp(amax / 6.0)
    byte = np.clip(np.where(amax > 0, np.where(mant > 0.5, ex, ex - 1) + 127, 1), 1, 254)
    scaled = (w * np.exp2(127.0 - byte)[:, None, :]).reshape(k, n).astype(np.float32)
    c = np.ascontiguousarray(scaled.reshape(k // 512, 128, 4, n).transpose(0, 1, 3, 2)).astype(ml_dtypes.float4_e2m1fn).view(np.uint8) & 0xF
    words = (c[..., 0::2] | (c[..., 1::2] << 4)).reshape(k // 512, 128, 2 * n)
    return np.ascontiguousarray(words), np.ascontiguousarray(byte.astype(np.uint8).reshape(k // 512, 16, n))


def unpack_fp4(words, scales):
    g, _, n = scales.shape
    words = np.ascontiguousarray(words).reshape(g, 128, n, 2)
    nib = np.empty((g, 128, n, 4), np.uint8)
    nib[..., 0::2] = words & 0xF
    nib[..., 1::2] = words >> 4
    vals = E2M1[nib] * np.repeat(np.exp2(scales.astype(np.float64) - 127.0), 8, axis=1)[..., None]
    return vals.transpose(0, 1, 3, 2).reshape(g * 512, n)


K, T, S, H, N, U = 1024, 2048, 512, 512, 128, 1024


def setup_inputs():
    n = np.random.standard_normal
    s = mx_kscale(K)[:, None]
    u = mx_kscale(H)
    packed_xT = pack_weight(n((K, T)) * s)
    packed_w2 = pack_fp4(n((H, N)) / np.sqrt(H) / u[:, None])
    return {
        "x_words": packed_xT[0],
        "x_scales": packed_xT[1],
        "w1": (n((K, H)) / np.sqrt(K) / s * u).astype(np.float32),
        "w2_words": packed_w2[0],
        "w2_scales": packed_w2[1],
        "skip": (n((H, U)) * u[:, None]).astype(np.float32),
        "offs": striped(np.random.permutation(T)[:S]),
        "cell": striped(np.random.permutation(U)[:S]),
    }


def reference(x_words, x_scales, w1, w2_words, w2_scales, skip, offs, cell):
    xq = unpack_weight(x_words, x_scales)[:, unstriped(offs)]
    up = np.zeros((H, U))
    up[:, unstriped(cell)] = mxq(f64(w1), 0, "e4m3").T @ xq
    z = up + f64(skip)
    return unpack_fp4(w2_words, w2_scales).T @ mxq(z, 0, "e4m3")

@@ -1,0 +1,155 @@
+from contextlib import ExitStack
+
+import concourse.mybir as mybir
+
+K, T, S, H, N, U = 1024, 2048, 512, 512, 128, 1024
+FLOPS = 2 * K * H * S + 2 * H * N * U
+
+F32 = mybir.dt.float32
+BF16 = mybir.dt.bfloat16
+I32 = mybir.dt.int32
+U32 = mybir.dt.uint32
+U16 = mybir.dt.uint16
+U8 = mybir.dt.uint8
+FP8X4 = mybir.dt.float8_e4m3fn_x4
+FP4X4 = mybir.dt.float4_e2m1fn_x4
+ADD = mybir.AluOpType.add
+
+P = 128
+PACK = 4
+PASSES = K // (P * PACK)
+HALF = S // 2
+CHUNK = 256
+CHUNKS = U // CHUNK
+
+
+def tile_picked_unet_none_p_kernel(
+    tc, x_words, x_scales, w1, w2_words, w2_scales, skip, offs, cell, out
+):
+    nc = tc.nc
+    with ExitStack() as ctx:
+        sb = ctx.enter_context(tc.tile_pool(name="sb", bufs=1))
+        ps = ctx.enter_context(tc.psum_pool(name="ps", bufs=1))
+
+        offs_t = sb.tile([P, S // 16], U16, name="offs_t")
+        cell_t = sb.tile([P, S // 16], U16, name="cell_t")
+        xs = sb.tile([P, T], U8, name="xs", align_bytes=64)
+        w2s = sb.tile([P, N], U8, name="w2s", align_bytes=64)
+        w2w = sb.tile([P, 2 * N], U8, name="w2w", align_bytes=64)
+        xw = [sb.tile([P, T], I32, name="xw%d" % g, align_bytes=64) for g in range(PASSES)]
+        w1raw = [sb.tile([P, PACK, H], F32, name="w1raw%d" % g, align_bytes=64) for g in range(PASSES)]
+        skip_t = [sb.tile([P, U], F32, name="skip%d" % t, align_bytes=64) for t in range(PACK)]
+        up = [sb.tile([P, U], F32, name="up%d" % t, align_bytes=64) for t in range(PACK)]
+
+        nc.gpsimd.memset(xs[:].bitcast(I32), 0)
+        nc.sync.dma_start(offs_t[:], offs)
+        w1_rows = w1.rearrange("(g p j) c -> g p j c", p=P, j=PACK)
+        nc.sync.dma_start(out=w1raw[0][:], in_=w1_rows[0])
+        for q in range(4):
+            nc.sync.dma_start(
+                out=xs[32 * q : 32 * q + 4 * PASSES, :].bitcast(I32),
+                in_=x_scales[:, 4 * q : 4 * q + 4, :].bitcast(I32),
+            )
+        nc.sync.dma_start(out=xw[0][:], in_=x_words[0].rearrange("p n t -> p (n t)").bitcast(I32))
+        nc.sync.dma_start(out=w1raw[1][:], in_=w1_rows[1])
+        nc.sync.dma_start(out=xw[1][:], in_=x_words[1].rearrange("p n t -> p (n t)").bitcast(I32))
+        nc.sync.dma_start(cell_t[:], cell)
+        skip_rows = skip.rearrange("(p t) v -> p t v", t=PACK)
+        for t in range(PACK):
+            nc.sync.dma_start(out=skip_t[t][:], in_=skip_rows[:, t, :])
+        nc.gpsimd.memset(w2s[:].bitcast(I32), 0)
+        nc.sync.dma_start(out=w2w[:].bitcast(I32), in_=w2_words[0].bitcast(I32))
+        for q in range(4):
+            nc.sync.dma_start(
+                out=w2s[32 * q : 32 * q + 4, :].bitcast(I32),
+                in_=w2_scales[0, 4 * q : 4 * q + 4, :].bitcast(I32),
+            )
+        for t in range(PACK):
+            nc.gpsimd.memset(up[t][:], 0.0)
+
+        xsg = sb.tile([P, S], U8, name="xsg", align_bytes=64)
+        nc.vector.tensor_copy(xsg[:], xs[:].indirect(offs_t[:]))
+
+        w1c = []
+        w1s = []
+        xg = [sb.tile([P, S], U32, name="xg%d" % g, align_bytes=64) for g in range(PASSES)]
+        for g in range(PASSES):
+            grouped = sb.tile([P, PACK, P, PACK], BF16, name="w1g%d" % g, align_bytes=64)
+            src = w1raw[g][:].rearrange("p j (m t) -> p m t j", t=PACK)
+            dst = grouped[:].rearrange("p t m j -> p m t j")
+            nc.scalar.copy(dst[:, 0:64], src[:, 0:64])
+            nc.vector.tensor_copy(dst[:, 64:128], src[:, 64:128])
+            codes = sb.tile([P, H], U32, name="w1c%d" % g, align_bytes=64)
+            scales = sb.tile([P, H], U8, name="w1s%d" % g, align_bytes=64)
+            nc.vector.quantize_mx(out=codes[:].bitcast(FP8X4), scales=scales[:], in_=grouped[:].rearrange("p t m j -> p (t m j)"))
+            w1c.append(codes)
+            w1s.append(scales)
+            if g == 0:
+                nc.vector.tensor_copy(xg[0][:], xw[0][:].bitcast(U32).indirect(offs_t[:]))
+
+
+        def product(bank, t, g, cols):
+            nc.tensor.matmul_mx(
+                out=bank,
+                lhsT=w1c[g][:, P * t : P * (t + 1)].bitcast(FP8X4),
+                lhsT_scale=w1s[g][:, P * t : P * (t + 1)],
+                rhs=xg[g][:, cols].bitcast(FP8X4),
+                rhs_scale=xsg[4 * g : P, cols],
+                start=(g == 0),
+                stop=(g == PASSES - 1),
+            )
+
+        halves = [slice(0, HALF), slice(HALF, S)]
+        first = [ps.tile([P, HALF], F32, name="first%d" % a) for a in range(2)]
+        rest = [ps.tile([P, S], F32, name="rest%d" % t) for t in range(1, PACK)]
+        for a in range(2):
+            product(first[a][:], 0, 0, halves[a])
+        for t in range(1, PACK):
+            product(rest[t - 1][:], t, 0, slice(0, S))
+
+        h = [sb.tile([P, S], F32, name="h%d" % t, align_bytes=64) for t in range(PACK)]
+        for a in range(2):
+            nc.vector.tensor_copy(xg[1][:, halves[a]], xw[1][:].bitcast(U32).indirect(offs_t[:, 16 * a : 16 * (a + 1)]))
+        for a in range(2):
+            product(first[a][:], 0, 1, halves[a])
+            nc.scalar.copy(h[0][:, halves[a]], first[a][:])
+        for t in range(1, PACK):
+            product(rest[t - 1][:], t, 1, slice(0, S))
+            nc.scalar.copy(h[t][:], rest[t - 1][:])
+
+        low = sb.tile([P, 2, U], BF16, name="low", align_bytes=64)
+        high = [sb.tile([P, 2, CHUNK], BF16, name="high%d" % c, align_bytes=64) for c in range(CHUNKS)]
+        z = [sb.tile([P, CHUNK, PACK], BF16, name="z%d" % c, align_bytes=64) for c in range(CHUNKS)]
+        chunk = [slice(CHUNK * c, CHUNK * (c + 1)) for c in range(CHUNKS)]
+
+        for a in range(2):
+            nc.vector.tensor_copy(up[0][:].indirect(cell_t[:, 16 * a : 16 * (a + 1)]), h[0][:, halves[a]])
+        for t in range(1, PACK):
+            nc.vector.tensor_copy(up[t][:].indirect(cell_t[:]), h[t][:])
+
+        for t in range(2):
+            nc.gpsimd.tensor_tensor(low[:, t, :], up[t][:], skip_t[t][:], ADD)
+        for c in range(CHUNKS):
+            nc.scalar.copy(z[c][:, :, 0:2], low[:, :, chunk[c]].rearrange("p e v -> p v e"))
+        for c in range(CHUNKS):
+            nc.gpsimd.tensor_tensor(high[c][:, 0, :], up[2][:, chunk[c]], skip_t[2][:, chunk[c]], ADD)
+        for c in range(CHUNKS):
+            nc.vector.tensor_tensor(high[c][:, 1, :], up[3][:, chunk[c]], skip_t[3][:, chunk[c]], ADD)
+        for c in range(CHUNKS):
+            if c < 2:
+                nc.scalar.copy(z[c][:, :, 2:4], high[c][:].rearrange("p e v -> p v e"))
+            else:
+                nc.vector.tensor_copy(z[c][:, :, 2:4], high[c][:].rearrange("p e v -> p v e"))
+
+        for i, c in enumerate((0, 2, 3, 1)):
+            zc = sb.tile([P, CHUNK], U32, name="zc%d" % c, align_bytes=64)
+            zs = sb.tile([P, CHUNK], U8, name="zs%d" % c, align_bytes=64)
+            nc.vector.quantize_mx(out=zc[:].bitcast(FP8X4), scales=zs[:], in_=z[c][:].rearrange("p v t -> p (v t)"))
+            acc = ps.tile([P, CHUNK], F32, name="acc%d" % (i % 3))
+            nc.tensor.matmul_mx(
+                out=acc[:], lhsT=w2w[:].bitcast(FP4X4), lhsT_scale=w2s[:],
+                rhs=zc[:].bitcast(FP8X4), rhs_scale=zs[:], start=True, stop=True,
+            )
+            res = sb.tile([P, CHUNK], F32, name="res%d" % c, align_bytes=64)
+            nc.scalar.copy(res[:], acc[:])
+            nc.sync.dma_start(out=out[:, chunk[c]], in_=res[:])

@@ -21,6 +21,7 @@ PASSES = K // (P * PACK)
 HALF = S // 2
 CHUNK = 256
 CHUNKS = U // CHUNK
+HP = P // 2
 
 
 def tile_picked_unet_none_p_kernel(
@@ -31,32 +32,42 @@ def tile_picked_unet_none_p_kernel(
         sb = ctx.enter_context(tc.tile_pool(name="sb", bufs=1))
         ps = ctx.enter_context(tc.psum_pool(name="ps", bufs=1))
 
+        def tile(shape, dtype, name):
+            return sb.tile(shape, dtype, name=name, align_bytes=64)
+
         offs_t = sb.tile([P, S // 16], U16, name="offs_t")
         cell_t = sb.tile([P, S // 16], U16, name="cell_t")
-        xs = sb.tile([P, T], U8, name="xs", align_bytes=64)
-        w2s = sb.tile([P, N], U8, name="w2s", align_bytes=64)
-        w2w = sb.tile([P, 2 * N], U8, name="w2w", align_bytes=64)
-        xw = [sb.tile([P, T], I32, name="xw%d" % g, align_bytes=64) for g in range(PASSES)]
-        w1raw = [sb.tile([P, PACK, H], F32, name="w1raw%d" % g, align_bytes=64) for g in range(PASSES)]
-        skip_t = [sb.tile([P, U], F32, name="skip%d" % t, align_bytes=64) for t in range(PACK)]
-        up = [sb.tile([P, U], F32, name="up%d" % t, align_bytes=64) for t in range(PACK)]
+        xs = tile([P, T], U8, "xs")
+        w2s = tile([P, N], U8, "w2s")
+        w2w = tile([P, 2 * N], U8, "w2w")
+        xw = [tile([P, T], I32, "xw%d" % g) for g in range(PASSES)]
+        w1raw = [[tile([P, PACK, H // 2], F32, "w1raw%d%d" % (g, a)) for a in range(2)] for g in range(PASSES)]
+        skip_t = [tile([P, U], F32, "skip%d" % t) for t in range(PACK)]
+        up = [tile([P, U], F32, "up%d" % t) for t in range(PACK)]
 
+        w1_rows = w1.rearrange("(g p j) (a c) -> g a p j c", p=P, j=PACK, a=2)
         nc.gpsimd.memset(xs[:].bitcast(I32), 0)
+        nc.sync.dma_start(out=w1raw[0][0][:], in_=w1_rows[0, 0])
         nc.sync.dma_start(offs_t[:], offs)
-        w1_rows = w1.rearrange("(g p j) c -> g p j c", p=P, j=PACK)
-        nc.sync.dma_start(out=w1raw[0][:], in_=w1_rows[0])
         for q in range(4):
             nc.sync.dma_start(
                 out=xs[32 * q : 32 * q + 4 * PASSES, :].bitcast(I32),
                 in_=x_scales[:, 4 * q : 4 * q + 4, :].bitcast(I32),
             )
-        nc.sync.dma_start(out=xw[0][:], in_=x_words[0].rearrange("p n t -> p (n t)").bitcast(I32))
-        nc.sync.dma_start(out=w1raw[1][:], in_=w1_rows[1])
-        nc.sync.dma_start(out=xw[1][:], in_=x_words[1].rearrange("p n t -> p (n t)").bitcast(I32))
+        for g in range(PASSES):
+            nc.sync.dma_start(out=xw[g][:], in_=x_words[g].rearrange("p n t -> p (n t)").bitcast(I32))
+        nc.sync.dma_start(out=w1raw[1][0][:], in_=w1_rows[1, 0])
         nc.sync.dma_start(cell_t[:], cell)
+        for g in range(PASSES):
+            nc.sync.dma_start(out=w1raw[g][1][:], in_=w1_rows[g, 1])
+        skip_pairs = skip.rearrange("(a m t) v -> a m t v", a=2, t=PACK)
         skip_rows = skip.rearrange("(p t) v -> p t v", t=PACK)
-        for t in range(PACK):
+        for a in range(2):
+            nc.sync.dma_start(out=skip_t[a][:], in_=skip_pairs[a, :, 0:2, :])
+        for t in range(2, PACK):
             nc.sync.dma_start(out=skip_t[t][:], in_=skip_rows[:, t, :])
+        for t in range(PACK):
+            nc.gpsimd.memset(up[t][:], 0.0)
         nc.gpsimd.memset(w2s[:].bitcast(I32), 0)
         nc.sync.dma_start(out=w2w[:].bitcast(I32), in_=w2_words[0].bitcast(I32))
         for q in range(4):
@@ -64,92 +75,124 @@ def tile_picked_unet_none_p_kernel(
                 out=w2s[32 * q : 32 * q + 4, :].bitcast(I32),
                 in_=w2_scales[0, 4 * q : 4 * q + 4, :].bitcast(I32),
             )
-        for t in range(PACK):
-            nc.gpsimd.memset(up[t][:], 0.0)
 
-        xsg = sb.tile([P, S], U8, name="xsg", align_bytes=64)
-        nc.vector.tensor_copy(xsg[:], xs[:].indirect(offs_t[:]))
+        xsg = tile([P, S], U8, "xsg")
+        xg = [tile([P, S], U32, "xg%d" % g) for g in range(PASSES)]
+        pair_in = [[tile([P, HP, 2, PACK], BF16, "pair_in%d%d" % (g, a)) for a in range(2)] for g in range(PASSES)]
+        rest_in = [tile([P, 2, P, PACK], BF16, "rest_in%d" % g) for g in range(PASSES)]
+        codes = {}
+        scales = {}
 
-        w1c = []
-        w1s = []
-        xg = [sb.tile([P, S], U32, name="xg%d" % g, align_bytes=64) for g in range(PASSES)]
-        for g in range(PASSES):
-            grouped = sb.tile([P, PACK, P, PACK], BF16, name="w1g%d" % g, align_bytes=64)
-            src = w1raw[g][:].rearrange("p j (m t) -> p m t j", t=PACK)
-            dst = grouped[:].rearrange("p t m j -> p m t j")
-            nc.scalar.copy(dst[:, 0:64], src[:, 0:64])
-            nc.vector.tensor_copy(dst[:, 64:128], src[:, 64:128])
-            codes = sb.tile([P, H], U32, name="w1c%d" % g, align_bytes=64)
-            scales = sb.tile([P, H], U8, name="w1s%d" % g, align_bytes=64)
-            nc.vector.quantize_mx(out=codes[:].bitcast(FP8X4), scales=scales[:], in_=grouped[:].rearrange("p t m j -> p (t m j)"))
-            w1c.append(codes)
-            w1s.append(scales)
-            if g == 0:
-                nc.vector.tensor_copy(xg[0][:], xw[0][:].bitcast(U32).indirect(offs_t[:]))
+        def cast(copy, dst, src):
+            copy(dst, src)
 
+        def cast_pair(copy, g, a):
+            src = w1raw[g][a][:].rearrange("p j (m t) -> p m t j", t=PACK)
+            copy(pair_in[g][a][:], src[:, :, 0:2, :])
+
+        def cast_rest(copy, g, a):
+            src = w1raw[g][a][:].rearrange("p j (m t) -> p m t j", t=PACK)
+            copy(rest_in[g][:, :, HP * a : HP * (a + 1), :].rearrange("p t m j -> p m t j"), src[:, :, 2:4, :])
+
+        def quantise_pair(g, a):
+            c = tile([P, P], U32, "pc%d%d" % (g, a))
+            s = tile([P, P], U8, "ps%d%d" % (g, a))
+            nc.vector.quantize_mx(out=c[:].bitcast(FP8X4), scales=s[:], in_=pair_in[g][a][:].rearrange("p m e j -> p (m e j)"))
+            codes[g, a] = c[:]
+            scales[g, a] = s[:]
+
+        def quantise_rest(g):
+            c = tile([P, 2 * P], U32, "rc%d" % g)
+            s = tile([P, 2 * P], U8, "rs%d" % g)
+            nc.vector.quantize_mx(out=c[:].bitcast(FP8X4), scales=s[:], in_=rest_in[g][:].rearrange("p t m j -> p (t m j)"))
+            for t in range(2):
+                codes[g, 2 + t] = c[:, P * t : P * (t + 1)]
+                scales[g, 2 + t] = s[:, P * t : P * (t + 1)]
 
         def product(bank, t, g, cols):
             nc.tensor.matmul_mx(
-                out=bank,
-                lhsT=w1c[g][:, P * t : P * (t + 1)].bitcast(FP8X4),
-                lhsT_scale=w1s[g][:, P * t : P * (t + 1)],
-                rhs=xg[g][:, cols].bitcast(FP8X4),
-                rhs_scale=xsg[4 * g : P, cols],
-                start=(g == 0),
-                stop=(g == PASSES - 1),
+                out=bank, lhsT=codes[g, t].bitcast(FP8X4), lhsT_scale=scales[g, t],
+                rhs=xg[g][:, cols].bitcast(FP8X4), rhs_scale=xsg[4 * g : P, cols],
+                start=(g == 0), stop=(g == PASSES - 1),
             )
 
         halves = [slice(0, HALF), slice(HALF, S)]
-        first = [ps.tile([P, HALF], F32, name="first%d" % a) for a in range(2)]
-        rest = [ps.tile([P, S], F32, name="rest%d" % t) for t in range(1, PACK)]
-        for a in range(2):
-            product(first[a][:], 0, 0, halves[a])
-        for t in range(1, PACK):
-            product(rest[t - 1][:], t, 0, slice(0, S))
+        bank = [[ps.tile([P, HALF], F32, name="bank%d%d" % (a, b)) for b in range(2)] for a in range(2)]
+        wide = [ps.tile([P, S], F32, name="wide%d" % t) for t in range(2)]
 
-        h = [sb.tile([P, S], F32, name="h%d" % t, align_bytes=64) for t in range(PACK)]
-        for a in range(2):
-            nc.vector.tensor_copy(xg[1][:, halves[a]], xw[1][:].bitcast(U32).indirect(offs_t[:, 16 * a : 16 * (a + 1)]))
-        for a in range(2):
-            product(first[a][:], 0, 1, halves[a])
-            nc.scalar.copy(h[0][:, halves[a]], first[a][:])
-        for t in range(1, PACK):
-            product(rest[t - 1][:], t, 1, slice(0, S))
-            nc.scalar.copy(h[t][:], rest[t - 1][:])
-
-        low = sb.tile([P, 2, U], BF16, name="low", align_bytes=64)
-        high = [sb.tile([P, 2, CHUNK], BF16, name="high%d" % c, align_bytes=64) for c in range(CHUNKS)]
-        z = [sb.tile([P, CHUNK, PACK], BF16, name="z%d" % c, align_bytes=64) for c in range(CHUNKS)]
-        chunk = [slice(CHUNK * c, CHUNK * (c + 1)) for c in range(CHUNKS)]
-
-        for a in range(2):
-            nc.vector.tensor_copy(up[0][:].indirect(cell_t[:, 16 * a : 16 * (a + 1)]), h[0][:, halves[a]])
+        nc.vector.tensor_copy(xsg[:], xs[:].indirect(offs_t[:]))
+        cast_pair(nc.scalar.copy, 0, 0)
+        cast_rest(nc.scalar.copy, 0, 0)
+        quantise_pair(0, 0)
+        for g in range(PASSES):
+            nc.vector.tensor_copy(xg[g][:], xw[g][:].bitcast(U32).indirect(offs_t[:]))
+        for b in range(2):
+            product(bank[0][b][:], 0, 0, halves[b])
+        cast_pair(nc.vector.tensor_copy, 1, 0)
+        cast_rest(nc.scalar.copy, 1, 0)
+        quantise_pair(1, 0)
+        for b in range(2):
+            product(bank[0][b][:], 0, 1, halves[b])
+        cast_pair(nc.vector.tensor_copy, 0, 1)
+        cast_rest(nc.scalar.copy, 0, 1)
+        h_first = tile([P, HALF], F32, "w1raw01")
+        nc.scalar.copy(h_first[:], bank[0][0][:])
+        quantise_pair(0, 1)
+        quantise_rest(0)
+        for b in range(2):
+            product(bank[1][b][:], 1, 0, halves[b])
+        nc.vector.tensor_copy(up[0][:].indirect(cell_t[:, 0:16]), h_first[:])
+        cast_pair(nc.scalar.copy, 1, 1)
+        cast_rest(nc.scalar.copy, 1, 1)
+        h_second = tile([P, HALF], F32, "w1raw11")
+        nc.scalar.copy(h_second[:], bank[0][1][:])
+        quantise_pair(1, 1)
+        quantise_rest(1)
+        nc.vector.tensor_copy(up[0][:].indirect(cell_t[:, 16:32]), h_second[:])
+        h = {t: tile([P, S], F32, "h%d" % t) for t in range(1, PACK)}
+        for b in range(2):
+            product(bank[1][b][:], 1, 1, halves[b])
+            nc.scalar.copy(h[1][:, halves[b]], bank[1][b][:])
+        for t in range(2, PACK):
+            for g in range(PASSES):
+                product(wide[t - 2][:], t, g, slice(0, S))
+            nc.scalar.copy(h[t][:], wide[t - 2][:])
         for t in range(1, PACK):
             nc.vector.tensor_copy(up[t][:].indirect(cell_t[:]), h[t][:])
 
-        for t in range(2):
-            nc.gpsimd.tensor_tensor(low[:, t, :], up[t][:], skip_t[t][:], ADD)
-        for c in range(CHUNKS):
-            nc.scalar.copy(z[c][:, :, 0:2], low[:, :, chunk[c]].rearrange("p e v -> p v e"))
-        for c in range(CHUNKS):
-            nc.gpsimd.tensor_tensor(high[c][:, 0, :], up[2][:, chunk[c]], skip_t[2][:, chunk[c]], ADD)
-        for c in range(CHUNKS):
-            nc.vector.tensor_tensor(high[c][:, 1, :], up[3][:, chunk[c]], skip_t[3][:, chunk[c]], ADD)
-        for c in range(CHUNKS):
-            if c < 2:
-                nc.scalar.copy(z[c][:, :, 2:4], high[c][:].rearrange("p e v -> p v e"))
-            else:
-                nc.vector.tensor_copy(z[c][:, :, 2:4], high[c][:].rearrange("p e v -> p v e"))
+        chunk = [slice(CHUNK * c, CHUNK * (c + 1)) for c in range(CHUNKS)]
+        double = [slice(2 * CHUNK * c, 2 * CHUNK * (c + 1)) for c in range(2)]
+        high = tile([P, 2, U], BF16, "high")
+        low = [tile([P, U], BF16, "low")[:], high[:, 1, :]]
+        z = [tile([P, CHUNK, PACK], BF16, "z%d" % c) for c in range(CHUNKS)]
 
-        for i, c in enumerate((0, 2, 3, 1)):
-            zc = sb.tile([P, CHUNK], U32, name="zc%d" % c, align_bytes=64)
-            zs = sb.tile([P, CHUNK], U8, name="zs%d" % c, align_bytes=64)
-            nc.vector.quantize_mx(out=zc[:].bitcast(FP8X4), scales=zs[:], in_=z[c][:].rearrange("p v t -> p (v t)"))
-            acc = ps.tile([P, CHUNK], F32, name="acc%d" % (i % 3))
+        for a in range(2):
+            for d in range(2):
+                zp = tile([P, 2 * CHUNK], BF16, "zp%d%d" % (a, d))
+                nc.gpsimd.tensor_tensor(zp[:], up[a][:, double[d]], skip_t[a][:, double[d]], ADD)
+                nc.sync.dma_start(out=low[d][HP * a : HP * (a + 1), :], in_=zp[:])
+        for c in range(CHUNKS):
+            src = low[c // 2].rearrange("p (e v) -> p v e", e=2)
+            nc.scalar.copy(z[c][:, :, 0:2], src[:, chunk[c % 2], :])
+        nc.gpsimd.tensor_tensor(high[:, 0, :], up[2][:], skip_t[2][:], ADD)
+        for c in (0, 2, 1, 3):
+            nc.vector.tensor_tensor(high[:, 1, chunk[c]], up[3][:, chunk[c]], skip_t[3][:, chunk[c]], ADD)
+        for c in (0, 2):
+            nc.scalar.copy(z[c][:, :, 2:4], high[:, :, chunk[c]].rearrange("p e v -> p v e"))
+        for c in (1, 3):
+            nc.vector.tensor_copy(z[c][:, :, 2:4], high[:, :, chunk[c]].rearrange("p e v -> p v e"))
+
+        pieces = [(0, 0, CHUNK), (1, 0, CHUNK), (2, 0, CHUNK), (3, 0, P), (3, P, P)]
+        names = ["bank00", "bank01", "bank10", "bank11", "wide0"]
+        for i, (c, v0, w) in enumerate(pieces):
+            zc = tile([P, w], U32, "zc%d" % i)
+            zs = tile([P, w], U8, "zs%d" % i)
+            nc.vector.quantize_mx(out=zc[:].bitcast(FP8X4), scales=zs[:], in_=z[c][:, v0 : v0 + w, :].rearrange("p v t -> p (v t)"))
+            acc = ps.tile([P, w], F32, name=names[i])
             nc.tensor.matmul_mx(
                 out=acc[:], lhsT=w2w[:].bitcast(FP4X4), lhsT_scale=w2s[:],
                 rhs=zc[:].bitcast(FP8X4), rhs_scale=zs[:], start=True, stop=True,
             )
-            res = sb.tile([P, CHUNK], F32, name="res%d" % c, align_bytes=64)
+            res = tile([P, w], F32, "res%d" % i)
             nc.scalar.copy(res[:], acc[:])
-            nc.sync.dma_start(out=out[:, chunk[c]], in_=res[:])
+            nc.sync.dma_start(out=out[:, CHUNK * c + v0 : CHUNK * c + v0 + w], in_=res[:])

@@ -1,6 +1,7 @@
 from contextlib import ExitStack
 
 import concourse.mybir as mybir
+from concourse.masks import make_identity
 
 K, T, S, H, N, U = 1024, 2048, 512, 512, 128, 1024
 FLOPS = 2 * K * H * S + 2 * H * N * U
@@ -49,12 +50,12 @@ def tile_picked_unet_none_p_kernel(
         nc.gpsimd.memset(xs[:].bitcast(I32), 0)
         nc.sync.dma_start(out=w1raw[0][0][:], in_=w1_rows[0, 0])
         nc.sync.dma_start(offs_t[:], offs)
-        for q in range(4):
-            nc.sync.dma_start(
-                out=xs[32 * q : 32 * q + 4 * PASSES, :].bitcast(I32),
-                in_=x_scales[:, 4 * q : 4 * q + 4, :].bitcast(I32),
-            )
         for g in range(PASSES):
+            for r in range(4):
+                nc.sync.dma_start(
+                    out=xs[4 * g + r : P : 32, :].bitcast(I32),
+                    in_=x_scales[g, r:16:4, :].bitcast(I32),
+                )
             nc.sync.dma_start(out=xw[g][:], in_=x_words[g].rearrange("p n t -> p (n t)").bitcast(I32))
         nc.sync.dma_start(out=w1raw[1][0][:], in_=w1_rows[1, 0])
         nc.sync.dma_start(cell_t[:], cell)
@@ -69,6 +70,8 @@ def tile_picked_unet_none_p_kernel(
         for t in range(PACK):
             nc.gpsimd.memset(up[t][:], 0.0)
         nc.gpsimd.memset(w2s[:].bitcast(I32), 0)
+        ident = tile([P, P], F32, "ident")
+        make_identity(nc, ident[:])
         nc.sync.dma_start(out=w2w[:].bitcast(I32), in_=w2_words[0].bitcast(I32))
         for q in range(4):
             nc.sync.dma_start(
@@ -87,12 +90,12 @@ def tile_picked_unet_none_p_kernel(
             copy(dst, src)
 
         def cast_pair(copy, g, a):
-            src = w1raw[g][a][:].rearrange("p j (m t) -> p m t j", t=PACK)
-            copy(pair_in[g][a][:], src[:, :, 0:2, :])
+            src = w1raw[g][a][:].rearrange("p j (m t) -> p m j t", t=PACK)
+            copy(pair_in[g][a][:].rearrange("p m e j -> p m j e"), src[:, :, :, 0:2])
 
         def cast_rest(copy, g, a):
-            src = w1raw[g][a][:].rearrange("p j (m t) -> p m t j", t=PACK)
-            copy(rest_in[g][:, :, HP * a : HP * (a + 1), :].rearrange("p t m j -> p m t j"), src[:, :, 2:4, :])
+            src = w1raw[g][a][:].rearrange("p j (m t) -> p m j t", t=PACK)
+            copy(rest_in[g][:, :, HP * a : HP * (a + 1), :].rearrange("p t m j -> p m j t"), src[:, :, :, 2:4])
 
         def quantise_pair(g, a):
             c = tile([P, P], U32, "pc%d%d" % (g, a))
@@ -163,17 +166,28 @@ def tile_picked_unet_none_p_kernel(
         chunk = [slice(CHUNK * c, CHUNK * (c + 1)) for c in range(CHUNKS)]
         double = [slice(2 * CHUNK * c, 2 * CHUNK * (c + 1)) for c in range(2)]
         high = tile([P, 2, U], BF16, "high")
-        low = [tile([P, U], BF16, "low")[:], high[:, 1, :]]
+        turned = [tile([P, U], BF16, "turned")[:], high[:, 1, :]]
         z = [tile([P, CHUNK, PACK], BF16, "z%d" % c) for c in range(CHUNKS)]
 
         for a in range(2):
+            sums = [ps.tile([P, 4, P], F32, name="bank%d%d" % (a, d)) for d in range(2)]
+            for first, src in ((True, skip_t[a]), (False, up[a])):
+                for d in range(2):
+                    for j in range(4):
+                        v0 = P * (4 * d + j)
+                        nc.tensor.matmul(
+                            sums[d][:, j, :], lhsT=src[:, v0 : v0 + P], rhs=ident[:], is_transpose=True,
+                            start=(first and j == 0), stop=(not first and j == 3),
+                        )
             for d in range(2):
-                zp = tile([P, 2 * CHUNK], BF16, "zp%d%d" % (a, d))
-                nc.gpsimd.tensor_tensor(zp[:], up[a][:, double[d]], skip_t[a][:, double[d]], ADD)
-                nc.sync.dma_start(out=low[d][HP * a : HP * (a + 1), :], in_=zp[:])
-        for c in range(CHUNKS):
-            src = low[c // 2].rearrange("p (e v) -> p v e", e=2)
-            nc.scalar.copy(z[c][:, :, 0:2], src[:, chunk[c % 2], :])
+                nc.scalar.copy(turned[d].rearrange("p (j q) -> p j q", j=4)[:, :, P * a : P * (a + 1)], sums[d][:])
+        for d in range(2):
+            back = ps.tile([P, 4, P], F32, name="back%d" % d)
+            for j in range(4):
+                nc.tensor.transpose(back[:, j, :], turned[d][:, 2 * P * j : 2 * P * (j + 1)].bitcast(F32), ident[:])
+            for c in range(2):
+                words = z[2 * d + c][:].rearrange("p v t -> p (v t)").bitcast(F32).rearrange("p (v u) -> p v u", u=2)
+                nc.scalar.copy(words[:, :, 0], back[:, 2 * c : 2 * c + 2, :].rearrange("p j v -> p (j v)"))
         nc.gpsimd.tensor_tensor(high[:, 0, :], up[2][:], skip_t[2][:], ADD)
         for c in (0, 2, 1, 3):
             nc.vector.tensor_tensor(high[:, 1, chunk[c]], up[3][:, chunk[c]], skip_t[3][:, chunk[c]], ADD)
@@ -183,7 +197,7 @@ def tile_picked_unet_none_p_kernel(
             nc.vector.tensor_copy(z[c][:, :, 2:4], high[:, :, chunk[c]].rearrange("p e v -> p v e"))
 
         pieces = [(0, 0, CHUNK), (1, 0, CHUNK), (2, 0, CHUNK), (3, 0, P), (3, P, P)]
-        names = ["bank00", "bank01", "bank10", "bank11", "wide0"]
+        names = ["wide0", "wide1", "bank00", "bank01", "bank10"]
         for i, (c, v0, w) in enumerate(pieces):
             zc = tile([P, w], U32, "zc%d" % i)
             zs = tile([P, w], U8, "zs%d" % i)
@@ -195,4 +209,5 @@ def tile_picked_unet_none_p_kernel(
             )
             res = tile([P, w], F32, "res%d" % i)
             nc.scalar.copy(res[:], acc[:])
-            nc.sync.dma_start(out=out[:, CHUNK * c + v0 : CHUNK * c + v0 + w], in_=res[:])
+            queue = nc.scalar if i == len(pieces) - 1 else nc.sync
+            queue.dma_start(out=out[:, CHUNK * c + v0 : CHUNK * c + v0 + w], in_=res[:])

@@ -170,7 +170,7 @@ def tile_picked_unet_none_p_kernel(
         z = [tile([P, CHUNK, PACK], BF16, "z%d" % c) for c in range(CHUNKS)]
 
         for a in range(2):
-            sums = [ps.tile([P, 4, P], F32, name="bank%d%d" % (a, d)) for d in range(2)]
+            sums = [ps.tile([P, 4, P], F32, name=("wide%d", "bank1%d")[a] % d) for d in range(2)]
             for first, src in ((True, skip_t[a]), (False, up[a])):
                 for d in range(2):
                     for j in range(4):
@@ -197,7 +197,7 @@ def tile_picked_unet_none_p_kernel(
             nc.vector.tensor_copy(z[c][:, :, 2:4], high[:, :, chunk[c]].rearrange("p e v -> p v e"))
 
         pieces = [(0, 0, CHUNK), (1, 0, CHUNK), (2, 0, CHUNK), (3, 0, P), (3, P, P)]
-        names = ["wide0", "wide1", "bank00", "bank01", "bank10"]
+        names = ["bank00", "bank01", "wide0", "wide1", "bank10"]
         for i, (c, v0, w) in enumerate(pieces):
             zc = tile([P, w], U32, "zc%d" % i)
             zs = tile([P, w], U8, "zs%d" % i)

@@ -14,7 +14,6 @@ U16 = mybir.dt.uint16
 U8 = mybir.dt.uint8
 FP8X4 = mybir.dt.float8_e4m3fn_x4
 FP4X4 = mybir.dt.float4_e2m1fn_x4
-ADD = mybir.AluOpType.add
 
 P = 128
 PACK = 4
@@ -23,6 +22,8 @@ HALF = S // 2
 CHUNK = 256
 CHUNKS = U // CHUNK
 HP = P // 2
+QP = P // 4
+BACK = (0, 1, 0, 0)
 
 
 def tile_picked_unet_none_p_kernel(
@@ -42,31 +43,44 @@ def tile_picked_unet_none_p_kernel(
         w2s = tile([P, N], U8, "w2s")
         w2w = tile([P, 2 * N], U8, "w2w")
         xw = [tile([P, T], I32, "xw%d" % g) for g in range(PASSES)]
-        w1raw = [[tile([P, PACK, H // 2], F32, "w1raw%d%d" % (g, a)) for a in range(2)] for g in range(PASSES)]
+        cols = [slice(0, P), slice(P, 2 * P), slice(2 * P, H)]
+        width = [P, P, 2 * P]
+        w1raw = [[tile([P, PACK, width[a]], F32, "w1raw%d%d" % (a, g)) for g in range(PASSES)] for a in range(3)]
         skip_t = [tile([P, U], F32, "skip%d" % t) for t in range(PACK)]
         up = [tile([P, U], F32, "up%d" % t) for t in range(PACK)]
 
-        w1_rows = w1.rearrange("(g p j) (a c) -> g a p j c", p=P, j=PACK, a=2)
-        nc.gpsimd.memset(xs[:].bitcast(I32), 0)
-        nc.sync.dma_start(out=w1raw[0][0][:], in_=w1_rows[0, 0])
-        nc.sync.dma_start(offs_t[:], offs)
-        for g in range(PASSES):
+        w1_rows = w1.rearrange("(g p j) c -> g p j c", p=P, j=PACK)
+
+        def load_w1(a, g):
+            nc.sync.dma_start(out=w1raw[a][g][:], in_=w1_rows[g, :, :, cols[a]])
+
+        def load_scales(g):
             for r in range(4):
                 nc.sync.dma_start(
                     out=xs[4 * g + r : P : 32, :].bitcast(I32),
                     in_=x_scales[g, r:16:4, :].bitcast(I32),
                 )
+
+        def load_x(g):
             nc.sync.dma_start(out=xw[g][:], in_=x_words[g].rearrange("p n t -> p (n t)").bitcast(I32))
-        nc.sync.dma_start(out=w1raw[1][0][:], in_=w1_rows[1, 0])
+
+        nc.gpsimd.memset(xs[:].bitcast(I32), 0)
+        load_w1(0, 0)
+        nc.sync.dma_start(offs_t[:], offs)
+        load_scales(0)
+        load_x(0)
+        load_scales(1)
+        load_w1(0, 1)
+        load_x(1)
         nc.sync.dma_start(cell_t[:], cell)
-        for g in range(PASSES):
-            nc.sync.dma_start(out=w1raw[g][1][:], in_=w1_rows[g, 1])
-        skip_pairs = skip.rearrange("(a m t) v -> a m t v", a=2, t=PACK)
-        skip_rows = skip.rearrange("(p t) v -> p t v", t=PACK)
+        for a in range(1, 3):
+            for g in range(PASSES):
+                load_w1(a, g)
         for a in range(2):
-            nc.sync.dma_start(out=skip_t[a][:], in_=skip_pairs[a, :, 0:2, :])
-        for t in range(2, PACK):
-            nc.sync.dma_start(out=skip_t[t][:], in_=skip_rows[:, t, :])
+            nc.sync.dma_start(out=skip_t[a][:], in_=skip[P * a : P * (a + 1), :])
+        skip_pairs = skip[2 * P : H, :].rearrange("(m t) v -> m t v", t=PACK)
+        for u in range(2):
+            nc.sync.dma_start(out=skip_t[2 + u][:], in_=skip_pairs[:, 2 * u : 2 * u + 2, :])
         for t in range(PACK):
             nc.gpsimd.memset(up[t][:], 0.0)
         nc.gpsimd.memset(w2s[:].bitcast(I32), 0)
@@ -81,123 +95,142 @@ def tile_picked_unet_none_p_kernel(
 
         xsg = tile([P, S], U8, "xsg")
         xg = [tile([P, S], U32, "xg%d" % g) for g in range(PASSES)]
-        pair_in = [[tile([P, HP, 2, PACK], BF16, "pair_in%d%d" % (g, a)) for a in range(2)] for g in range(PASSES)]
-        rest_in = [tile([P, 2, P, PACK], BF16, "rest_in%d" % g) for g in range(PASSES)]
+        rounded = [[tile([P, width[a], PACK], BF16, "rounded%d%d" % (a, g)) for g in range(PASSES)] for a in range(3)]
         codes = {}
         scales = {}
 
-        def cast(copy, dst, src):
-            copy(dst, src)
+        def round_w1(a, g):
+            if a < 2:
+                src = w1raw[a][g][:].rearrange("p j (m t) -> p m j t", t=PACK)
+                dst = rounded[a][g][:].rearrange("p (m t) j -> p m j t", t=PACK)
+            else:
+                src = w1raw[a][g][:].rearrange("p j (m u e) -> p m j u e", u=2, e=2)
+                dst = rounded[a][g][:].rearrange("p (u m e) j -> p m j u e", u=2, e=2)
+            nc.scalar.copy(dst, src)
 
-        def cast_pair(copy, g, a):
-            src = w1raw[g][a][:].rearrange("p j (m t) -> p m j t", t=PACK)
-            copy(pair_in[g][a][:].rearrange("p m e j -> p m j e"), src[:, :, :, 0:2])
+        def quantise_w1(a, g):
+            c = tile([P, width[a]], U32, "wc%d%d" % (a, g))
+            s = tile([P, width[a]], U8, "ws%d%d" % (a, g))
+            nc.vector.quantize_mx(out=c[:].bitcast(FP8X4), scales=s[:], in_=rounded[a][g][:].rearrange("p c j -> p (c j)"))
+            for i in range(width[a] // P):
+                codes[a + i, g] = c[:, P * i : P * (i + 1)]
+                scales[a + i, g] = s[:, P * i : P * (i + 1)]
 
-        def cast_rest(copy, g, a):
-            src = w1raw[g][a][:].rearrange("p j (m t) -> p m j t", t=PACK)
-            copy(rest_in[g][:, :, HP * a : HP * (a + 1), :].rearrange("p t m j -> p m j t"), src[:, :, :, 2:4])
+        halves = [slice(0, HALF), slice(HALF, S)]
+        lists = [slice(0, HALF // 16), slice(HALF // 16, S // 16)]
 
-        def quantise_pair(g, a):
-            c = tile([P, P], U32, "pc%d%d" % (g, a))
-            s = tile([P, P], U8, "ps%d%d" % (g, a))
-            nc.vector.quantize_mx(out=c[:].bitcast(FP8X4), scales=s[:], in_=pair_in[g][a][:].rearrange("p m e j -> p (m e j)"))
-            codes[g, a] = c[:]
-            scales[g, a] = s[:]
-
-        def quantise_rest(g):
-            c = tile([P, 2 * P], U32, "rc%d" % g)
-            s = tile([P, 2 * P], U8, "rs%d" % g)
-            nc.vector.quantize_mx(out=c[:].bitcast(FP8X4), scales=s[:], in_=rest_in[g][:].rearrange("p t m j -> p (t m j)"))
-            for t in range(2):
-                codes[g, 2 + t] = c[:, P * t : P * (t + 1)]
-                scales[g, 2 + t] = s[:, P * t : P * (t + 1)]
-
-        def product(bank, t, g, cols):
+        def product(bank, t, g, b):
             nc.tensor.matmul_mx(
-                out=bank, lhsT=codes[g, t].bitcast(FP8X4), lhsT_scale=scales[g, t],
-                rhs=xg[g][:, cols].bitcast(FP8X4), rhs_scale=xsg[4 * g : P, cols],
+                out=bank[:], lhsT=codes[t, g].bitcast(FP8X4), lhsT_scale=scales[t, g],
+                rhs=xg[g][:, halves[b]].bitcast(FP8X4), rhs_scale=xsg[4 * g : P, halves[b]],
                 start=(g == 0), stop=(g == PASSES - 1),
             )
 
-        halves = [slice(0, HALF), slice(HALF, S)]
-        bank = [[ps.tile([P, HALF], F32, name="bank%d%d" % (a, b)) for b in range(2)] for a in range(2)]
-        wide = [ps.tile([P, S], F32, name="wide%d" % t) for t in range(2)]
+        def banks(name, shape):
+            return [ps.tile(shape, F32, name="%s%d" % (name, d)) for d in range(2)]
 
-        nc.vector.tensor_copy(xsg[:], xs[:].indirect(offs_t[:]))
-        cast_pair(nc.scalar.copy, 0, 0)
-        cast_rest(nc.scalar.copy, 0, 0)
-        quantise_pair(0, 0)
-        for g in range(PASSES):
-            nc.vector.tensor_copy(xg[g][:], xw[g][:].bitcast(U32).indirect(offs_t[:]))
-        for b in range(2):
-            product(bank[0][b][:], 0, 0, halves[b])
-        cast_pair(nc.vector.tensor_copy, 1, 0)
-        cast_rest(nc.scalar.copy, 1, 0)
-        quantise_pair(1, 0)
-        for b in range(2):
-            product(bank[0][b][:], 0, 1, halves[b])
-        cast_pair(nc.vector.tensor_copy, 0, 1)
-        cast_rest(nc.scalar.copy, 0, 1)
-        h_first = tile([P, HALF], F32, "w1raw01")
-        nc.scalar.copy(h_first[:], bank[0][0][:])
-        quantise_pair(0, 1)
-        quantise_rest(0)
-        for b in range(2):
-            product(bank[1][b][:], 1, 0, halves[b])
-        nc.vector.tensor_copy(up[0][:].indirect(cell_t[:, 0:16]), h_first[:])
-        cast_pair(nc.scalar.copy, 1, 1)
-        cast_rest(nc.scalar.copy, 1, 1)
-        h_second = tile([P, HALF], F32, "w1raw11")
-        nc.scalar.copy(h_second[:], bank[0][1][:])
-        quantise_pair(1, 1)
-        quantise_rest(1)
-        nc.vector.tensor_copy(up[0][:].indirect(cell_t[:, 16:32]), h_second[:])
-        h = {t: tile([P, S], F32, "h%d" % t) for t in range(1, PACK)}
-        for b in range(2):
-            product(bank[1][b][:], 1, 1, halves[b])
-            nc.scalar.copy(h[1][:, halves[b]], bank[1][b][:])
-        for t in range(2, PACK):
-            for g in range(PASSES):
-                product(wide[t - 2][:], t, g, slice(0, S))
-            nc.scalar.copy(h[t][:], wide[t - 2][:])
-        for t in range(1, PACK):
-            nc.vector.tensor_copy(up[t][:].indirect(cell_t[:]), h[t][:])
+        def turn(dst, src, start, stop):
+            nc.tensor.matmul(dst, lhsT=src, rhs=ident[:], is_transpose=True, start=start, stop=stop)
 
-        chunk = [slice(CHUNK * c, CHUNK * (c + 1)) for c in range(CHUNKS)]
-        double = [slice(2 * CHUNK * c, 2 * CHUNK * (c + 1)) for c in range(2)]
-        high = tile([P, 2, U], BF16, "high")
-        turned = [tile([P, U], BF16, "turned")[:], high[:, 1, :]]
-        z = [tile([P, CHUNK, PACK], BF16, "z%d" % c) for c in range(CHUNKS)]
+        zt = tile([P, 2 * U], F32, "zt")
+        zt_values = zt[:].bitcast(BF16).rearrange("p (u j d m e) -> p u j d m e", u=2, j=4, d=2, e=2)
 
-        for a in range(2):
-            sums = [ps.tile([P, 4, P], F32, name=("wide%d", "bank1%d")[a] % d) for d in range(2)]
-            for first, src in ((True, skip_t[a]), (False, up[a])):
+        def add_and_turn(t, name):
+            sums = banks(name, [P, 4, P])
+            for first, src in ((True, skip_t[t]), (False, up[t])):
                 for d in range(2):
                     for j in range(4):
-                        v0 = P * (4 * d + j)
-                        nc.tensor.matmul(
-                            sums[d][:, j, :], lhsT=src[:, v0 : v0 + P], rhs=ident[:], is_transpose=True,
-                            start=(first and j == 0), stop=(not first and j == 3),
-                        )
+                        v0 = P * (2 * j + d)
+                        turn(sums[d][:, j, :], src[:, v0 : v0 + P], first and j == 0, not first and j == 3)
             for d in range(2):
-                nc.scalar.copy(turned[d].rearrange("p (j q) -> p j q", j=4)[:, :, P * a : P * (a + 1)], sums[d][:])
+                if t < 2:
+                    nc.scalar.copy(
+                        zt_values[:, :, :, d, QP * t : QP * (t + 1), :],
+                        sums[d][:].rearrange("p j (m u e) -> p u j m e", u=2, e=2),
+                    )
+                else:
+                    nc.scalar.copy(zt_values[:, 0, :, d, HP:P, :], sums[d][:].rearrange("p j (m e) -> p j m e", e=2))
+
+        nc.vector.tensor_copy(xsg[:], xs[:].indirect(offs_t[:]))
+        round_w1(0, 0)
+        quantise_w1(0, 0)
+        nc.vector.tensor_copy(xg[0][:], xw[0][:].bitcast(U32).indirect(offs_t[:]))
+        first = banks("tail", [P, HALF])
+        for b in range(2):
+            product(first[b], 0, 0, b)
+        round_w1(0, 1)
+        quantise_w1(0, 1)
+        for b in range(2):
+            nc.vector.tensor_copy(xg[1][:, halves[b]], xw[1][:].bitcast(U32).indirect(offs_t[:, lists[b]]))
+            product(first[b], 0, 1, b)
+
+        h = tile([P, HALF], F32, "h00")
+        nc.scalar.copy(h[:], first[0][:])
+        nc.vector.tensor_copy(up[0][:].indirect(cell_t[:, lists[0]]), h[:])
+        second = banks("a", [P, HALF])
+        for g in range(PASSES):
+            round_w1(1, g)
+            quantise_w1(1, g)
+            for b in range(2):
+                product(second[b], 1, g, b)
+        h = tile([P, HALF], F32, "w1raw11")
+        nc.scalar.copy(h[:], first[1][:])
+        nc.vector.tensor_copy(up[0][:].indirect(cell_t[:, lists[1]]), h[:])
+        h = tile([P, HALF], F32, "h10")
+        nc.scalar.copy(h[:], second[0][:])
+        nc.vector.tensor_copy(up[1][:].indirect(cell_t[:, lists[0]]), h[:])
+        third = banks("b", [P, HALF])
+        for g in range(PASSES):
+            round_w1(2, g)
+            quantise_w1(2, g)
+            for b in range(2):
+                product(third[b], 2, g, b)
+        h = tile([P, HALF], F32, "w1raw21")
+        nc.scalar.copy(h[:], second[1][:])
+        nc.vector.tensor_copy(up[1][:].indirect(cell_t[:, lists[1]]), h[:])
+        h = tile([P, S], F32, "h2")
+        for b in range(2):
+            nc.scalar.copy(h[:, halves[b]], third[b][:])
+        nc.vector.tensor_copy(up[2][:].indirect(cell_t[:]), h[:])
+        add_and_turn(0, "a")
+        fourth = banks("a", [P, HALF])
+        h = tile([P, S], F32, "h3")
+        for b in range(2):
+            for g in range(PASSES):
+                product(fourth[b], 3, g, b)
+            nc.scalar.copy(h[:, halves[b]], fourth[b][:])
+        nc.vector.tensor_copy(up[3][:].indirect(cell_t[:]), h[:])
+        add_and_turn(1, "b")
+
+        tail = [ps.tile([P, 2, CHUNK], F32, name="tail%d" % c) for c in range(CHUNKS)]
+
+        def block(src, base, c, d):
+            v0 = base + P * (2 * c + d)
+            return src[:, v0 : v0 + P]
+
+        for c in range(CHUNKS):
+            for d in range(2):
+                turn(tail[c][:, 1, P * d : P * (d + 1)], block(skip_t[3], 0, c, d), d == 0, False)
+        add_and_turn(2, "a")
         for d in range(2):
-            back = ps.tile([P, 4, P], F32, name="back%d" % d)
-            for j in range(4):
-                nc.tensor.transpose(back[:, j, :], turned[d][:, 2 * P * j : 2 * P * (j + 1)].bitcast(F32), ident[:])
-            for c in range(2):
-                words = z[2 * d + c][:].rearrange("p v t -> p (v t)").bitcast(F32).rearrange("p (v u) -> p v u", u=2)
-                nc.scalar.copy(words[:, :, 0], back[:, 2 * c : 2 * c + 2, :].rearrange("p j v -> p (j v)"))
-        nc.gpsimd.tensor_tensor(high[:, 0, :], up[2][:], skip_t[2][:], ADD)
-        for c in (0, 2, 1, 3):
-            nc.vector.tensor_tensor(high[:, 1, chunk[c]], up[3][:, chunk[c]], skip_t[3][:, chunk[c]], ADD)
-        for c in (0, 2):
-            nc.scalar.copy(z[c][:, :, 2:4], high[:, :, chunk[c]].rearrange("p e v -> p v e"))
-        for c in (1, 3):
-            nc.vector.tensor_copy(z[c][:, :, 2:4], high[:, :, chunk[c]].rearrange("p e v -> p v e"))
+            for c in range(CHUNKS):
+                turn(tail[c][:, 0, P * d : P * (d + 1)], block(zt, 0, c, d), False, False)
+        for c in range(CHUNKS):
+            for d in range(2):
+                turn(tail[c][:, 1, P * d : P * (d + 1)], block(up[3], 0, c, d), False, d == 1)
+
+        copy_of = [nc.scalar.copy, nc.vector.tensor_copy]
+        for c in range(CHUNKS):
+            copy_of[c % 2](zt_values[:, 1, c, :, HP:P, :], tail[c][:, 1, :].rearrange("p (d m e) -> p d m e", d=2, e=2))
+        z = [tile([P, CHUNK, PACK], BF16, "z%d" % c) for c in range(CHUNKS)]
+        for c in range(CHUNKS):
+            for d in range(2):
+                turn(tail[c][:, 1, P * d : P * (d + 1)], block(zt, U, c, d), True, True)
+            words = z[c][:].rearrange("p v t -> p (v t)").bitcast(F32).rearrange("p (v u) -> p v u", u=2)
+            copy_of[BACK[c]](words, tail[c][:].rearrange("p u v -> p v u"))
 
         pieces = [(0, 0, CHUNK), (1, 0, CHUNK), (2, 0, CHUNK), (3, 0, P), (3, P, P)]
-        names = ["bank00", "bank01", "wide0", "wide1", "bank10"]
+        names = ["b0", "b1", "a0", "a1", "tail0"]
         for i, (c, v0, w) in enumerate(pieces):
             zc = tile([P, w], U32, "zc%d" % i)
             zs = tile([P, w], U8, "zs%d" % i)

@@ -24,6 +24,8 @@ CHUNKS = U // CHUNK
 HP = P // 2
 QP = P // 4
 BACK = (0, 1, 0, 0)
+OUT = (0, 0, 1, 0, 0)
+ROW0, STEP = 11, 7
 
 
 def tile_picked_unet_none_p_kernel(
@@ -39,61 +41,40 @@ def tile_picked_unet_none_p_kernel(
 
         offs_t = sb.tile([P, S // 16], U16, name="offs_t")
         cell_t = sb.tile([P, S // 16], U16, name="cell_t")
-        xs = tile([P, T], U8, "xs")
-        w2s = tile([P, N], U8, "w2s")
-        w2w = tile([P, 2 * N], U8, "w2w")
+        xs = tile([P, PASSES, T], U8, "xs")
+        xsg = tile([P, PASSES, S], U8, "xsg")
+        xsm = tile([P, PASSES, S], U8, "xsm")
         xw = [tile([P, T], I32, "xw%d" % g) for g in range(PASSES)]
         cols = [slice(0, P), slice(P, 2 * P), slice(2 * P, H)]
         width = [P, P, 2 * P]
-        w1raw = [[tile([P, PACK, width[a]], F32, "w1raw%d%d" % (a, g)) for g in range(PASSES)] for a in range(3)]
-        skip_t = [tile([P, U], F32, "skip%d" % t) for t in range(PACK)]
+        w1raw = {(0, g): tile([P, PACK, P], F32, "w1raw0%d" % g)[:] for g in range(PASSES)}
         up = [tile([P, U], F32, "up%d" % t) for t in range(PACK)]
 
         w1_rows = w1.rearrange("(g p j) c -> g p j c", p=P, j=PACK)
 
         def load_w1(a, g):
-            nc.sync.dma_start(out=w1raw[a][g][:], in_=w1_rows[g, :, :, cols[a]])
-
-        def load_scales(g):
-            for r in range(4):
-                nc.sync.dma_start(
-                    out=xs[4 * g + r : P : 32, :].bitcast(I32),
-                    in_=x_scales[g, r:16:4, :].bitcast(I32),
-                )
+            nc.sync.dma_start(out=w1raw[a, g], in_=w1_rows[g, :, :, cols[a]])
 
         def load_x(g):
             nc.sync.dma_start(out=xw[g][:], in_=x_words[g].rearrange("p n t -> p (n t)").bitcast(I32))
 
-        nc.gpsimd.memset(xs[:].bitcast(I32), 0)
+        nc.gpsimd.memset(xs[:].rearrange("p g n -> p (g n)").bitcast(I32), 0)
         load_w1(0, 0)
         nc.sync.dma_start(offs_t[:], offs)
-        load_scales(0)
+        nc.sync.dma_start(
+            out=xs[ROW0 : ROW0 + 15 * STEP + 1 : STEP, :, :].bitcast(I32),
+            in_=x_scales.rearrange("g q n -> q g n").bitcast(I32),
+        )
+        nc.sync.dma_start(cell_t[:], cell)
         load_x(0)
-        load_scales(1)
         load_w1(0, 1)
         load_x(1)
-        nc.sync.dma_start(cell_t[:], cell)
-        for a in range(1, 3):
-            for g in range(PASSES):
-                load_w1(a, g)
-        for a in range(2):
-            nc.sync.dma_start(out=skip_t[a][:], in_=skip[P * a : P * (a + 1), :])
-        skip_pairs = skip[2 * P : H, :].rearrange("(m t) v -> m t v", t=PACK)
-        for u in range(2):
-            nc.sync.dma_start(out=skip_t[2 + u][:], in_=skip_pairs[:, 2 * u : 2 * u + 2, :])
+        nc.gpsimd.memset(xsm[:].rearrange("p g n -> p (g n)").bitcast(I32), 0)
         for t in range(PACK):
-            nc.gpsimd.memset(up[t][:], 0.0)
-        nc.gpsimd.memset(w2s[:].bitcast(I32), 0)
+            (nc.vector if t < 2 else nc.gpsimd).memset(up[t][:], 0.0)
         ident = tile([P, P], F32, "ident")
         make_identity(nc, ident[:])
-        nc.sync.dma_start(out=w2w[:].bitcast(I32), in_=w2_words[0].bitcast(I32))
-        for q in range(4):
-            nc.sync.dma_start(
-                out=w2s[32 * q : 32 * q + 4, :].bitcast(I32),
-                in_=w2_scales[0, 4 * q : 4 * q + 4, :].bitcast(I32),
-            )
 
-        xsg = tile([P, S], U8, "xsg")
         xg = [tile([P, S], U32, "xg%d" % g) for g in range(PASSES)]
         rounded = [[tile([P, width[a], PACK], BF16, "rounded%d%d" % (a, g)) for g in range(PASSES)] for a in range(3)]
         codes = {}
@@ -101,10 +82,10 @@ def tile_picked_unet_none_p_kernel(
 
         def round_w1(a, g):
             if a < 2:
-                src = w1raw[a][g][:].rearrange("p j (m t) -> p m j t", t=PACK)
+                src = w1raw[a, g].rearrange("p j (m t) -> p m j t", t=PACK)
                 dst = rounded[a][g][:].rearrange("p (m t) j -> p m j t", t=PACK)
             else:
-                src = w1raw[a][g][:].rearrange("p j (m u e) -> p m j u e", u=2, e=2)
+                src = w1raw[a, g].rearrange("p j (m u e) -> p m j u e", u=2, e=2)
                 dst = rounded[a][g][:].rearrange("p (u m e) j -> p m j u e", u=2, e=2)
             nc.scalar.copy(dst, src)
 
@@ -119,11 +100,11 @@ def tile_picked_unet_none_p_kernel(
         halves = [slice(0, HALF), slice(HALF, S)]
         lists = [slice(0, HALF // 16), slice(HALF // 16, S // 16)]
 
-        def product(bank, t, g, b):
+        def product(bank, t, g, b, opens=0):
             nc.tensor.matmul_mx(
                 out=bank[:], lhsT=codes[t, g].bitcast(FP8X4), lhsT_scale=scales[t, g],
-                rhs=xg[g][:, halves[b]].bitcast(FP8X4), rhs_scale=xsg[4 * g : P, halves[b]],
-                start=(g == 0), stop=(g == PASSES - 1),
+                rhs=xg[g][:, halves[b]].bitcast(FP8X4), rhs_scale=xsm[:, g, halves[b]],
+                start=(g == opens), stop=(g != opens),
             )
 
         def banks(name, shape):
@@ -151,18 +132,48 @@ def tile_picked_unet_none_p_kernel(
                 else:
                     nc.scalar.copy(zt_values[:, 0, :, d, HP:P, :], sums[d][:].rearrange("p j (m e) -> p j m e", e=2))
 
-        nc.vector.tensor_copy(xsg[:], xs[:].indirect(offs_t[:]))
+        for g in range(PASSES):
+            nc.vector.tensor_copy(xsg[:, g, :], xs[:, g, :].indirect(offs_t[:]))
+        for r in range(4):
+            row = ROW0 + STEP * r
+            nc.sync.dma_start(
+                out=xsm[r:P:32, :, :].rearrange("p g n -> p (g n)").bitcast(I32),
+                in_=xsg[row : row + 12 * STEP + 1 : 4 * STEP, :, :].rearrange("p g n -> p (g n)").bitcast(I32),
+            )
+        late = tile([P, PASSES * PACK * P], F32, "xs")
+        for g in range(PASSES):
+            w1raw[1, g] = late[:, PACK * P * g : PACK * P * (g + 1)].rearrange("p (j c) -> p j c", j=PACK)
+            load_w1(1, g)
         round_w1(0, 0)
         quantise_w1(0, 0)
         nc.vector.tensor_copy(xg[0][:], xw[0][:].bitcast(U32).indirect(offs_t[:]))
-        first = banks("tail", [P, HALF])
-        for b in range(2):
-            product(first[b], 0, 0, b)
+        late = tile([P, PASSES * PACK * 2 * P], F32, "xw0")
+        for g in range(PASSES):
+            w1raw[2, g] = late[:, PACK * 2 * P * g : PACK * 2 * P * (g + 1)].rearrange("p (j c) -> p j c", j=PACK)
+            load_w1(2, g)
         round_w1(0, 1)
         quantise_w1(0, 1)
+        skip_all = tile([P, PACK, U], F32, "w1raw01")
+        skip_t = [skip_all[:, t, :] for t in range(PACK)]
+        for a in range(2):
+            nc.sync.dma_start(out=skip_t[a], in_=skip[P * a : P * (a + 1), :])
+        skip_pairs = skip[2 * P : H, :].rearrange("(m t) v -> m t v", t=PACK)
+        for u in range(2):
+            nc.sync.dma_start(out=skip_t[2 + u], in_=skip_pairs[:, 2 * u : 2 * u + 2, :])
+        w2s = tile([P, N], U8, "rounded01")
+        nc.gpsimd.memset(w2s[:].bitcast(I32), 0)
+        w2w = tile([P, 2 * N], U8, "xsg")
+        nc.sync.dma_start(out=w2w[:].bitcast(I32), in_=w2_words[0].bitcast(I32))
+        for q in range(4):
+            nc.sync.dma_start(
+                out=w2s[32 * q : 32 * q + 4, :].bitcast(I32),
+                in_=w2_scales[0, 4 * q : 4 * q + 4, :].bitcast(I32),
+            )
+        first = banks("tail", [P, HALF])
         for b in range(2):
             nc.vector.tensor_copy(xg[1][:, halves[b]], xw[1][:].bitcast(U32).indirect(offs_t[:, lists[b]]))
-            product(first[b], 0, 1, b)
+            for g in (b, 1 - b):
+                product(first[b], 0, g, b, opens=b)
 
         h = tile([P, HALF], F32, "h00")
         nc.scalar.copy(h[:], first[0][:])
@@ -173,7 +184,7 @@ def tile_picked_unet_none_p_kernel(
             quantise_w1(1, g)
             for b in range(2):
                 product(second[b], 1, g, b)
-        h = tile([P, HALF], F32, "w1raw11")
+        h = tile([P, HALF], F32, "xs")
         nc.scalar.copy(h[:], first[1][:])
         nc.vector.tensor_copy(up[0][:].indirect(cell_t[:, lists[1]]), h[:])
         h = tile([P, HALF], F32, "h10")
@@ -185,7 +196,7 @@ def tile_picked_unet_none_p_kernel(
             quantise_w1(2, g)
             for b in range(2):
                 product(third[b], 2, g, b)
-        h = tile([P, HALF], F32, "w1raw21")
+        h = tile([P, HALF], F32, "xw0")
         nc.scalar.copy(h[:], second[1][:])
         nc.vector.tensor_copy(up[1][:].indirect(cell_t[:, lists[1]]), h[:])
         h = tile([P, S], F32, "h2")
@@ -241,6 +252,6 @@ def tile_picked_unet_none_p_kernel(
                 rhs=zc[:].bitcast(FP8X4), rhs_scale=zs[:], start=True, stop=True,
             )
             res = tile([P, w], F32, "res%d" % i)
-            nc.scalar.copy(res[:], acc[:])
+            copy_of[OUT[i]](res[:], acc[:])
             queue = nc.scalar if i == len(pieces) - 1 else nc.sync
             queue.dma_start(out=out[:, CHUNK * c + v0 : CHUNK * c + v0 + w], in_=res[:])

@@ -24,7 +24,7 @@ CHUNKS = U // CHUNK
 HP = P // 2
 QP = P // 4
 BACK = (0, 1, 0, 0)
-OUT = (0, 0, 1, 0, 0)
+OUT = (0, 1, 0, 1, 0)
 ROW0, STEP = 11, 7
 
 
@@ -41,7 +41,7 @@ def tile_picked_unet_none_p_kernel(
 
         offs_t = sb.tile([P, S // 16], U16, name="offs_t")
         cell_t = sb.tile([P, S // 16], U16, name="cell_t")
-        xs = tile([P, PASSES, T], U8, "xs")
+        xs = [tile([P, T], U8, "xs%d" % g) for g in range(PASSES)]
         xsg = tile([P, PASSES, S], U8, "xsg")
         xsm = tile([P, PASSES, S], U8, "xsm")
         xw = [tile([P, T], I32, "xw%d" % g) for g in range(PASSES)]
@@ -58,16 +58,20 @@ def tile_picked_unet_none_p_kernel(
         def load_x(g):
             nc.sync.dma_start(out=xw[g][:], in_=x_words[g].rearrange("p n t -> p (n t)").bitcast(I32))
 
-        nc.gpsimd.memset(xs[:].rearrange("p g n -> p (g n)").bitcast(I32), 0)
+        def load_scales(g):
+            nc.gpsimd.memset(xs[g][:].bitcast(I32), 0)
+            nc.sync.dma_start(
+                out=xs[g][ROW0 : ROW0 + 15 * STEP + 1 : STEP, :].bitcast(I32),
+                in_=x_scales[g].bitcast(I32),
+            )
+
         load_w1(0, 0)
         nc.sync.dma_start(offs_t[:], offs)
-        nc.sync.dma_start(
-            out=xs[ROW0 : ROW0 + 15 * STEP + 1 : STEP, :, :].bitcast(I32),
-            in_=x_scales.rearrange("g q n -> q g n").bitcast(I32),
-        )
+        load_scales(0)
         nc.sync.dma_start(cell_t[:], cell)
-        load_x(0)
         load_w1(0, 1)
+        load_scales(1)
+        load_x(0)
         load_x(1)
         nc.gpsimd.memset(xsm[:].rearrange("p g n -> p (g n)").bitcast(I32), 0)
         for t in range(PACK):
@@ -133,14 +137,14 @@ def tile_picked_unet_none_p_kernel(
                     nc.scalar.copy(zt_values[:, 0, :, d, HP:P, :], sums[d][:].rearrange("p j (m e) -> p j m e", e=2))
 
         for g in range(PASSES):
-            nc.vector.tensor_copy(xsg[:, g, :], xs[:, g, :].indirect(offs_t[:]))
+            nc.vector.tensor_copy(xsg[:, g, :], xs[g][:].indirect(offs_t[:]))
         for r in range(4):
             row = ROW0 + STEP * r
             nc.sync.dma_start(
                 out=xsm[r:P:32, :, :].rearrange("p g n -> p (g n)").bitcast(I32),
                 in_=xsg[row : row + 12 * STEP + 1 : 4 * STEP, :, :].rearrange("p g n -> p (g n)").bitcast(I32),
             )
-        late = tile([P, PASSES * PACK * P], F32, "xs")
+        late = tile([P, PASSES * PACK * P], F32, "xs1")
         for g in range(PASSES):
             w1raw[1, g] = late[:, PACK * P * g : PACK * P * (g + 1)].rearrange("p (j c) -> p j c", j=PACK)
             load_w1(1, g)
@@ -153,13 +157,6 @@ def tile_picked_unet_none_p_kernel(
             load_w1(2, g)
         round_w1(0, 1)
         quantise_w1(0, 1)
-        skip_all = tile([P, PACK, U], F32, "w1raw01")
-        skip_t = [skip_all[:, t, :] for t in range(PACK)]
-        for a in range(2):
-            nc.sync.dma_start(out=skip_t[a], in_=skip[P * a : P * (a + 1), :])
-        skip_pairs = skip[2 * P : H, :].rearrange("(m t) v -> m t v", t=PACK)
-        for u in range(2):
-            nc.sync.dma_start(out=skip_t[2 + u], in_=skip_pairs[:, 2 * u : 2 * u + 2, :])
         w2s = tile([P, N], U8, "rounded01")
         nc.gpsimd.memset(w2s[:].bitcast(I32), 0)
         w2w = tile([P, 2 * N], U8, "xsg")
@@ -175,6 +172,13 @@ def tile_picked_unet_none_p_kernel(
             for g in (b, 1 - b):
                 product(first[b], 0, g, b, opens=b)
 
+        skip_all = tile([P, PACK, U], F32, "xw1")
+        skip_t = [skip_all[:, t, :] for t in range(PACK)]
+        for a in range(2):
+            nc.sync.dma_start(out=skip_t[a], in_=skip[P * a : P * (a + 1), :])
+        skip_pairs = skip[2 * P : H, :].rearrange("(m t) v -> m t v", t=PACK)
+        for u in range(2):
+            nc.sync.dma_start(out=skip_t[2 + u], in_=skip_pairs[:, 2 * u : 2 * u + 2, :])
         h = tile([P, HALF], F32, "h00")
         nc.scalar.copy(h[:], first[0][:])
         nc.vector.tensor_copy(up[0][:].indirect(cell_t[:, lists[0]]), h[:])
@@ -184,7 +188,7 @@ def tile_picked_unet_none_p_kernel(
             quantise_w1(1, g)
             for b in range(2):
                 product(second[b], 1, g, b)
-        h = tile([P, HALF], F32, "xs")
+        h = tile([P, HALF], F32, "xs1")
         nc.scalar.copy(h[:], first[1][:])
         nc.vector.tensor_copy(up[0][:].indirect(cell_t[:, lists[1]]), h[:])
         h = tile([P, HALF], F32, "h10")
@@ -242,6 +246,7 @@ def tile_picked_unet_none_p_kernel(
 
         pieces = [(0, 0, CHUNK), (1, 0, CHUNK), (2, 0, CHUNK), (3, 0, P), (3, P, P)]
         names = ["b0", "b1", "a0", "a1", "tail0"]
+        accs = []
         for i, (c, v0, w) in enumerate(pieces):
             zc = tile([P, w], U32, "zc%d" % i)
             zs = tile([P, w], U8, "zs%d" % i)
@@ -251,7 +256,9 @@ def tile_picked_unet_none_p_kernel(
                 out=acc[:], lhsT=w2w[:].bitcast(FP4X4), lhsT_scale=w2s[:],
                 rhs=zc[:].bitcast(FP8X4), rhs_scale=zs[:], start=True, stop=True,
             )
-            res = tile([P, w], F32, "res%d" % i)
-            copy_of[OUT[i]](res[:], acc[:])
+            accs.append(acc)
+        for i, (c, v0, w) in enumerate(pieces):
+            res = tile([P, w], F32, "z3" if i == 1 else "res%d" % i)
+            copy_of[OUT[i]](res[:], accs[i][:])
             queue = nc.scalar if i == len(pieces) - 1 else nc.sync
             queue.dma_start(out=out[:, CHUNK * c + v0 : CHUNK * c + v0 + w], in_=res[:])

@@ -48,7 +48,7 @@ def tile_picked_unet_none_p_kernel(
         cols = [slice(0, P), slice(P, 2 * P), slice(2 * P, H)]
         width = [P, P, 2 * P]
         w1raw = {(0, g): tile([P, PACK, P], F32, "w1raw0%d" % g)[:] for g in range(PASSES)}
-        up = [tile([P, U], F32, "up%d" % t) for t in range(PACK)]
+        up = [tile([P, U], F32, "up%d" % t) for t in range(2)]
 
         w1_rows = w1.rearrange("(g p j) c -> g p j c", p=P, j=PACK)
 
@@ -74,8 +74,8 @@ def tile_picked_unet_none_p_kernel(
         load_x(0)
         load_x(1)
         nc.gpsimd.memset(xsm[:].rearrange("p g n -> p (g n)").bitcast(I32), 0)
-        for t in range(PACK):
-            (nc.vector if t < 2 else nc.gpsimd).memset(up[t][:], 0.0)
+        for t in range(2):
+            nc.gpsimd.memset(up[t][:], 0.0)
         ident = tile([P, P], F32, "ident")
         make_identity(nc, ident[:])
 
@@ -157,15 +157,6 @@ def tile_picked_unet_none_p_kernel(
             load_w1(2, g)
         round_w1(0, 1)
         quantise_w1(0, 1)
-        w2s = tile([P, N], U8, "rounded01")
-        nc.gpsimd.memset(w2s[:].bitcast(I32), 0)
-        w2w = tile([P, 2 * N], U8, "xsg")
-        nc.sync.dma_start(out=w2w[:].bitcast(I32), in_=w2_words[0].bitcast(I32))
-        for q in range(4):
-            nc.sync.dma_start(
-                out=w2s[32 * q : 32 * q + 4, :].bitcast(I32),
-                in_=w2_scales[0, 4 * q : 4 * q + 4, :].bitcast(I32),
-            )
         first = banks("tail", [P, HALF])
         for b in range(2):
             nc.vector.tensor_copy(xg[1][:, halves[b]], xw[1][:].bitcast(U32).indirect(offs_t[:, lists[b]]))
@@ -188,9 +179,22 @@ def tile_picked_unet_none_p_kernel(
             quantise_w1(1, g)
             for b in range(2):
                 product(second[b], 1, g, b)
+        w2s = tile([P, N], U8, "rounded11")
+        nc.gpsimd.memset(w2s[:].bitcast(I32), 0)
+        w2w = tile([P, 2 * N], U8, "rounded10")
+        nc.sync.dma_start(out=w2w[:].bitcast(I32), in_=w2_words[0].bitcast(I32))
+        for q in range(4):
+            nc.sync.dma_start(
+                out=w2s[32 * q : 32 * q + 4, :].bitcast(I32),
+                in_=w2_scales[0, 4 * q : 4 * q + 4, :].bitcast(I32),
+            )
+        up.append(tile([P, U], F32, "h00"))
+        nc.gpsimd.memset(up[2][:], 0.0)
         h = tile([P, HALF], F32, "xs1")
         nc.scalar.copy(h[:], first[1][:])
         nc.vector.tensor_copy(up[0][:].indirect(cell_t[:, lists[1]]), h[:])
+        up.append(tile([P, U], F32, "xs1"))
+        nc.gpsimd.memset(up[3][:], 0.0)
         h = tile([P, HALF], F32, "h10")
         nc.scalar.copy(h[:], second[0][:])
         nc.vector.tensor_copy(up[1][:].indirect(cell_t[:, lists[0]]), h[:])

@@ -48,7 +48,7 @@ def tile_picked_unet_none_p_kernel(
         cols = [slice(0, P), slice(P, 2 * P), slice(2 * P, H)]
         width = [P, P, 2 * P]
         w1raw = {(0, g): tile([P, PACK, P], F32, "w1raw0%d" % g)[:] for g in range(PASSES)}
-        up = [tile([P, U], F32, "up%d" % t) for t in range(2)]
+        up = [tile([P, U], F32, "up0")]
 
         w1_rows = w1.rearrange("(g p j) c -> g p j c", p=P, j=PACK)
 
@@ -74,8 +74,7 @@ def tile_picked_unet_none_p_kernel(
         load_x(0)
         load_x(1)
         nc.gpsimd.memset(xsm[:].rearrange("p g n -> p (g n)").bitcast(I32), 0)
-        for t in range(2):
-            nc.gpsimd.memset(up[t][:], 0.0)
+        nc.gpsimd.memset(up[0][:], 0.0)
         ident = tile([P, P], F32, "ident")
         make_identity(nc, ident[:])
 
@@ -157,6 +156,8 @@ def tile_picked_unet_none_p_kernel(
             load_w1(2, g)
         round_w1(0, 1)
         quantise_w1(0, 1)
+        up.append(tile([P, U], F32, "rounded01"))
+        nc.gpsimd.memset(up[1][:], 0.0)
         first = banks("tail", [P, HALF])
         for b in range(2):
             nc.vector.tensor_copy(xg[1][:, halves[b]], xw[1][:].bitcast(U32).indirect(offs_t[:, lists[b]]))
@@ -179,7 +180,7 @@ def tile_picked_unet_none_p_kernel(
             quantise_w1(1, g)
             for b in range(2):
                 product(second[b], 1, g, b)
-        w2s = tile([P, N], U8, "rounded11")
+        w2s = tile([P, N], U8, "h00")
         nc.gpsimd.memset(w2s[:].bitcast(I32), 0)
         w2w = tile([P, 2 * N], U8, "rounded10")
         nc.sync.dma_start(out=w2w[:].bitcast(I32), in_=w2_words[0].bitcast(I32))
@@ -188,7 +189,7 @@ def tile_picked_unet_none_p_kernel(
                 out=w2s[32 * q : 32 * q + 4, :].bitcast(I32),
                 in_=w2_scales[0, 4 * q : 4 * q + 4, :].bitcast(I32),
             )
-        up.append(tile([P, U], F32, "h00"))
+        up.append(tile([P, U], F32, "rounded11"))
         nc.gpsimd.memset(up[2][:], 0.0)
         h = tile([P, HALF], F32, "xs1")
         nc.scalar.copy(h[:], first[1][:])

@@ -15,16 +15,17 @@ U8 = mybir.dt.uint8
 FP8X4 = mybir.dt.float8_e4m3fn_x4
 FP4X4 = mybir.dt.float4_e2m1fn_x4
 
+COPY = mybir.ActivationFunctionType.Copy
+ADD = mybir.AluOpType.add
+
 P = 128
 PACK = 4
 PASSES = K // (P * PACK)
 HALF = S // 2
-CHUNK = 256
-CHUNKS = U // CHUNK
+SIDE = U // 2
+CHUNK = SIDE // 2
 HP = P // 2
 QP = P // 4
-BACK = (0, 1, 0, 0)
-OUT = (0, 1, 0, 1, 0)
 ROW0, STEP = 11, 7
 
 
@@ -45,18 +46,9 @@ def tile_picked_unet_none_p_kernel(
         xsg = tile([P, PASSES, S], U8, "xsg")
         xsm = tile([P, PASSES, S], U8, "xsm")
         xw = [tile([P, T], I32, "xw%d" % g) for g in range(PASSES)]
-        cols = [slice(0, P), slice(P, 2 * P), slice(2 * P, H)]
-        width = [P, P, 2 * P]
-        w1raw = {(0, g): tile([P, PACK, P], F32, "w1raw0%d" % g)[:] for g in range(PASSES)}
         up = [tile([P, U], F32, "up0")]
-
+        w1raw = {(0, g): tile([P, PACK, P], F32, "w1raw0%d" % g)[:] for g in range(PASSES)}
         w1_rows = w1.rearrange("(g p j) c -> g p j c", p=P, j=PACK)
-
-        def load_w1(a, g):
-            nc.sync.dma_start(out=w1raw[a, g], in_=w1_rows[g, :, :, cols[a]])
-
-        def load_x(g):
-            nc.sync.dma_start(out=xw[g][:], in_=x_words[g].rearrange("p n t -> p (n t)").bitcast(I32))
 
         def load_scales(g):
             nc.gpsimd.memset(xs[g][:].bitcast(I32), 0)
@@ -65,75 +57,55 @@ def tile_picked_unet_none_p_kernel(
                 in_=x_scales[g].bitcast(I32),
             )
 
-        load_w1(0, 0)
+        nc.sync.dma_start(out=w1raw[0, 0], in_=w1_rows[0, :, :, 0:P])
         nc.sync.dma_start(offs_t[:], offs)
         load_scales(0)
         nc.sync.dma_start(cell_t[:], cell)
-        load_w1(0, 1)
+        nc.sync.dma_start(out=w1raw[0, 1], in_=w1_rows[1, :, :, 0:P])
         load_scales(1)
-        load_x(0)
-        load_x(1)
+        for g in range(PASSES):
+            nc.sync.dma_start(out=xw[g][:], in_=x_words[g].rearrange("p n t -> p (n t)").bitcast(I32))
         nc.gpsimd.memset(xsm[:].rearrange("p g n -> p (g n)").bitcast(I32), 0)
         nc.gpsimd.memset(up[0][:], 0.0)
         ident = tile([P, P], F32, "ident")
         make_identity(nc, ident[:])
 
         xg = [tile([P, S], U32, "xg%d" % g) for g in range(PASSES)]
-        rounded = [[tile([P, width[a], PACK], BF16, "rounded%d%d" % (a, g)) for g in range(PASSES)] for a in range(3)]
+        rounded = {}
         codes = {}
         scales = {}
+        copy_on = {"scalar": nc.scalar.copy, "vector": nc.vector.tensor_copy}
 
-        def round_w1(a, g):
-            if a < 2:
-                src = w1raw[a, g].rearrange("p j (m t) -> p m j t", t=PACK)
-                dst = rounded[a][g][:].rearrange("p (m t) j -> p m j t", t=PACK)
-            else:
-                src = w1raw[a, g].rearrange("p j (m u e) -> p m j u e", u=2, e=2)
-                dst = rounded[a][g][:].rearrange("p (u m e) j -> p m j u e", u=2, e=2)
-            nc.scalar.copy(dst, src)
+        def round_w1(t, g, engine):
+            rounded[t, g] = tile([P, P, PACK], BF16, "rounded%d%d" % (t, g))
+            copy_on[engine](
+                rounded[t, g][:].rearrange("p (m i) j -> p m j i", i=PACK),
+                w1raw[t, g].rearrange("p j (m i) -> p m j i", i=PACK),
+            )
 
-        def quantise_w1(a, g):
-            c = tile([P, width[a]], U32, "wc%d%d" % (a, g))
-            s = tile([P, width[a]], U8, "ws%d%d" % (a, g))
-            nc.vector.quantize_mx(out=c[:].bitcast(FP8X4), scales=s[:], in_=rounded[a][g][:].rearrange("p c j -> p (c j)"))
-            for i in range(width[a] // P):
-                codes[a + i, g] = c[:, P * i : P * (i + 1)]
-                scales[a + i, g] = s[:, P * i : P * (i + 1)]
+        def quantise_w1(t, g):
+            codes[t, g] = tile([P, P], U32, "wc%d%d" % (t, g))
+            scales[t, g] = tile([P, P], U8, "ws%d%d" % (t, g))
+            nc.vector.quantize_mx(
+                out=codes[t, g][:].bitcast(FP8X4), scales=scales[t, g][:],
+                in_=rounded[t, g][:].rearrange("p c j -> p (c j)"),
+            )
 
         halves = [slice(0, HALF), slice(HALF, S)]
         lists = [slice(0, HALF // 16), slice(HALF // 16, S // 16)]
 
         def product(bank, t, g, b, opens=0):
             nc.tensor.matmul_mx(
-                out=bank[:], lhsT=codes[t, g].bitcast(FP8X4), lhsT_scale=scales[t, g],
+                out=bank[:], lhsT=codes[t, g][:].bitcast(FP8X4), lhsT_scale=scales[t, g][:],
                 rhs=xg[g][:, halves[b]].bitcast(FP8X4), rhs_scale=xsm[:, g, halves[b]],
                 start=(g == opens), stop=(g != opens),
             )
 
-        def banks(name, shape):
-            return [ps.tile(shape, F32, name="%s%d" % (name, d)) for d in range(2)]
-
         def turn(dst, src, start, stop):
             nc.tensor.matmul(dst, lhsT=src, rhs=ident[:], is_transpose=True, start=start, stop=stop)
 
-        zt = tile([P, 2 * U], F32, "zt")
-        zt_values = zt[:].bitcast(BF16).rearrange("p (u j d m e) -> p u j d m e", u=2, j=4, d=2, e=2)
-
-        def add_and_turn(t, name):
-            sums = banks(name, [P, 4, P])
-            for first, src in ((True, skip_t[t]), (False, up[t])):
-                for d in range(2):
-                    for j in range(4):
-                        v0 = P * (2 * j + d)
-                        turn(sums[d][:, j, :], src[:, v0 : v0 + P], first and j == 0, not first and j == 3)
-            for d in range(2):
-                if t < 2:
-                    nc.scalar.copy(
-                        zt_values[:, :, :, d, QP * t : QP * (t + 1), :],
-                        sums[d][:].rearrange("p j (m u e) -> p u j m e", u=2, e=2),
-                    )
-                else:
-                    nc.scalar.copy(zt_values[:, 0, :, d, HP:P, :], sums[d][:].rearrange("p j (m e) -> p j m e", e=2))
+        def scalar_scatter(t, b, h):
+            nc.scalar.activation(out=up[t][:].indirect(cell_t[:, lists[b]]), in_=h, func=COPY)
 
         for g in range(PASSES):
             nc.vector.tensor_copy(xsg[:, g, :], xs[g][:].indirect(offs_t[:]))
@@ -146,124 +118,171 @@ def tile_picked_unet_none_p_kernel(
         late = tile([P, PASSES * PACK * P], F32, "xs1")
         for g in range(PASSES):
             w1raw[1, g] = late[:, PACK * P * g : PACK * P * (g + 1)].rearrange("p (j c) -> p j c", j=PACK)
-            load_w1(1, g)
-        round_w1(0, 0)
+            nc.sync.dma_start(out=w1raw[1, g], in_=w1_rows[g, :, :, P : 2 * P])
+        round_w1(0, 0, "scalar")
         quantise_w1(0, 0)
         nc.vector.tensor_copy(xg[0][:], xw[0][:].bitcast(U32).indirect(offs_t[:]))
         late = tile([P, PASSES * PACK * 2 * P], F32, "xw0")
         for g in range(PASSES):
-            w1raw[2, g] = late[:, PACK * 2 * P * g : PACK * 2 * P * (g + 1)].rearrange("p (j c) -> p j c", j=PACK)
-            load_w1(2, g)
-        round_w1(0, 1)
+            both = late[:, PACK * 2 * P * g : PACK * 2 * P * (g + 1)].rearrange("p (j c) -> p j c", j=PACK)
+            nc.sync.dma_start(out=both, in_=w1_rows[g, :, :, 2 * P : H])
+            for t in (2, 3):
+                w1raw[t, g] = both[:, :, P * (t - 2) : P * (t - 1)]
+        round_w1(0, 1, "scalar")
         quantise_w1(0, 1)
-        up.append(tile([P, U], F32, "rounded01"))
-        nc.gpsimd.memset(up[1][:], 0.0)
-        first = banks("tail", [P, HALF])
+        for name in ("w1raw00", "w1raw01", "rounded01"):
+            up.append(tile([P, U], F32, name))
+            nc.scalar.copy(up[-1][:], up[0][:])
+        bank = {(0, b): ps.tile([P, HALF], F32, name="x%d" % b) for b in range(2)}
         for b in range(2):
             nc.vector.tensor_copy(xg[1][:, halves[b]], xw[1][:].bitcast(U32).indirect(offs_t[:, lists[b]]))
             for g in (b, 1 - b):
-                product(first[b], 0, g, b, opens=b)
+                product(bank[0, b], 0, g, b, opens=b)
 
-        skip_all = tile([P, PACK, U], F32, "xw1")
-        skip_t = [skip_all[:, t, :] for t in range(PACK)]
-        for a in range(2):
-            nc.sync.dma_start(out=skip_t[a], in_=skip[P * a : P * (a + 1), :])
-        skip_pairs = skip[2 * P : H, :].rearrange("(m t) v -> m t v", t=PACK)
-        for u in range(2):
-            nc.sync.dma_start(out=skip_t[2 + u], in_=skip_pairs[:, 2 * u : 2 * u + 2, :])
-        h = tile([P, HALF], F32, "h00")
-        nc.scalar.copy(h[:], first[0][:])
-        nc.vector.tensor_copy(up[0][:].indirect(cell_t[:, lists[0]]), h[:])
-        second = banks("a", [P, HALF])
+        skip_all = tile([P, 4 * U], F32, "xw1")
+        skip_t = [skip_all[:, U * t : U * (t + 1)] for t in range(4)]
+        for t in range(2):
+            nc.sync.dma_start(out=skip_t[t], in_=skip[P * t : P * (t + 1), :])
+        nc.sync.dma_start(
+            out=skip_all[:, 2 * U : 4 * U].rearrange("p (t v) -> p t v", t=2),
+            in_=skip[2 * P : H, :].rearrange("(t p) v -> p t v", p=P),
+        )
+
+        h = tile([P, P], F32, "h00")
+        nc.vector.tensor_copy(h[:], bank[0, 0][:, 0:P])
+        nc.vector.tensor_copy(up[0][:].indirect(cell_t[:, 0 : P // 16]), h[:])
+        for b in range(2):
+            bank[1, b] = ps.tile([P, HALF], F32, name="x%d" % (2 + b))
         for g in range(PASSES):
-            round_w1(1, g)
+            round_w1(1, g, "scalar")
             quantise_w1(1, g)
             for b in range(2):
-                product(second[b], 1, g, b)
-        w2s = tile([P, N], U8, "h00")
-        nc.gpsimd.memset(w2s[:].bitcast(I32), 0)
-        w2w = tile([P, 2 * N], U8, "rounded10")
-        nc.sync.dma_start(out=w2w[:].bitcast(I32), in_=w2_words[0].bitcast(I32))
-        for q in range(4):
-            nc.sync.dma_start(
-                out=w2s[32 * q : 32 * q + 4, :].bitcast(I32),
-                in_=w2_scales[0, 4 * q : 4 * q + 4, :].bitcast(I32),
-            )
-        up.append(tile([P, U], F32, "rounded11"))
-        nc.gpsimd.memset(up[2][:], 0.0)
-        h = tile([P, HALF], F32, "xs1")
-        nc.scalar.copy(h[:], first[1][:])
-        nc.vector.tensor_copy(up[0][:].indirect(cell_t[:, lists[1]]), h[:])
-        up.append(tile([P, U], F32, "xs1"))
-        nc.gpsimd.memset(up[3][:], 0.0)
+                product(bank[1, b], 1, g, b)
+        h = tile([P, S - P], F32, "xs1")
+        nc.scalar.copy(h[:, 0:P], bank[0, 0][:, P:HALF])
+        nc.scalar.copy(h[:, P : S - P], bank[0, 1][:])
+        nc.vector.tensor_copy(up[0][:].indirect(cell_t[:, P // 16 : S // 16]), h[:])
+        round_w1(2, 0, "scalar")
         h = tile([P, HALF], F32, "h10")
-        nc.scalar.copy(h[:], second[0][:])
-        nc.vector.tensor_copy(up[1][:].indirect(cell_t[:, lists[0]]), h[:])
-        third = banks("b", [P, HALF])
+        nc.scalar.copy(h[:], bank[1, 0][:])
+        scalar_scatter(1, 0, h[:])
+        round_w1(2, 1, "scalar")
+        h = tile([P, HALF], F32, "h11")
+        nc.scalar.copy(h[:], bank[1, 1][:])
+        scalar_scatter(1, 1, h[:])
         for g in range(PASSES):
-            round_w1(2, g)
-            quantise_w1(2, g)
+            round_w1(3, g, "vector")
+        for t in (3, 2):
             for b in range(2):
-                product(third[b], 2, g, b)
-        h = tile([P, HALF], F32, "xw0")
-        nc.scalar.copy(h[:], second[1][:])
-        nc.vector.tensor_copy(up[1][:].indirect(cell_t[:, lists[1]]), h[:])
-        h = tile([P, S], F32, "h2")
-        for b in range(2):
-            nc.scalar.copy(h[:, halves[b]], third[b][:])
-        nc.vector.tensor_copy(up[2][:].indirect(cell_t[:]), h[:])
-        add_and_turn(0, "a")
-        fourth = banks("a", [P, HALF])
+                bank[t, b] = ps.tile([P, HALF], F32, name="x%d" % (2 * (3 - t) + b))
+            for g in range(PASSES):
+                quantise_w1(t, g)
+                for b in range(2):
+                    product(bank[t, b], t, g, b)
+        rows = {}
+
+        def add_skip(t, s, engine, name):
+            side = slice(SIDE * s, SIDE * (s + 1))
+            rows[t, s] = tile([P, SIDE], BF16, name)
+            engine.tensor_tensor(rows[t, s][:], up[t][:, side], skip_t[t][:, side], ADD)
+
+        add_skip(0, 0, nc.vector, "rounded20")
         h = tile([P, S], F32, "h3")
         for b in range(2):
-            for g in range(PASSES):
-                product(fourth[b], 3, g, b)
-            nc.scalar.copy(h[:, halves[b]], fourth[b][:])
+            nc.vector.tensor_copy(h[:, halves[b]], bank[3, b][:])
         nc.vector.tensor_copy(up[3][:].indirect(cell_t[:]), h[:])
-        add_and_turn(1, "b")
+        for b in range(2):
+            h = tile([P, HALF], F32, "h2%d" % b)
+            nc.scalar.copy(h[:], bank[2, b][:])
+            scalar_scatter(2, b, h[:])
+        add_skip(0, 1, nc.gpsimd, "rounded21")
+        for s in range(2):
+            add_skip(1, s, nc.gpsimd, "rounded3%d" % s)
 
-        tail = [ps.tile([P, 2, CHUNK], F32, name="tail%d" % c) for c in range(CHUNKS)]
+        w2w = {}
+        for a in range(2):
+            for s in range(2):
+                w2w[a, s] = tile([P, 2 * N], U8, ("wc1%d", "ws1%d")[a] % s)
+                nc.gpsimd.memset(w2w[a, s][:].bitcast(I32), 0)
+                nc.sync.dma_start(
+                    out=w2w[a, s][HP * s : HP * (s + 1), :].bitcast(I32),
+                    in_=w2_words[0, HP * a : HP * (a + 1), :].bitcast(I32),
+                )
+        w2s = []
+        for swap in range(2):
+            plane = tile([P, N], U8, "rounded1%d" % swap)
+            nc.gpsimd.memset(plane[:].bitcast(I32), 0)
+            for q in range(4):
+                row = 4 * ((q + 2 * swap) % 4)
+                nc.sync.dma_start(
+                    out=plane[32 * q : 32 * q + 4, :].bitcast(I32),
+                    in_=w2_scales[0, row : row + 4, :].bitcast(I32),
+                )
+            w2s.append(plane)
 
-        def block(src, base, c, d):
-            v0 = base + P * (2 * c + d)
-            return src[:, v0 : v0 + P]
+        planes = tile([P, PACK * SIDE], BF16, "planes")
+        for t in range(2):
+            for s in range(2):
+                p0 = HP * s + QP * t
+                for j in range(PACK):
+                    nc.sync.dma_start(out=planes[p0 : p0 + QP, SIDE * j : SIDE * (j + 1)], in_=rows[t, s][j:P:PACK, :])
 
-        for c in range(CHUNKS):
+        zt = [tile([P, 4 * P], F32, "zt%d" % d) for d in range(2)]
+        sums = {(t, d): ps.tile([P, 4, P], F32, name="s%d%d" % (t, d)) for t in (2, 3) for d in range(2)}
+
+        def turn_into_sums(t, src, first):
             for d in range(2):
-                turn(tail[c][:, 1, P * d : P * (d + 1)], block(skip_t[3], 0, c, d), d == 0, False)
-        add_and_turn(2, "a")
+                for i in range(4):
+                    v0 = SIDE * (i % 2) + CHUNK * d + P * (i // 2)
+                    turn(sums[t, d][:, i, :], src[:, v0 : v0 + P], first and i == 0, not first and i == 3)
+
+        for t in (3, 2):
+            turn_into_sums(t, skip_t[t], True)
+        for t, engine in ((3, "vector"), (2, "scalar")):
+            turn_into_sums(t, up[t], False)
+            for d in range(2):
+                values = zt[d][:].bitcast(BF16).rearrange("p (u i m e) -> p u i m e", u=2, i=4, e=2)
+                copy_on[engine](
+                    values[:, :, :, QP * (t - 2) : QP * (t - 1), :],
+                    sums[t, d][:].rearrange("p i (m u e) -> p u i m e", u=2, e=2),
+                )
+
+        zq = {}
+
+        def quantise_z(a, d, z):
+            zc = tile([P, CHUNK], U32, ("zc%d", "za%d")[a] % d)
+            zs = tile([P, CHUNK], U8, "zs%d%d" % (a, d))
+            nc.vector.quantize_mx(out=zc[:].bitcast(FP8X4), scales=zs[:], in_=z[:].rearrange("p v t -> p (v t)"))
+            zq[a, d] = (zc, zs)
+
         for d in range(2):
-            for c in range(CHUNKS):
-                turn(tail[c][:, 0, P * d : P * (d + 1)], block(zt, 0, c, d), False, False)
-        for c in range(CHUNKS):
-            for d in range(2):
-                turn(tail[c][:, 1, P * d : P * (d + 1)], block(up[3], 0, c, d), False, d == 1)
-
-        copy_of = [nc.scalar.copy, nc.vector.tensor_copy]
-        for c in range(CHUNKS):
-            copy_of[c % 2](zt_values[:, 1, c, :, HP:P, :], tail[c][:, 1, :].rearrange("p (d m e) -> p d m e", d=2, e=2))
-        z = [tile([P, CHUNK, PACK], BF16, "z%d" % c) for c in range(CHUNKS)]
-        for c in range(CHUNKS):
-            for d in range(2):
-                turn(tail[c][:, 1, P * d : P * (d + 1)], block(zt, U, c, d), True, True)
-            words = z[c][:].rearrange("p v t -> p (v t)").bitcast(F32).rearrange("p (v u) -> p v u", u=2)
-            copy_of[BACK[c]](words, tail[c][:].rearrange("p u v -> p v u"))
-
-        pieces = [(0, 0, CHUNK), (1, 0, CHUNK), (2, 0, CHUNK), (3, 0, P), (3, P, P)]
-        names = ["b0", "b1", "a0", "a1", "tail0"]
-        accs = []
-        for i, (c, v0, w) in enumerate(pieces):
-            zc = tile([P, w], U32, "zc%d" % i)
-            zs = tile([P, w], U8, "zs%d" % i)
-            nc.vector.quantize_mx(out=zc[:].bitcast(FP8X4), scales=zs[:], in_=z[c][:, v0 : v0 + w, :].rearrange("p v t -> p (v t)"))
-            acc = ps.tile([P, w], F32, name=names[i])
-            nc.tensor.matmul_mx(
-                out=acc[:], lhsT=w2w[:].bitcast(FP4X4), lhsT_scale=w2s[:],
-                rhs=zc[:].bitcast(FP8X4), rhs_scale=zs[:], start=True, stop=True,
+            z = tile([P, CHUNK, PACK], BF16, "za%d" % d)
+            nc.vector.tensor_copy(
+                z[:].rearrange("p (c i) t -> p c t i", i=PACK),
+                planes[:].rearrange("p (t c i) -> p c t i", t=PACK, i=PACK)[:, CHUNK // PACK * d : CHUNK // PACK * (d + 1), :, :],
             )
-            accs.append(acc)
-        for i, (c, v0, w) in enumerate(pieces):
-            res = tile([P, w], F32, "z3" if i == 1 else "res%d" % i)
-            copy_of[OUT[i]](res[:], accs[i][:])
-            queue = nc.scalar if i == len(pieces) - 1 else nc.sync
-            queue.dma_start(out=out[:, CHUNK * c + v0 : CHUNK * c + v0 + w], in_=res[:])
+            quantise_z(0, d, z)
+        for d in range(2):
+            z = tile([P, CHUNK, PACK], BF16, "z%d" % d)
+            words = z[:].rearrange("p v t -> p (v t)").bitcast(F32).rearrange("p (v u) -> p v u", u=2)
+            for i, engine in ((0, "scalar"), (1, "scalar")):
+                back = ps.tile([P, 2, P], F32, name="x%d" % (2 * d + i))
+                for u in range(2):
+                    w0 = 2 * P * u + P * i
+                    turn(back[:, u, :], zt[d][:, w0 : w0 + P], True, True)
+                copy_on[engine](words[:, P * i : P * (i + 1), :], back[:].rearrange("p u v -> p v u"))
+            quantise_z(1, d, z)
+
+        for d in range(2):
+            for s, engine in ((0, "scalar"), (1, "vector")):
+                acc = ps.tile([P, CHUNK], F32, name="s%d%d" % (2 + s, d))
+                for a in range(2):
+                    zc, zs = zq[a, d]
+                    nc.tensor.matmul_mx(
+                        out=acc[:], lhsT=w2w[a, s][:].bitcast(FP4X4), lhsT_scale=w2s[(a + s) % 2][:],
+                        rhs=zc[:].bitcast(FP8X4), rhs_scale=zs[:], start=(a == 0), stop=(a == 1),
+                    )
+                res = tile([P, CHUNK], F32, "res%d%d" % (d, s))
+                copy_on[engine](res[:], acc[:])
+                v0 = SIDE * s + CHUNK * d
+                nc.sync.dma_start(out=out[:, v0 : v0 + CHUNK], in_=res[:])

@@ -17,6 +17,7 @@ FP4X4 = mybir.dt.float4_e2m1fn_x4
 
 COPY = mybir.ActivationFunctionType.Copy
 ADD = mybir.AluOpType.add
+MULT = mybir.AluOpType.mult
 
 P = 128
 PACK = 4
@@ -78,16 +79,22 @@ def tile_picked_unet_none_p_kernel(
 
         def round_w1(t, g, engine):
             rounded[t, g] = tile([P, P, PACK], BF16, "rounded%d%d" % (t, g))
-            copy_on[engine](
-                rounded[t, g][:].rearrange("p (m i) j -> p m j i", i=PACK),
-                w1raw[t, g].rearrange("p j (m i) -> p m j i", i=PACK),
-            )
+            if t < 2:
+                src = w1raw[t, g].rearrange("p j (m i) -> p m j i", i=PACK)
+            else:
+                src = w1raw[t, g].rearrange("p j m i -> p m j i")
+            copy_on[engine](rounded[t, g][:].rearrange("p (m i) j -> p m j i", i=src.shape[3]), src)
 
         def quantise_w1(t, g):
-            codes[t, g] = tile([P, P], U32, "wc%d%d" % (t, g))
+            if t == 2:
+                if g == 0:
+                    codes[2] = tile([P, PASSES * P], U32, "rounded11")
+                codes[t, g] = codes[2][:, P * g : P * (g + 1)]
+            else:
+                codes[t, g] = tile([P, P], U32, "wc%d%d" % (t, g))[:]
             scales[t, g] = tile([P, P], U8, "ws%d%d" % (t, g))
             nc.vector.quantize_mx(
-                out=codes[t, g][:].bitcast(FP8X4), scales=scales[t, g][:],
+                out=codes[t, g].bitcast(FP8X4), scales=scales[t, g][:],
                 in_=rounded[t, g][:].rearrange("p c j -> p (c j)"),
             )
 
@@ -96,7 +103,7 @@ def tile_picked_unet_none_p_kernel(
 
         def product(bank, t, g, b, opens=0):
             nc.tensor.matmul_mx(
-                out=bank[:], lhsT=codes[t, g][:].bitcast(FP8X4), lhsT_scale=scales[t, g][:],
+                out=bank[:], lhsT=codes[t, g].bitcast(FP8X4), lhsT_scale=scales[t, g][:],
                 rhs=xg[g][:, halves[b]].bitcast(FP8X4), rhs_scale=xsm[:, g, halves[b]],
                 start=(g == opens), stop=(g != opens),
             )
@@ -127,7 +134,7 @@ def tile_picked_unet_none_p_kernel(
             both = late[:, PACK * 2 * P * g : PACK * 2 * P * (g + 1)].rearrange("p (j c) -> p j c", j=PACK)
             nc.sync.dma_start(out=both, in_=w1_rows[g, :, :, 2 * P : H])
             for t in (2, 3):
-                w1raw[t, g] = both[:, :, P * (t - 2) : P * (t - 1)]
+                w1raw[t, g] = both.rearrange("p j (m u e) -> p j m u e", u=2, e=2)[:, :, :, t - 2, :]
         round_w1(0, 1, "scalar")
         quantise_w1(0, 1)
         for name in ("w1raw00", "w1raw01", "rounded01"):
@@ -139,18 +146,18 @@ def tile_picked_unet_none_p_kernel(
             for g in (b, 1 - b):
                 product(bank[0, b], 0, g, b, opens=b)
 
-        skip_all = tile([P, 4 * U], F32, "xw1")
-        skip_t = [skip_all[:, U * t : U * (t + 1)] for t in range(4)]
+        skip_all = tile([P, 3 * U], F32, "xw1")
+        skip_t = [skip_all[:, U * t : U * (t + 1)] for t in range(3)]
         for t in range(2):
             nc.sync.dma_start(out=skip_t[t], in_=skip[P * t : P * (t + 1), :])
-        nc.sync.dma_start(
-            out=skip_all[:, 2 * U : 4 * U].rearrange("p (t v) -> p t v", t=2),
-            in_=skip[2 * P : H, :].rearrange("(t p) v -> p t v", p=P),
-        )
+        skip_pairs = skip[2 * P : H, :].rearrange("(m t) v -> m t v", t=PACK)
+        nc.sync.dma_start(out=skip_t[2], in_=skip_pairs[:, 0:2, :])
 
         h = tile([P, P], F32, "h00")
         nc.vector.tensor_copy(h[:], bank[0, 0][:, 0:P])
         nc.vector.tensor_copy(up[0][:].indirect(cell_t[:, 0 : P // 16]), h[:])
+        skip_t.append(tile([P, U], F32, "h00")[:])
+        nc.sync.dma_start(out=skip_t[3], in_=skip_pairs[:, 2:4, :])
         for b in range(2):
             bank[1, b] = ps.tile([P, HALF], F32, name="x%d" % (2 + b))
         for g in range(PASSES):
@@ -162,16 +169,20 @@ def tile_picked_unet_none_p_kernel(
         nc.scalar.copy(h[:, 0:P], bank[0, 0][:, P:HALF])
         nc.scalar.copy(h[:, P : S - P], bank[0, 1][:])
         nc.vector.tensor_copy(up[0][:].indirect(cell_t[:, P // 16 : S // 16]), h[:])
+        round_w1(3, 0, "scalar")
         round_w1(2, 0, "scalar")
+        round_w1(2, 1, "scalar")
+        rounded[3, 1] = tile([P, P, PACK], BF16, "rounded11")
+        nc.gpsimd.tensor_scalar(
+            rounded[3, 1][:].rearrange("p (m e) j -> p m e j", e=2),
+            w1raw[3, 1].rearrange("p j m e -> p m e j"), 1.0, 0.0, MULT, ADD,
+        )
         h = tile([P, HALF], F32, "h10")
         nc.scalar.copy(h[:], bank[1, 0][:])
         scalar_scatter(1, 0, h[:])
-        round_w1(2, 1, "scalar")
         h = tile([P, HALF], F32, "h11")
         nc.scalar.copy(h[:], bank[1, 1][:])
         scalar_scatter(1, 1, h[:])
-        for g in range(PASSES):
-            round_w1(3, g, "vector")
         for t in (3, 2):
             for b in range(2):
                 bank[t, b] = ps.tile([P, HALF], F32, name="x%d" % (2 * (3 - t) + b))
@@ -191,13 +202,12 @@ def tile_picked_unet_none_p_kernel(
         for b in range(2):
             nc.vector.tensor_copy(h[:, halves[b]], bank[3, b][:])
         nc.vector.tensor_copy(up[3][:].indirect(cell_t[:]), h[:])
-        for b in range(2):
-            h = tile([P, HALF], F32, "h2%d" % b)
-            nc.scalar.copy(h[:], bank[2, b][:])
-            scalar_scatter(2, b, h[:])
+        h = tile([P, HALF], F32, "h20")
+        nc.scalar.copy(h[:], bank[2, 0][:])
+        scalar_scatter(2, 0, h[:])
         add_skip(0, 1, nc.gpsimd, "rounded21")
         for s in range(2):
-            add_skip(1, s, nc.gpsimd, "rounded3%d" % s)
+            add_skip(1, s, nc.gpsimd, ("rounded30", "rounded11")[s])
 
         w2w = {}
         for a in range(2):
@@ -210,7 +220,7 @@ def tile_picked_unet_none_p_kernel(
                 )
         w2s = []
         for swap in range(2):
-            plane = tile([P, N], U8, "rounded1%d" % swap)
+            plane = tile([P, N], U8, ("rounded10", "h10")[swap])
             nc.gpsimd.memset(plane[:].bitcast(I32), 0)
             for q in range(4):
                 row = 4 * ((q + 2 * swap) % 4)
@@ -227,62 +237,78 @@ def tile_picked_unet_none_p_kernel(
                 for j in range(PACK):
                     nc.sync.dma_start(out=planes[p0 : p0 + QP, SIDE * j : SIDE * (j + 1)], in_=rows[t, s][j:P:PACK, :])
 
-        zt = [tile([P, 4 * P], F32, "zt%d" % d) for d in range(2)]
-        sums = {(t, d): ps.tile([P, 4, P], F32, name="s%d%d" % (t, d)) for t in (2, 3) for d in range(2)}
+        zt = {(t, j): tile([P, P], F32, "zt%d%d" % (t, j)) for t in (2, 3) for j in range(4)}
+        early = [ps.tile([P, 2, 2, P], F32, name="x%d" % d) for d in range(2)]
+        sums = {(3, j): early[j // 2][:, j % 2, :, :] for j in range(4)}
+        for j in range(4):
+            sums[2, j] = ps.tile([P, 2, P], F32, name="s%d" % j)[:]
 
         def turn_into_sums(t, src, first):
-            for d in range(2):
-                for i in range(4):
-                    v0 = SIDE * (i % 2) + CHUNK * d + P * (i // 2)
-                    turn(sums[t, d][:, i, :], src[:, v0 : v0 + P], first and i == 0, not first and i == 3)
+            blocks = 4 if t == 3 else 2
+            for i in range(8):
+                j, s = divmod(i, 2)
+                v0 = SIDE * s + P * j
+                turn(sums[t, j][:, s, :], src[:, v0 : v0 + P], first and i % blocks == 0, not first and i % blocks == blocks - 1)
 
-        for t in (3, 2):
+        def round_sums(t, j, engine):
+            copy_on[engine](zt[t, j][:].bitcast(BF16), sums[t, j].rearrange("p s c -> p (s c)"))
+
+        for t in (2, 3):
             turn_into_sums(t, skip_t[t], True)
-        for t, engine in ((3, "vector"), (2, "scalar")):
-            turn_into_sums(t, up[t], False)
-            for d in range(2):
-                values = zt[d][:].bitcast(BF16).rearrange("p (u i m e) -> p u i m e", u=2, i=4, e=2)
-                copy_on[engine](
-                    values[:, :, :, QP * (t - 2) : QP * (t - 1), :],
-                    sums[t, d][:].rearrange("p i (m u e) -> p u i m e", u=2, e=2),
-                )
+        h = tile([P, HALF], F32, "h00")
+        nc.scalar.copy(h[:], bank[2, 1][:])
+        scalar_scatter(2, 1, h[:])
+        turn_into_sums(3, up[3], False)
+        for j in range(4):
+            round_sums(3, j, "vector")
+        back = [ps.tile([P, 2, P], F32, name="x%d" % ((j + 2) % 4)) for j in range(4)]
+        for j in range(4):
+            turn(back[j][:, 1, :], zt[3, j][:], True, True)
+        turn_into_sums(2, up[2], False)
+        for j in range(4):
+            round_sums(2, j, "scalar")
 
-        zq = {}
+        def quantise_z(z, zc, scale_name):
+            zs = tile([P, zc.shape[1]], U8, scale_name)
+            nc.vector.quantize_mx(out=zc.bitcast(FP8X4), scales=zs[:], in_=z.rearrange("p v t -> p (v t)"))
+            return zc, zs[:]
 
-        def quantise_z(a, d, z):
-            zc = tile([P, CHUNK], U32, ("zc%d", "za%d")[a] % d)
-            zs = tile([P, CHUNK], U8, "zs%d%d" % (a, d))
-            nc.vector.quantize_mx(out=zc[:].bitcast(FP8X4), scales=zs[:], in_=z[:].rearrange("p v t -> p (v t)"))
-            zq[a, d] = (zc, zs)
-
+        first = []
+        chunks = []
+        woven = tile([P, SIDE * PACK], BF16, "rounded01")
         for d in range(2):
-            z = tile([P, CHUNK, PACK], BF16, "za%d" % d)
+            z = woven[:, CHUNK * PACK * d : CHUNK * PACK * (d + 1)].rearrange("p (v t) -> p v t", t=PACK)
             nc.vector.tensor_copy(
-                z[:].rearrange("p (c i) t -> p c t i", i=PACK),
+                z.rearrange("p (c i) t -> p c t i", i=PACK),
                 planes[:].rearrange("p (t c i) -> p c t i", t=PACK, i=PACK)[:, CHUNK // PACK * d : CHUNK // PACK * (d + 1), :, :],
             )
-            quantise_z(0, d, z)
+            chunks.append(z)
         for d in range(2):
-            z = tile([P, CHUNK, PACK], BF16, "z%d" % d)
+            first.append(quantise_z(chunks[d], tile([P, CHUNK], U32, "zc%d" % d)[:], "zs%d" % d))
+        second = []
+        last_codes = tile([P, SIDE], U32, "rounded01")
+        for j in range(4):
+            z = tile([P, P, PACK], BF16, "zb%d" % j)
             words = z[:].rearrange("p v t -> p (v t)").bitcast(F32).rearrange("p (v u) -> p v u", u=2)
-            for i, engine in ((0, "scalar"), (1, "scalar")):
-                back = ps.tile([P, 2, P], F32, name="x%d" % (2 * d + i))
-                for u in range(2):
-                    w0 = 2 * P * u + P * i
-                    turn(back[:, u, :], zt[d][:, w0 : w0 + P], True, True)
-                copy_on[engine](words[:, P * i : P * (i + 1), :], back[:].rearrange("p u v -> p v u"))
-            quantise_z(1, d, z)
+            turn(back[j][:, 0, :], zt[2, j][:], True, True)
+            nc.scalar.copy(words, back[j][:].rearrange("p u v -> p v u"))
+            second.append(quantise_z(z[:], last_codes[:, P * j : P * (j + 1)], "zr%d" % j))
+
+        def product2(acc, a, s, operand, start, stop):
+            nc.tensor.matmul_mx(
+                out=acc, lhsT=w2w[a, s][:].bitcast(FP4X4), lhsT_scale=w2s[(a + s) % 2][:],
+                rhs=operand[0].bitcast(FP8X4), rhs_scale=operand[1], start=start, stop=stop,
+            )
 
         for d in range(2):
+            accs = [ps.tile([P, CHUNK], F32, name="x%d" % ((2 * d + s + 2) % 4)) for s in range(2)]
+            for s in range(2):
+                product2(accs[s][:], 0, s, first[d], True, False)
+            for i in range(2):
+                for s in range(2):
+                    product2(accs[s][:, P * i : P * (i + 1)], 1, s, second[2 * d + i], False, i == 1)
             for s, engine in ((0, "scalar"), (1, "vector")):
-                acc = ps.tile([P, CHUNK], F32, name="s%d%d" % (2 + s, d))
-                for a in range(2):
-                    zc, zs = zq[a, d]
-                    nc.tensor.matmul_mx(
-                        out=acc[:], lhsT=w2w[a, s][:].bitcast(FP4X4), lhsT_scale=w2s[(a + s) % 2][:],
-                        rhs=zc[:].bitcast(FP8X4), rhs_scale=zs[:], start=(a == 0), stop=(a == 1),
-                    )
                 res = tile([P, CHUNK], F32, "res%d%d" % (d, s))
-                copy_on[engine](res[:], acc[:])
+                copy_on[engine](res[:], accs[s][:])
                 v0 = SIDE * s + CHUNK * d
                 nc.sync.dma_start(out=out[:, v0 : v0 + CHUNK], in_=res[:])

@@ -17,7 +17,6 @@ FP4X4 = mybir.dt.float4_e2m1fn_x4
 
 COPY = mybir.ActivationFunctionType.Copy
 ADD = mybir.AluOpType.add
-MULT = mybir.AluOpType.mult
 
 P = 128
 PACK = 4
@@ -88,7 +87,7 @@ def tile_picked_unet_none_p_kernel(
         def quantise_w1(t, g):
             if t == 2:
                 if g == 0:
-                    codes[2] = tile([P, PASSES * P], U32, "rounded11")
+                    codes[2] = tile([P, PASSES * P], U32, "rounded31")
                 codes[t, g] = codes[2][:, P * g : P * (g + 1)]
             else:
                 codes[t, g] = tile([P, P], U32, "wc%d%d" % (t, g))[:]
@@ -108,8 +107,8 @@ def tile_picked_unet_none_p_kernel(
                 start=(g == opens), stop=(g != opens),
             )
 
-        def turn(dst, src, start, stop):
-            nc.tensor.matmul(dst, lhsT=src, rhs=ident[:], is_transpose=True, start=start, stop=stop)
+        def turn(dst, src, start, stop, by=ident):
+            nc.tensor.matmul(dst, lhsT=src, rhs=by[:], is_transpose=True, start=start, stop=stop)
 
         def scalar_scatter(t, b, h):
             nc.scalar.activation(out=up[t][:].indirect(cell_t[:, lists[b]]), in_=h, func=COPY)
@@ -171,18 +170,14 @@ def tile_picked_unet_none_p_kernel(
         nc.vector.tensor_copy(up[0][:].indirect(cell_t[:, P // 16 : S // 16]), h[:])
         round_w1(3, 0, "scalar")
         round_w1(2, 0, "scalar")
-        round_w1(2, 1, "scalar")
-        rounded[3, 1] = tile([P, P, PACK], BF16, "rounded11")
-        nc.gpsimd.tensor_scalar(
-            rounded[3, 1][:].rearrange("p (m e) j -> p m e j", e=2),
-            w1raw[3, 1].rearrange("p j m e -> p m e j"), 1.0, 0.0, MULT, ADD,
-        )
         h = tile([P, HALF], F32, "h10")
         nc.scalar.copy(h[:], bank[1, 0][:])
         scalar_scatter(1, 0, h[:])
+        round_w1(2, 1, "scalar")
         h = tile([P, HALF], F32, "h11")
         nc.scalar.copy(h[:], bank[1, 1][:])
         scalar_scatter(1, 1, h[:])
+        round_w1(3, 1, "vector")
         for t in (3, 2):
             for b in range(2):
                 bank[t, b] = ps.tile([P, HALF], F32, name="x%d" % (2 * (3 - t) + b))
@@ -202,12 +197,13 @@ def tile_picked_unet_none_p_kernel(
         for b in range(2):
             nc.vector.tensor_copy(h[:, halves[b]], bank[3, b][:])
         nc.vector.tensor_copy(up[3][:].indirect(cell_t[:]), h[:])
-        h = tile([P, HALF], F32, "h20")
-        nc.scalar.copy(h[:], bank[2, 0][:])
-        scalar_scatter(2, 0, h[:])
+        for b in range(2):
+            h = tile([P, HALF], F32, "h2%d" % b)
+            nc.scalar.copy(h[:], bank[2, b][:])
+            scalar_scatter(2, b, h[:])
         add_skip(0, 1, nc.gpsimd, "rounded21")
         for s in range(2):
-            add_skip(1, s, nc.gpsimd, ("rounded30", "rounded11")[s])
+            add_skip(1, s, nc.gpsimd, "rounded3%d" % s)
 
         w2w = {}
         for a in range(2):
@@ -220,7 +216,7 @@ def tile_picked_unet_none_p_kernel(
                 )
         w2s = []
         for swap in range(2):
-            plane = tile([P, N], U8, ("rounded10", "h10")[swap])
+            plane = tile([P, N], U8, "rounded1%d" % swap)
             nc.gpsimd.memset(plane[:].bitcast(I32), 0)
             for q in range(4):
                 row = 4 * ((q + 2 * swap) % 4)
@@ -243,28 +239,27 @@ def tile_picked_unet_none_p_kernel(
         for j in range(4):
             sums[2, j] = ps.tile([P, 2, P], F32, name="s%d" % j)[:]
 
-        def turn_into_sums(t, src, first):
+        def turn_into_sums(t, src, first, by=ident):
             blocks = 4 if t == 3 else 2
             for i in range(8):
                 j, s = divmod(i, 2)
                 v0 = SIDE * s + P * j
-                turn(sums[t, j][:, s, :], src[:, v0 : v0 + P], first and i % blocks == 0, not first and i % blocks == blocks - 1)
+                turn(sums[t, j][:, s, :], src[:, v0 : v0 + P], first and i % blocks == 0, not first and i % blocks == blocks - 1, by)
 
         def round_sums(t, j, engine):
             copy_on[engine](zt[t, j][:].bitcast(BF16), sums[t, j].rearrange("p s c -> p (s c)"))
 
         for t in (2, 3):
             turn_into_sums(t, skip_t[t], True)
-        h = tile([P, HALF], F32, "h00")
-        nc.scalar.copy(h[:], bank[2, 1][:])
-        scalar_scatter(2, 1, h[:])
+        last_ident = tile([P, P], F32, "h00")
+        make_identity(nc, last_ident[:])
         turn_into_sums(3, up[3], False)
         for j in range(4):
             round_sums(3, j, "vector")
         back = [ps.tile([P, 2, P], F32, name="x%d" % ((j + 2) % 4)) for j in range(4)]
         for j in range(4):
             turn(back[j][:, 1, :], zt[3, j][:], True, True)
-        turn_into_sums(2, up[2], False)
+        turn_into_sums(2, up[2], False, last_ident)
         for j in range(4):
             round_sums(2, j, "scalar")
 
@@ -287,12 +282,17 @@ def tile_picked_unet_none_p_kernel(
             first.append(quantise_z(chunks[d], tile([P, CHUNK], U32, "zc%d" % d)[:], "zs%d" % d))
         second = []
         last_codes = tile([P, SIDE], U32, "rounded01")
-        for j in range(4):
-            z = tile([P, P, PACK], BF16, "zb%d" % j)
-            words = z[:].rearrange("p v t -> p (v t)").bitcast(F32).rearrange("p (v u) -> p v u", u=2)
-            turn(back[j][:, 0, :], zt[2, j][:], True, True)
-            nc.scalar.copy(words, back[j][:].rearrange("p u v -> p v u"))
-            second.append(quantise_z(z[:], last_codes[:, P * j : P * (j + 1)], "zr%d" % j))
+        for d in range(2):
+            words = tile([P, 2 * CHUNK], F32, "zb%d" % d)
+            for i in range(2):
+                j = 2 * d + i
+                turn(back[j][:, 0, :], zt[2, j][:], True, True)
+                nc.scalar.copy(
+                    words[:, CHUNK * i : CHUNK * (i + 1)].rearrange("p (v u) -> p v u", u=2),
+                    back[j][:].rearrange("p u v -> p v u"),
+                )
+            z = words[:].bitcast(BF16).rearrange("p (v t) -> p v t", t=PACK)
+            second.append(quantise_z(z, last_codes[:, CHUNK * d : CHUNK * (d + 1)], "zr%d" % d))
 
         def product2(acc, a, s, operand, start, stop):
             nc.tensor.matmul_mx(
@@ -304,9 +304,8 @@ def tile_picked_unet_none_p_kernel(
             accs = [ps.tile([P, CHUNK], F32, name="x%d" % ((2 * d + s + 2) % 4)) for s in range(2)]
             for s in range(2):
                 product2(accs[s][:], 0, s, first[d], True, False)
-            for i in range(2):
-                for s in range(2):
-                    product2(accs[s][:, P * i : P * (i + 1)], 1, s, second[2 * d + i], False, i == 1)
+            for s in range(2):
+                product2(accs[s][:], 1, s, second[d], False, True)
             for s, engine in ((0, "scalar"), (1, "vector")):
                 res = tile([P, CHUNK], F32, "res%d%d" % (d, s))
                 copy_on[engine](res[:], accs[s][:])

@@ -107,8 +107,8 @@ def tile_picked_unet_none_p_kernel(
                 start=(g == opens), stop=(g != opens),
             )
 
-        def turn(dst, src, start, stop, by=ident):
-            nc.tensor.matmul(dst, lhsT=src, rhs=by[:], is_transpose=True, start=start, stop=stop)
+        def turn(dst, src, start, stop):
+            nc.tensor.matmul(dst, lhsT=src, rhs=ident[:], is_transpose=True, start=start, stop=stop)
 
         def scalar_scatter(t, b, h):
             nc.scalar.activation(out=up[t][:].indirect(cell_t[:, lists[b]]), in_=h, func=COPY)
@@ -145,18 +145,19 @@ def tile_picked_unet_none_p_kernel(
             for g in (b, 1 - b):
                 product(bank[0, b], 0, g, b, opens=b)
 
-        skip_all = tile([P, 3 * U], F32, "xw1")
-        skip_t = [skip_all[:, U * t : U * (t + 1)] for t in range(3)]
+        skip_all = tile([P, 4 * U], F32, "xw1")
+        skip_t = [skip_all[:, U * t : U * (t + 1)] for t in range(4)]
         for t in range(2):
             nc.sync.dma_start(out=skip_t[t], in_=skip[P * t : P * (t + 1), :])
-        skip_pairs = skip[2 * P : H, :].rearrange("(m t) v -> m t v", t=PACK)
-        nc.sync.dma_start(out=skip_t[2], in_=skip_pairs[:, 0:2, :])
+        skip_pairs = skip[2 * P : H, :].rearrange("(m u e) v -> e m u v", u=2, e=2)
+        for e in range(2):
+            nc.sync.dma_start(
+                out=skip_all[e:P:2, 2 * U : 4 * U].rearrange("p (u v) -> p u v", u=2), in_=skip_pairs[e]
+            )
 
         h = tile([P, P], F32, "h00")
         nc.vector.tensor_copy(h[:], bank[0, 0][:, 0:P])
         nc.vector.tensor_copy(up[0][:].indirect(cell_t[:, 0 : P // 16]), h[:])
-        skip_t.append(tile([P, U], F32, "h00")[:])
-        nc.sync.dma_start(out=skip_t[3], in_=skip_pairs[:, 2:4, :])
         for b in range(2):
             bank[1, b] = ps.tile([P, HALF], F32, name="x%d" % (2 + b))
         for g in range(PASSES):
@@ -239,27 +240,25 @@ def tile_picked_unet_none_p_kernel(
         for j in range(4):
             sums[2, j] = ps.tile([P, 2, P], F32, name="s%d" % j)[:]
 
-        def turn_into_sums(t, src, first, by=ident):
+        def turn_into_sums(t, src, first):
             blocks = 4 if t == 3 else 2
             for i in range(8):
                 j, s = divmod(i, 2)
                 v0 = SIDE * s + P * j
-                turn(sums[t, j][:, s, :], src[:, v0 : v0 + P], first and i % blocks == 0, not first and i % blocks == blocks - 1, by)
+                turn(sums[t, j][:, s, :], src[:, v0 : v0 + P], first and i % blocks == 0, not first and i % blocks == blocks - 1)
 
         def round_sums(t, j, engine):
             copy_on[engine](zt[t, j][:].bitcast(BF16), sums[t, j].rearrange("p s c -> p (s c)"))
 
-        for t in (2, 3):
+        for t in (3, 2):
             turn_into_sums(t, skip_t[t], True)
-        last_ident = tile([P, P], F32, "h00")
-        make_identity(nc, last_ident[:])
         turn_into_sums(3, up[3], False)
         for j in range(4):
             round_sums(3, j, "vector")
         back = [ps.tile([P, 2, P], F32, name="x%d" % ((j + 2) % 4)) for j in range(4)]
         for j in range(4):
             turn(back[j][:, 1, :], zt[3, j][:], True, True)
-        turn_into_sums(2, up[2], False, last_ident)
+        turn_into_sums(2, up[2], False)
         for j in range(4):
             round_sums(2, j, "scalar")
 
@@ -301,7 +300,7 @@ def tile_picked_unet_none_p_kernel(
             )
 
         for d in range(2):
-            accs = [ps.tile([P, CHUNK], F32, name="x%d" % ((2 * d + s + 2) % 4)) for s in range(2)]
+            accs = [ps.tile([P, CHUNK], F32, name="s%d" % (2 * d + s)) for s in range(2)]
             for s in range(2):
                 product2(accs[s][:], 0, s, first[d], True, False)
             for s in range(2):

@@ -77,32 +77,39 @@ def tile_picked_unet_none_p_kernel(
         copy_on = {"scalar": nc.scalar.copy, "vector": nc.vector.tensor_copy}
 
         def round_w1(t, g, engine):
-            rounded[t, g] = tile([P, P, PACK], BF16, "rounded%d%d" % (t, g))
-            if t < 2:
-                src = w1raw[t, g].rearrange("p j (m i) -> p m j i", i=PACK)
-            else:
-                src = w1raw[t, g].rearrange("p j m i -> p m j i")
-            copy_on[engine](rounded[t, g][:].rearrange("p (m i) j -> p m j i", i=src.shape[3]), src)
+            rounded[t, g] = tile([P, P * PACK], BF16, "rounded%d%d" % (t, g))
+            copy_on[engine](
+                rounded[t, g][:].rearrange("p (m i j) -> p m j i", i=PACK, j=PACK),
+                w1raw[t, g].rearrange("p j (m i) -> p m j i", i=PACK),
+            )
+
+        def round_pairs(g, engine):
+            rounded[2, g] = tile([P, 2 * P * PACK], BF16, "rounded2%d" % g)
+            copy_on[engine](
+                rounded[2, g][:].rearrange("p (u m e j) -> p m j u e", u=2, e=2, j=PACK),
+                w1raw[2, g].rearrange("p j (m u e) -> p m j u e", u=2, e=2),
+            )
+
+        def quantise(t, g, width):
+            c = tile([P, width], U32, "wc%d%d" % (t, g))
+            s = tile([P, width], U8, "ws%d%d" % (t, g))
+            nc.vector.quantize_mx(out=c[:].bitcast(FP8X4), scales=s[:], in_=rounded[t, g][:])
+            for i in range(width // P):
+                codes[t + i, g] = c[:, P * i : P * (i + 1)]
+                scales[t + i, g] = s[:, P * i : P * (i + 1)]
 
         def quantise_w1(t, g):
-            if t == 2:
-                if g == 0:
-                    codes[2] = tile([P, PASSES * P], U32, "rounded31")
-                codes[t, g] = codes[2][:, P * g : P * (g + 1)]
-            else:
-                codes[t, g] = tile([P, P], U32, "wc%d%d" % (t, g))[:]
-            scales[t, g] = tile([P, P], U8, "ws%d%d" % (t, g))
-            nc.vector.quantize_mx(
-                out=codes[t, g].bitcast(FP8X4), scales=scales[t, g][:],
-                in_=rounded[t, g][:].rearrange("p c j -> p (c j)"),
-            )
+            quantise(t, g, P)
+
+        def quantise_pairs(g):
+            quantise(2, g, 2 * P)
 
         halves = [slice(0, HALF), slice(HALF, S)]
         lists = [slice(0, HALF // 16), slice(HALF // 16, S // 16)]
 
         def product(bank, t, g, b, opens=0):
             nc.tensor.matmul_mx(
-                out=bank[:], lhsT=codes[t, g].bitcast(FP8X4), lhsT_scale=scales[t, g][:],
+                out=bank[:], lhsT=codes[t, g].bitcast(FP8X4), lhsT_scale=scales[t, g],
                 rhs=xg[g][:, halves[b]].bitcast(FP8X4), rhs_scale=xsm[:, g, halves[b]],
                 start=(g == opens), stop=(g != opens),
             )
@@ -130,10 +137,8 @@ def tile_picked_unet_none_p_kernel(
         nc.vector.tensor_copy(xg[0][:], xw[0][:].bitcast(U32).indirect(offs_t[:]))
         late = tile([P, PASSES * PACK * 2 * P], F32, "xw0")
         for g in range(PASSES):
-            both = late[:, PACK * 2 * P * g : PACK * 2 * P * (g + 1)].rearrange("p (j c) -> p j c", j=PACK)
-            nc.sync.dma_start(out=both, in_=w1_rows[g, :, :, 2 * P : H])
-            for t in (2, 3):
-                w1raw[t, g] = both.rearrange("p j (m u e) -> p j m u e", u=2, e=2)[:, :, :, t - 2, :]
+            w1raw[2, g] = late[:, PACK * 2 * P * g : PACK * 2 * P * (g + 1)].rearrange("p (j c) -> p j c", j=PACK)
+            nc.sync.dma_start(out=w1raw[2, g], in_=w1_rows[g, :, :, 2 * P : H])
         round_w1(0, 1, "scalar")
         quantise_w1(0, 1)
         for name in ("w1raw00", "w1raw01", "rounded01"):
@@ -169,23 +174,22 @@ def tile_picked_unet_none_p_kernel(
         nc.scalar.copy(h[:, 0:P], bank[0, 0][:, P:HALF])
         nc.scalar.copy(h[:, P : S - P], bank[0, 1][:])
         nc.vector.tensor_copy(up[0][:].indirect(cell_t[:, P // 16 : S // 16]), h[:])
-        round_w1(3, 0, "scalar")
-        round_w1(2, 0, "scalar")
+        round_pairs(0, "scalar")
         h = tile([P, HALF], F32, "h10")
         nc.scalar.copy(h[:], bank[1, 0][:])
         scalar_scatter(1, 0, h[:])
-        round_w1(2, 1, "scalar")
         h = tile([P, HALF], F32, "h11")
         nc.scalar.copy(h[:], bank[1, 1][:])
         scalar_scatter(1, 1, h[:])
-        round_w1(3, 1, "vector")
+        round_pairs(1, "vector")
+        for g in range(PASSES):
+            quantise_pairs(g)
         for t in (3, 2):
             for b in range(2):
                 bank[t, b] = ps.tile([P, HALF], F32, name="x%d" % (2 * (3 - t) + b))
-            for g in range(PASSES):
-                quantise_w1(t, g)
-                for b in range(2):
-                    product(bank[t, b], t, g, b)
+            for b in range(2):
+                for g in (3 - t, t - 2):
+                    product(bank[t, b], t, g, b, opens=3 - t)
         rows = {}
 
         def add_skip(t, s, engine, name):
@@ -193,7 +197,7 @@ def tile_picked_unet_none_p_kernel(
             rows[t, s] = tile([P, SIDE], BF16, name)
             engine.tensor_tensor(rows[t, s][:], up[t][:, side], skip_t[t][:, side], ADD)
 
-        add_skip(0, 0, nc.vector, "rounded20")
+        add_skip(0, 0, nc.vector, "rows00")
         h = tile([P, S], F32, "h3")
         for b in range(2):
             nc.vector.tensor_copy(h[:, halves[b]], bank[3, b][:])
@@ -204,7 +208,7 @@ def tile_picked_unet_none_p_kernel(
             scalar_scatter(2, b, h[:])
         add_skip(0, 1, nc.gpsimd, "rounded21")
         for s in range(2):
-            add_skip(1, s, nc.gpsimd, "rounded3%d" % s)
+            add_skip(1, s, nc.gpsimd, "rows1%d" % s)
 
         w2w = {}
         for a in range(2):

@@ -210,26 +210,18 @@ def tile_picked_unet_none_p_kernel(
         for s in range(2):
             add_skip(1, s, nc.gpsimd, "rows1%d" % s)
 
-        w2w = {}
-        for a in range(2):
-            for s in range(2):
-                w2w[a, s] = tile([P, 2 * N], U8, ("wc1%d", "ws1%d")[a] % s)
-                nc.gpsimd.memset(w2w[a, s][:].bitcast(I32), 0)
-                nc.sync.dma_start(
-                    out=w2w[a, s][HP * s : HP * (s + 1), :].bitcast(I32),
-                    in_=w2_words[0, HP * a : HP * (a + 1), :].bitcast(I32),
-                )
-        w2s = []
-        for swap in range(2):
-            plane = tile([P, N], U8, "rounded1%d" % swap)
-            nc.gpsimd.memset(plane[:].bitcast(I32), 0)
-            for q in range(4):
-                row = 4 * ((q + 2 * swap) % 4)
-                nc.sync.dma_start(
-                    out=plane[32 * q : 32 * q + 4, :].bitcast(I32),
-                    in_=w2_scales[0, row : row + 4, :].bitcast(I32),
-                )
-            w2s.append(plane)
+        w2w = tile([P, 2, 2, 2 * N], U8, "wc10")
+        nc.gpsimd.memset(w2w[:].rearrange("p s a c -> p (s a c)").bitcast(I32), 0)
+        for s in range(2):
+            nc.sync.dma_start(
+                out=w2w[HP * s : HP * (s + 1), s, :, :].bitcast(I32),
+                in_=w2_words[0].bitcast(I32).rearrange("(a p) c -> p a c", a=2),
+            )
+        w2s = tile([P, 2, N], U8, "rounded10")
+        nc.gpsimd.memset(w2s[:].rearrange("p a c -> p (a c)").bitcast(I32), 0)
+        scale_rows = w2_scales[0].bitcast(I32).rearrange("(a q r) c -> q r a c", a=2, q=2)
+        for q in range(4):
+            nc.sync.dma_start(out=w2s[32 * q : 32 * q + 4, :, :].bitcast(I32), in_=scale_rows[q % 2])
 
         planes = tile([P, PACK * SIDE], BF16, "planes")
         for t in range(2):
@@ -299,7 +291,7 @@ def tile_picked_unet_none_p_kernel(
 
         def product2(acc, a, s, operand, start, stop):
             nc.tensor.matmul_mx(
-                out=acc, lhsT=w2w[a, s][:].bitcast(FP4X4), lhsT_scale=w2s[(a + s) % 2][:],
+                out=acc, lhsT=w2w[:, s, a, :].bitcast(FP4X4), lhsT_scale=w2s[:, a, :],
                 rhs=operand[0].bitcast(FP8X4), rhs_scale=operand[1], start=start, stop=stop,
             )
 

@@ -1,7 +1,6 @@
 from contextlib import ExitStack
 
 import concourse.mybir as mybir
-from concourse.masks import make_identity
 
 K, T, S, H, N, U = 1024, 2048, 512, 512, 128, 1024
 FLOPS = 2 * K * H * S + 2 * H * N * U
@@ -23,10 +22,9 @@ PACK = 4
 PASSES = K // (P * PACK)
 HALF = S // 2
 SIDE = U // 2
-CHUNK = SIDE // 2
+CHUNK = U // 4
+WIDE = H // 2
 HP = P // 2
-QP = P // 4
-ROW0, STEP = 11, 7
 
 
 def tile_picked_unet_none_p_kernel(
@@ -40,269 +38,203 @@ def tile_picked_unet_none_p_kernel(
         def tile(shape, dtype, name):
             return sb.tile(shape, dtype, name=name, align_bytes=64)
 
-        offs_t = sb.tile([P, S // 16], U16, name="offs_t")
-        cell_t = sb.tile([P, S // 16], U16, name="cell_t")
-        xs = [tile([P, T], U8, "xs%d" % g) for g in range(PASSES)]
-        xsg = tile([P, PASSES, S], U8, "xsg")
-        xsm = tile([P, PASSES, S], U8, "xsm")
-        xw = [tile([P, T], I32, "xw%d" % g) for g in range(PASSES)]
-        up = [tile([P, U], F32, "up0")]
-        w1raw = {(0, g): tile([P, PACK, P], F32, "w1raw0%d" % g)[:] for g in range(PASSES)}
-        w1_rows = w1.rearrange("(g p j) c -> g p j c", p=P, j=PACK)
-
-        def load_scales(g):
-            nc.gpsimd.memset(xs[g][:].bitcast(I32), 0)
-            nc.sync.dma_start(
-                out=xs[g][ROW0 : ROW0 + 15 * STEP + 1 : STEP, :].bitcast(I32),
-                in_=x_scales[g].bitcast(I32),
-            )
-
-        nc.sync.dma_start(out=w1raw[0, 0], in_=w1_rows[0, :, :, 0:P])
-        nc.sync.dma_start(offs_t[:], offs)
-        load_scales(0)
-        nc.sync.dma_start(cell_t[:], cell)
-        nc.sync.dma_start(out=w1raw[0, 1], in_=w1_rows[1, :, :, 0:P])
-        load_scales(1)
-        for g in range(PASSES):
-            nc.sync.dma_start(out=xw[g][:], in_=x_words[g].rearrange("p n t -> p (n t)").bitcast(I32))
-        nc.gpsimd.memset(xsm[:].rearrange("p g n -> p (g n)").bitcast(I32), 0)
-        nc.gpsimd.memset(up[0][:], 0.0)
-        ident = tile([P, P], F32, "ident")
-        make_identity(nc, ident[:])
-
-        xg = [tile([P, S], U32, "xg%d" % g) for g in range(PASSES)]
-        rounded = {}
-        codes = {}
-        scales = {}
         copy_on = {"scalar": nc.scalar.copy, "vector": nc.vector.tensor_copy}
 
-        def round_w1(t, g, engine):
-            rounded[t, g] = tile([P, P * PACK], BF16, "rounded%d%d" % (t, g))
+        offs_t = sb.tile([P, S // 16], U16, name="offs_t")
+        cell_t = sb.tile([P, S // 16], U16, name="cell_t")
+        xs = tile([P, T], U8, "xs")
+        xsm = tile([P, PASSES * S], U8, "xsm")
+        nc.gpsimd.memset(xs[:].bitcast(I32), 0)
+        nc.gpsimd.memset(xsm[:].bitcast(I32), 0)
+        up = [tile([P, U], F32, "up%d" % t) for t in range(PACK)]
+        for t in range(PACK):
+            nc.gpsimd.memset(up[t][:], 0.0)
+
+        w1_rows = w1.rearrange("(g p j) c -> g p j c", p=P, j=PACK)
+        w1raw = {}
+
+        def load_w1(a, g, dst):
+            w1raw[a, g] = dst.rearrange("p (j c) -> p j c", j=PACK)
+            nc.sync.dma_start(out=w1raw[a, g], in_=w1_rows[g, :, :, WIDE * a : WIDE * (a + 1)])
+
+        def load_x(g, name):
+            xw.append(tile([P, T], I32, name))
+            nc.sync.dma_start(out=xw[g][:], in_=x_words[g].rearrange("p n t -> p (n t)").bitcast(I32))
+
+        xw = []
+        load_w1(0, 0, tile([P, PACK * WIDE], F32, "w1raw0")[:])
+        nc.sync.dma_start(out=xs[0:P:4, :].bitcast(I32), in_=x_scales.rearrange("g q n -> (g q) n").bitcast(I32))
+        nc.sync.dma_start(offs_t[:], offs)
+        load_w1(0, 1, tile([P, PACK * WIDE], F32, "w1raw1")[:])
+        nc.sync.dma_start(cell_t[:], cell)
+        load_x(0, "xw0")
+        load_x(1, "xw1")
+
+        xsg = tile([P, S], U8, "xsg")
+        nc.vector.tensor_copy(xsg[:], xs[:].indirect(offs_t[:]))
+        xsp = tile([P, PASSES * S], U8, "xsp")
+        for g in range(PASSES):
+            nc.vector.tensor_copy(xsp[0:HP, S * g : S * (g + 1)].bitcast(I32), xsg[HP * g : HP * (g + 1), :].bitcast(I32))
+        for r in range(4):
+            nc.sync.dma_start(out=xsm[r:P:32, :].bitcast(I32), in_=xsp[4 * r : HP : 16, :].bitcast(I32))
+        late = tile([P, PASSES * PACK * WIDE], F32, "xsg")
+        for g in range(PASSES):
+            load_w1(1, g, late[:, PACK * WIDE * g : PACK * WIDE * (g + 1)])
+
+        rounded = [tile([P, H * PACK], BF16, "rounded%d" % g) for g in range(PASSES)]
+        codes = {}
+        scales = {}
+
+        def round_w1(a, g, engine, some):
             copy_on[engine](
-                rounded[t, g][:].rearrange("p (m i j) -> p m j i", i=PACK, j=PACK),
-                w1raw[t, g].rearrange("p j (m i) -> p m j i", i=PACK),
+                rounded[g][:].rearrange("p (t m j) -> p m j t", t=PACK, j=PACK)[:, HP * a : HP * (a + 1), :, some],
+                w1raw[a, g].rearrange("p j (m t) -> p m j t", t=PACK)[:, :, :, some],
             )
 
-        def round_pairs(g, engine):
-            rounded[2, g] = tile([P, 2 * P * PACK], BF16, "rounded2%d" % g)
-            copy_on[engine](
-                rounded[2, g][:].rearrange("p (u m e j) -> p m j u e", u=2, e=2, j=PACK),
-                w1raw[2, g].rearrange("p j (m u e) -> p m j u e", u=2, e=2),
-            )
+        def quantise_pairs(a, g):
+            c = tile([P, P], U32, "wc%d%d" % (a, g))
+            s = tile([P, P], U8, "ws%d%d" % (a, g))
+            for e in range(2):
+                c0 = H * e + WIDE * a
+                cols = slice(HP * e, HP * (e + 1))
+                nc.vector.quantize_mx(out=c[:, cols].bitcast(FP8X4), scales=s[:, cols], in_=rounded[g][:, c0 : c0 + WIDE])
+            codes[a, g] = c[:]
+            scales[a, g] = s[:]
 
-        def quantise(t, g, width):
-            c = tile([P, width], U32, "wc%d%d" % (t, g))
-            s = tile([P, width], U8, "ws%d%d" % (t, g))
-            nc.vector.quantize_mx(out=c[:].bitcast(FP8X4), scales=s[:], in_=rounded[t, g][:])
-            for i in range(width // P):
-                codes[t + i, g] = c[:, P * i : P * (i + 1)]
-                scales[t + i, g] = s[:, P * i : P * (i + 1)]
+        def quantise_planes(g):
+            c = tile([P, 2 * P], U32, "wc2%d" % g)
+            s = tile([P, 2 * P], U8, "ws2%d" % g)
+            nc.vector.quantize_mx(out=c[:].bitcast(FP8X4), scales=s[:], in_=rounded[g][:, 2 * H : 4 * H])
+            for e in range(2):
+                codes[2 + e, g] = c[:, P * e : P * (e + 1)]
+                scales[2 + e, g] = s[:, P * e : P * (e + 1)]
 
-        def quantise_w1(t, g):
-            quantise(t, g, P)
-
-        def quantise_pairs(g):
-            quantise(2, g, 2 * P)
-
+        xg = [tile([P, S], U32, "xg%d" % g) for g in range(PASSES)]
+        whole = slice(0, S)
         halves = [slice(0, HALF), slice(HALF, S)]
-        lists = [slice(0, HALF // 16), slice(HALF // 16, S // 16)]
 
-        def product(bank, t, g, b, opens=0):
+        def entries(part):
+            return slice(part.start // 16, part.stop // 16)
+
+        def product(bank, t, g, part):
             nc.tensor.matmul_mx(
                 out=bank[:], lhsT=codes[t, g].bitcast(FP8X4), lhsT_scale=scales[t, g],
-                rhs=xg[g][:, halves[b]].bitcast(FP8X4), rhs_scale=xsm[:, g, halves[b]],
-                start=(g == opens), stop=(g != opens),
+                rhs=xg[g][:, part].bitcast(FP8X4), rhs_scale=xsm[:, S * g + part.start : S * g + part.stop],
+                start=(g == 0), stop=(g == PASSES - 1),
             )
 
-        def turn(dst, src, start, stop):
-            nc.tensor.matmul(dst, lhsT=src, rhs=ident[:], is_transpose=True, start=start, stop=stop)
-
-        def scalar_scatter(t, b, h):
-            nc.scalar.activation(out=up[t][:].indirect(cell_t[:, lists[b]]), in_=h, func=COPY)
-
         for g in range(PASSES):
-            nc.vector.tensor_copy(xsg[:, g, :], xs[g][:].indirect(offs_t[:]))
-        for r in range(4):
-            row = ROW0 + STEP * r
-            nc.sync.dma_start(
-                out=xsm[r:P:32, :, :].rearrange("p g n -> p (g n)").bitcast(I32),
-                in_=xsg[row : row + 12 * STEP + 1 : 4 * STEP, :, :].rearrange("p g n -> p (g n)").bitcast(I32),
-            )
-        late = tile([P, PASSES * PACK * P], F32, "xs1")
-        for g in range(PASSES):
-            w1raw[1, g] = late[:, PACK * P * g : PACK * P * (g + 1)].rearrange("p (j c) -> p j c", j=PACK)
-            nc.sync.dma_start(out=w1raw[1, g], in_=w1_rows[g, :, :, P : 2 * P])
-        round_w1(0, 0, "scalar")
-        quantise_w1(0, 0)
+            round_w1(0, g, "scalar", slice(0, PACK))
+            quantise_pairs(0, g)
         nc.vector.tensor_copy(xg[0][:], xw[0][:].bitcast(U32).indirect(offs_t[:]))
-        late = tile([P, PASSES * PACK * 2 * P], F32, "xw0")
-        for g in range(PASSES):
-            w1raw[2, g] = late[:, PACK * 2 * P * g : PACK * 2 * P * (g + 1)].rearrange("p (j c) -> p j c", j=PACK)
-            nc.sync.dma_start(out=w1raw[2, g], in_=w1_rows[g, :, :, 2 * P : H])
-        round_w1(0, 1, "scalar")
-        quantise_w1(0, 1)
-        for name in ("w1raw00", "w1raw01", "rounded01"):
-            up.append(tile([P, U], F32, name))
-            nc.scalar.copy(up[-1][:], up[0][:])
-        bank = {(0, b): ps.tile([P, HALF], F32, name="x%d" % b) for b in range(2)}
-        for b in range(2):
-            nc.vector.tensor_copy(xg[1][:, halves[b]], xw[1][:].bitcast(U32).indirect(offs_t[:, lists[b]]))
-            for g in (b, 1 - b):
-                product(bank[0, b], 0, g, b, opens=b)
+        skip_rows = skip.rearrange("(q t) v -> t q v", t=PACK)
+        skip_t = {}
+        for a in range(2):
+            skip_t[a] = tile([P, U], F32, "w1raw%d" % a)
+            for e in range(2):
+                nc.sync.dma_start(out=skip_t[a][HP * e : HP * (e + 1), :], in_=skip_rows[e, HP * a : HP * (a + 1), :])
+        skip_t[3] = tile([P, U], F32, "xw0")
+        nc.sync.dma_start(out=skip_t[3][:], in_=skip_rows[3])
 
-        skip_all = tile([P, 4 * U], F32, "xw1")
-        skip_t = [skip_all[:, U * t : U * (t + 1)] for t in range(4)]
-        for t in range(2):
-            nc.sync.dma_start(out=skip_t[t], in_=skip[P * t : P * (t + 1), :])
-        skip_pairs = skip[2 * P : H, :].rearrange("(m u e) v -> e m u v", u=2, e=2)
-        for e in range(2):
-            nc.sync.dma_start(
-                out=skip_all[e:P:2, 2 * U : 4 * U].rearrange("p (u v) -> p u v", u=2), in_=skip_pairs[e]
-            )
+        bank = {}
+        first = [slice(0, P), slice(P, HALF), slice(HALF, S)]
+        for part in (first[0], slice(P, S)):
+            nc.vector.tensor_copy(xg[1][:, part], xw[1][:].bitcast(U32).indirect(offs_t[:, entries(part)]))
+        for b, part in enumerate(first):
+            bank[0, b] = ps.tile([P, part.stop - part.start], F32, name="b%d" % b)
+            for g in range(PASSES):
+                product(bank[0, b], 0, g, part)
+        skip_t[2] = tile([P, U], F32, "xw1")
+        nc.sync.dma_start(out=skip_t[2][:], in_=skip_rows[2])
 
-        h = tile([P, P], F32, "h00")
-        nc.vector.tensor_copy(h[:], bank[0, 0][:, 0:P])
-        nc.vector.tensor_copy(up[0][:].indirect(cell_t[:, 0 : P // 16]), h[:])
         for b in range(2):
-            bank[1, b] = ps.tile([P, HALF], F32, name="x%d" % (2 + b))
+            bank[1, b] = ps.tile([P, HALF], F32, name="b%d" % (3 + b))
+        for t in (2, 3):
+            bank[t] = ps.tile([P, S], F32, name="b%d" % (3 + t))
+        round_w1(1, 0, "vector", slice(0, PACK))
+        quantise_pairs(1, 0)
+        for b in range(2):
+            product(bank[1, b], 1, 0, halves[b])
+        round_w1(1, 1, "vector", slice(0, 2))
+        quantise_pairs(1, 1)
+        for b in range(2):
+            product(bank[1, b], 1, 1, halves[b])
+        round_w1(1, 1, "vector", slice(2, PACK))
         for g in range(PASSES):
-            round_w1(1, g, "scalar")
-            quantise_w1(1, g)
-            for b in range(2):
-                product(bank[1, b], 1, g, b)
-        h = tile([P, S - P], F32, "xs1")
-        nc.scalar.copy(h[:, 0:P], bank[0, 0][:, P:HALF])
-        nc.scalar.copy(h[:, P : S - P], bank[0, 1][:])
-        nc.vector.tensor_copy(up[0][:].indirect(cell_t[:, P // 16 : S // 16]), h[:])
-        round_pairs(0, "scalar")
-        h = tile([P, HALF], F32, "h10")
-        nc.scalar.copy(h[:], bank[1, 0][:])
-        scalar_scatter(1, 0, h[:])
-        h = tile([P, HALF], F32, "h11")
-        nc.scalar.copy(h[:], bank[1, 1][:])
-        scalar_scatter(1, 1, h[:])
-        round_pairs(1, "vector")
-        for g in range(PASSES):
-            quantise_pairs(g)
+            quantise_planes(g)
         for t in (3, 2):
-            for b in range(2):
-                bank[t, b] = ps.tile([P, HALF], F32, name="x%d" % (2 * (3 - t) + b))
-            for b in range(2):
-                for g in (3 - t, t - 2):
-                    product(bank[t, b], t, g, b, opens=3 - t)
-        rows = {}
-
-        def add_skip(t, s, engine, name):
-            side = slice(SIDE * s, SIDE * (s + 1))
-            rows[t, s] = tile([P, SIDE], BF16, name)
-            engine.tensor_tensor(rows[t, s][:], up[t][:, side], skip_t[t][:, side], ADD)
-
-        add_skip(0, 0, nc.vector, "rows00")
-        h = tile([P, S], F32, "h3")
-        for b in range(2):
-            nc.vector.tensor_copy(h[:, halves[b]], bank[3, b][:])
-        nc.vector.tensor_copy(up[3][:].indirect(cell_t[:]), h[:])
-        for b in range(2):
-            h = tile([P, HALF], F32, "h2%d" % b)
-            nc.scalar.copy(h[:], bank[2, b][:])
-            scalar_scatter(2, b, h[:])
-        add_skip(0, 1, nc.gpsimd, "rounded21")
-        for s in range(2):
-            add_skip(1, s, nc.gpsimd, "rows1%d" % s)
-
-        w2w = tile([P, 2, 2, 2 * N], U8, "wc10")
-        nc.gpsimd.memset(w2w[:].rearrange("p s a c -> p (s a c)").bitcast(I32), 0)
-        for s in range(2):
-            nc.sync.dma_start(
-                out=w2w[HP * s : HP * (s + 1), s, :, :].bitcast(I32),
-                in_=w2_words[0].bitcast(I32).rearrange("(a p) c -> p a c", a=2),
-            )
-        w2s = tile([P, 2, N], U8, "rounded10")
-        nc.gpsimd.memset(w2s[:].rearrange("p a c -> p (a c)").bitcast(I32), 0)
-        scale_rows = w2_scales[0].bitcast(I32).rearrange("(a q r) c -> q r a c", a=2, q=2)
+            for g in range(PASSES):
+                product(bank[t], t, g, whole)
+        w2w = tile([P, 2 * N], U8, "xsg")
+        nc.sync.dma_start(out=w2w[:].bitcast(I32), in_=w2_words[0].bitcast(I32))
+        w2s = tile([P, N], U8, "rounded0")
+        nc.gpsimd.memset(w2s[:].bitcast(I32), 0)
         for q in range(4):
-            nc.sync.dma_start(out=w2s[32 * q : 32 * q + 4, :, :].bitcast(I32), in_=scale_rows[q % 2])
+            nc.sync.dma_start(out=w2s[32 * q : 32 * q + 4, :].bitcast(I32), in_=w2_scales[0].bitcast(I32)[4 * q : 4 * q + 4, :])
 
-        planes = tile([P, PACK * SIDE], BF16, "planes")
-        for t in range(2):
+        def scalar_scatter(t, part, h):
+            nc.scalar.activation(out=up[t][:].indirect(cell_t[:, entries(part)]), in_=h, func=COPY)
+
+        def vector_scatter(t, part, h):
+            nc.vector.tensor_copy(up[t][:].indirect(cell_t[:, entries(part)]), h)
+
+        h = tile([P, P], F32, "hs0")
+        nc.scalar.copy(h[:], bank[0, 0][:])
+        scalar_scatter(0, first[0], h[:])
+        h = tile([P, S - P], F32, "hs0")
+        nc.scalar.copy(h[:, 0:P], bank[0, 1][:])
+        nc.scalar.copy(h[:, P : S - P], bank[0, 2][:])
+        scalar_scatter(0, slice(P, S), h[:])
+        h = tile([P, HALF], F32, "hv0")
+        nc.vector.tensor_copy(h[:], bank[1, 0][:])
+        vector_scatter(1, halves[0], h[:])
+        h = tile([P, HALF], F32, "hs1")
+        nc.scalar.copy(h[:], bank[1, 1][:])
+        scalar_scatter(1, halves[1], h[:])
+        h = tile([P, S], F32, "hv0")
+        nc.vector.tensor_copy(h[:], bank[3][:])
+        vector_scatter(3, whole, h[:])
+        h = tile([P, S], F32, "hs0")
+        nc.scalar.copy(h[:], bank[2][:])
+        for b in range(2):
+            scalar_scatter(2, halves[b], h[:, halves[b]])
+
+        planes = [tile([P, PACK, SIDE], BF16, "planes%d" % s) for s in range(2)]
+
+        def add_skip(engine, t, dst, v0, width):
+            engine.tensor_tensor(dst, up[t][:, v0 : v0 + width], skip_t[t][:, v0 : v0 + width], ADD)
+
+        for a in range(2):
             for s in range(2):
-                p0 = HP * s + QP * t
-                for j in range(PACK):
-                    nc.sync.dma_start(out=planes[p0 : p0 + QP, SIDE * j : SIDE * (j + 1)], in_=rows[t, s][j:P:PACK, :])
+                rows = tile([P, SIDE], BF16, "rows%d%d" % (a, s))
+                add_skip(nc.gpsimd, a, rows[:], SIDE * s, SIDE)
+                for e in range(2):
+                    nc.sync.dma_start(out=planes[s][HP * a : HP * (a + 1), e, :], in_=rows[HP * e : HP * (e + 1), :])
+        for s in range(2):
+            add_skip(nc.vector, 3, planes[s][:, 3, :], SIDE * s, SIDE)
+        for d in range(4):
+            s, c0 = divmod(CHUNK * d, SIDE)
+            add_skip(nc.vector, 2, planes[s][:, 2, c0 : c0 + CHUNK], CHUNK * d, CHUNK)
 
-        zt = {(t, j): tile([P, P], F32, "zt%d%d" % (t, j)) for t in (2, 3) for j in range(4)}
-        early = [ps.tile([P, 2, 2, P], F32, name="x%d" % d) for d in range(2)]
-        sums = {(3, j): early[j // 2][:, j % 2, :, :] for j in range(4)}
-        for j in range(4):
-            sums[2, j] = ps.tile([P, 2, P], F32, name="s%d" % j)[:]
-
-        def turn_into_sums(t, src, first):
-            blocks = 4 if t == 3 else 2
-            for i in range(8):
-                j, s = divmod(i, 2)
-                v0 = SIDE * s + P * j
-                turn(sums[t, j][:, s, :], src[:, v0 : v0 + P], first and i % blocks == 0, not first and i % blocks == blocks - 1)
-
-        def round_sums(t, j, engine):
-            copy_on[engine](zt[t, j][:].bitcast(BF16), sums[t, j].rearrange("p s c -> p (s c)"))
-
-        for t in (3, 2):
-            turn_into_sums(t, skip_t[t], True)
-        turn_into_sums(3, up[3], False)
-        for j in range(4):
-            round_sums(3, j, "vector")
-        back = [ps.tile([P, 2, P], F32, name="x%d" % ((j + 2) % 4)) for j in range(4)]
-        for j in range(4):
-            turn(back[j][:, 1, :], zt[3, j][:], True, True)
-        turn_into_sums(2, up[2], False)
-        for j in range(4):
-            round_sums(2, j, "scalar")
-
-        def quantise_z(z, zc, scale_name):
-            zs = tile([P, zc.shape[1]], U8, scale_name)
-            nc.vector.quantize_mx(out=zc.bitcast(FP8X4), scales=zs[:], in_=z.rearrange("p v t -> p (v t)"))
-            return zc, zs[:]
-
-        first = []
-        chunks = []
-        woven = tile([P, SIDE * PACK], BF16, "rounded01")
-        for d in range(2):
-            z = woven[:, CHUNK * PACK * d : CHUNK * PACK * (d + 1)].rearrange("p (v t) -> p v t", t=PACK)
-            nc.vector.tensor_copy(
-                z.rearrange("p (c i) t -> p c t i", i=PACK),
-                planes[:].rearrange("p (t c i) -> p c t i", t=PACK, i=PACK)[:, CHUNK // PACK * d : CHUNK // PACK * (d + 1), :, :],
+        weave_on = ("scalar", "scalar", "vector", "vector")
+        result_on = ("scalar", "scalar", "scalar", "vector")
+        woven = []
+        for d in range(4):
+            s, c0 = divmod(CHUNK * d, SIDE)
+            woven.append(tile([P, CHUNK * PACK], BF16, "woven%d" % d))
+            copy_on[weave_on[d]](
+                woven[d][:].rearrange("p (c i t) -> p c t i", i=PACK, t=PACK),
+                planes[s][:, :, c0 : c0 + CHUNK].rearrange("p t (c i) -> p c t i", i=PACK),
             )
-            chunks.append(z)
-        for d in range(2):
-            first.append(quantise_z(chunks[d], tile([P, CHUNK], U32, "zc%d" % d)[:], "zs%d" % d))
-        second = []
-        last_codes = tile([P, SIDE], U32, "rounded01")
-        for d in range(2):
-            words = tile([P, 2 * CHUNK], F32, "zb%d" % d)
-            for i in range(2):
-                j = 2 * d + i
-                turn(back[j][:, 0, :], zt[2, j][:], True, True)
-                nc.scalar.copy(
-                    words[:, CHUNK * i : CHUNK * (i + 1)].rearrange("p (v u) -> p v u", u=2),
-                    back[j][:].rearrange("p u v -> p v u"),
-                )
-            z = words[:].bitcast(BF16).rearrange("p (v t) -> p v t", t=PACK)
-            second.append(quantise_z(z, last_codes[:, CHUNK * d : CHUNK * (d + 1)], "zr%d" % d))
-
-        def product2(acc, a, s, operand, start, stop):
+        for d in range(4):
+            zc = tile([P, CHUNK], U32, "zc%d" % d)
+            zs = tile([P, CHUNK], U8, "planes1" if d == 0 else "zs%d" % d)
+            nc.vector.quantize_mx(out=zc[:].bitcast(FP8X4), scales=zs[:], in_=woven[d][:])
+            acc = ps.tile([P, CHUNK], F32, name="b%d" % d)
             nc.tensor.matmul_mx(
-                out=acc, lhsT=w2w[:, s, a, :].bitcast(FP4X4), lhsT_scale=w2s[:, a, :],
-                rhs=operand[0].bitcast(FP8X4), rhs_scale=operand[1], start=start, stop=stop,
+                out=acc[:], lhsT=w2w[:].bitcast(FP4X4), lhsT_scale=w2s[:],
+                rhs=zc[:].bitcast(FP8X4), rhs_scale=zs[:], start=True, stop=True,
             )
-
-        for d in range(2):
-            accs = [ps.tile([P, CHUNK], F32, name="s%d" % (2 * d + s)) for s in range(2)]
-            for s in range(2):
-                product2(accs[s][:], 0, s, first[d], True, False)
-            for s in range(2):
-                product2(accs[s][:], 1, s, second[d], False, True)
-            for s, engine in ((0, "scalar"), (1, "vector")):
-                res = tile([P, CHUNK], F32, "res%d%d" % (d, s))
-                copy_on[engine](res[:], accs[s][:])
-                v0 = SIDE * s + CHUNK * d
-                nc.sync.dma_start(out=out[:, v0 : v0 + CHUNK], in_=res[:])
+            res = tile([P, CHUNK], F32, "res%d" % d)
+            copy_on[result_on[d]](res[:], acc[:])
+            nc.sync.dma_start(out=out[:, CHUNK * d : CHUNK * (d + 1)], in_=res[:])

@@ -77,37 +77,37 @@ def tile_picked_unet_none_p_kernel(
             nc.vector.tensor_copy(xsp[0:HP, S * g : S * (g + 1)].bitcast(I32), xsg[HP * g : HP * (g + 1), :].bitcast(I32))
         for r in range(4):
             nc.sync.dma_start(out=xsm[r:P:32, :].bitcast(I32), in_=xsp[4 * r : HP : 16, :].bitcast(I32))
-        late = tile([P, PASSES * PACK * WIDE], F32, "xsg")
+        second = tile([P, PASSES * PACK * WIDE], F32, "xsg")
         for g in range(PASSES):
-            load_w1(1, g, late[:, PACK * WIDE * g : PACK * WIDE * (g + 1)])
+            load_w1(1, g, second[:, PACK * WIDE * g : PACK * WIDE * (g + 1)])
 
-        rounded = [tile([P, H * PACK], BF16, "rounded%d" % g) for g in range(PASSES)]
+        pairs = {}
+        rounded = [tile([P, 2 * P * PACK], BF16, "rounded%d" % g) for g in range(PASSES)]
         codes = {}
         scales = {}
 
-        def round_w1(a, g, engine, some):
+        def columns(a, g):
+            return w1raw[a, g].rearrange("p j (m t) -> p m j t", t=PACK)
+
+        def round_pairs(a, g, engine):
+            pairs[a, g] = tile([P, P * PACK], BF16, "pairs%d%d" % (a, g))
+            order = ("p (m e j) -> p m j e", "p (e m j) -> p m j e")[a]
+            copy_on[engine](pairs[a, g][:].rearrange(order, e=2, j=PACK), columns(a, g)[:, :, :, 0:2])
+
+        def round_planes(a, g, engine):
             copy_on[engine](
-                rounded[g][:].rearrange("p (t m j) -> p m j t", t=PACK, j=PACK)[:, HP * a : HP * (a + 1), :, some],
-                w1raw[a, g].rearrange("p j (m t) -> p m j t", t=PACK)[:, :, :, some],
+                rounded[g][:].rearrange("p (e m j) -> p m j e", e=2, j=PACK)[:, HP * a : HP * (a + 1), :, :],
+                columns(a, g)[:, :, :, 2:PACK],
             )
 
-        def quantise_pairs(a, g):
-            c = tile([P, P], U32, "wc%d%d" % (a, g))
-            s = tile([P, P], U8, "ws%d%d" % (a, g))
-            for e in range(2):
-                c0 = H * e + WIDE * a
-                cols = slice(HP * e, HP * (e + 1))
-                nc.vector.quantize_mx(out=c[:, cols].bitcast(FP8X4), scales=s[:, cols], in_=rounded[g][:, c0 : c0 + WIDE])
-            codes[a, g] = c[:]
-            scales[a, g] = s[:]
-
-        def quantise_planes(g):
-            c = tile([P, 2 * P], U32, "wc2%d" % g)
-            s = tile([P, 2 * P], U8, "ws2%d" % g)
-            nc.vector.quantize_mx(out=c[:].bitcast(FP8X4), scales=s[:], in_=rounded[g][:, 2 * H : 4 * H])
-            for e in range(2):
-                codes[2 + e, g] = c[:, P * e : P * (e + 1)]
-                scales[2 + e, g] = s[:, P * e : P * (e + 1)]
+        def quantise(src, t, g):
+            width = src.shape[1] // PACK
+            c = tile([P, width], U32, "wc%d%d" % (t, g))
+            s = tile([P, width], U8, "ws%d%d" % (t, g))
+            nc.vector.quantize_mx(out=c[:].bitcast(FP8X4), scales=s[:], in_=src[:])
+            for e in range(width // P):
+                codes[t + e, g] = c[:, P * e : P * (e + 1)]
+                scales[t + e, g] = s[:, P * e : P * (e + 1)]
 
         xg = [tile([P, S], U32, "xg%d" % g) for g in range(PASSES)]
         whole = slice(0, S)
@@ -124,15 +124,17 @@ def tile_picked_unet_none_p_kernel(
             )
 
         for g in range(PASSES):
-            round_w1(0, g, "scalar", slice(0, PACK))
-            quantise_pairs(0, g)
+            round_pairs(0, g, "scalar")
+            quantise(pairs[0, g], 0, g)
+            round_planes(0, g, "scalar")
         nc.vector.tensor_copy(xg[0][:], xw[0][:].bitcast(U32).indirect(offs_t[:]))
         skip_rows = skip.rearrange("(q t) v -> t q v", t=PACK)
         skip_t = {}
-        for a in range(2):
-            skip_t[a] = tile([P, U], F32, "w1raw%d" % a)
-            for e in range(2):
-                nc.sync.dma_start(out=skip_t[a][HP * e : HP * (e + 1), :], in_=skip_rows[e, HP * a : HP * (a + 1), :])
+        skip_t[0] = tile([P, U], F32, "w1raw0")
+        nc.sync.dma_start(out=skip_t[0][:], in_=skip.rearrange("(q t) v -> q t v", t=PACK)[0:HP, 0:2, :])
+        skip_t[1] = tile([P, U], F32, "w1raw1")
+        for e in range(2):
+            nc.sync.dma_start(out=skip_t[1][HP * e : HP * (e + 1), :], in_=skip_rows[e, HP:P, :])
         skip_t[3] = tile([P, U], F32, "xw0")
         nc.sync.dma_start(out=skip_t[3][:], in_=skip_rows[3])
 
@@ -141,9 +143,12 @@ def tile_picked_unet_none_p_kernel(
         for part in (first[0], slice(P, S)):
             nc.vector.tensor_copy(xg[1][:, part], xw[1][:].bitcast(U32).indirect(offs_t[:, entries(part)]))
         for b, part in enumerate(first):
-            bank[0, b] = ps.tile([P, part.stop - part.start], F32, name="b%d" % b)
+            bank[0, b] = ps.tile([P, part.stop - part.start], F32, name="b%d" % (b // 2))
             for g in range(PASSES):
                 product(bank[0, b], 0, g, part)
+            if b == 0:
+                h_first = tile([P, P], F32, "hs2")
+                nc.scalar.copy(h_first[:], bank[0, 0][:])
         skip_t[2] = tile([P, U], F32, "xw1")
         nc.sync.dma_start(out=skip_t[2][:], in_=skip_rows[2])
 
@@ -151,18 +156,19 @@ def tile_picked_unet_none_p_kernel(
             bank[1, b] = ps.tile([P, HALF], F32, name="b%d" % (3 + b))
         for t in (2, 3):
             bank[t] = ps.tile([P, S], F32, name="b%d" % (3 + t))
-        round_w1(1, 0, "vector", slice(0, PACK))
-        quantise_pairs(1, 0)
+        round_pairs(1, 0, "vector")
+        round_planes(1, 0, "vector")
+        quantise(pairs[1, 0], 1, 0)
         for b in range(2):
             product(bank[1, b], 1, 0, halves[b])
-        round_w1(1, 1, "vector", slice(0, 2))
-        quantise_pairs(1, 1)
+        round_pairs(1, 1, "vector")
+        quantise(rounded[0], 2, 0)
+        quantise(pairs[1, 1], 1, 1)
         for b in range(2):
             product(bank[1, b], 1, 1, halves[b])
-        round_w1(1, 1, "vector", slice(2, PACK))
-        for g in range(PASSES):
-            quantise_planes(g)
-        for t in (3, 2):
+        round_planes(1, 1, "vector")
+        quantise(rounded[1], 2, 1)
+        for t in (2, 3):
             for g in range(PASSES):
                 product(bank[t], t, g, whole)
         w2w = tile([P, 2 * N], U8, "xsg")
@@ -178,26 +184,22 @@ def tile_picked_unet_none_p_kernel(
         def vector_scatter(t, part, h):
             nc.vector.tensor_copy(up[t][:].indirect(cell_t[:, entries(part)]), h)
 
-        h = tile([P, P], F32, "hs0")
-        nc.scalar.copy(h[:], bank[0, 0][:])
-        scalar_scatter(0, first[0], h[:])
+        scalar_scatter(0, first[0], h_first[:])
         h = tile([P, S - P], F32, "hs0")
         nc.scalar.copy(h[:, 0:P], bank[0, 1][:])
         nc.scalar.copy(h[:, P : S - P], bank[0, 2][:])
         scalar_scatter(0, slice(P, S), h[:])
-        h = tile([P, HALF], F32, "hv0")
-        nc.vector.tensor_copy(h[:], bank[1, 0][:])
-        vector_scatter(1, halves[0], h[:])
-        h = tile([P, HALF], F32, "hs1")
-        nc.scalar.copy(h[:], bank[1, 1][:])
-        scalar_scatter(1, halves[1], h[:])
         h = tile([P, S], F32, "hv0")
-        nc.vector.tensor_copy(h[:], bank[3][:])
-        vector_scatter(3, whole, h[:])
-        h = tile([P, S], F32, "hs0")
-        nc.scalar.copy(h[:], bank[2][:])
         for b in range(2):
-            scalar_scatter(2, halves[b], h[:, halves[b]])
+            nc.vector.tensor_copy(h[:, halves[b]], bank[1, b][:])
+        vector_scatter(1, slice(0, S - P), h[:, 0 : S - P])
+        late = tile([P, 2 * S], F32, "late")
+        for i, t in enumerate((2, 3)):
+            nc.scalar.copy(late[:, S * i : S * (i + 1)], bank[t][:])
+        scalar_scatter(2, first[0], late[:, 0:P])
+        scalar_scatter(1, slice(S - P, S), h[:, S - P : S])
+        vector_scatter(3, whole, late[:, S : 2 * S])
+        scalar_scatter(2, slice(P, S), late[:, P:S])
 
         planes = [tile([P, PACK, SIDE], BF16, "planes%d" % s) for s in range(2)]
 
@@ -205,36 +207,49 @@ def tile_picked_unet_none_p_kernel(
             engine.tensor_tensor(dst, up[t][:, v0 : v0 + width], skip_t[t][:, v0 : v0 + width], ADD)
 
         for a in range(2):
-            for s in range(2):
+            for s in (1, 0):
                 rows = tile([P, SIDE], BF16, "rows%d%d" % (a, s))
                 add_skip(nc.gpsimd, a, rows[:], SIDE * s, SIDE)
                 for e in range(2):
-                    nc.sync.dma_start(out=planes[s][HP * a : HP * (a + 1), e, :], in_=rows[HP * e : HP * (e + 1), :])
+                    dst = planes[s][HP * a : HP * (a + 1), e, :]
+                    if a == 0:
+                        nc.sync.dma_start(out=dst, in_=rows[e:P:2, :])
+                    elif s == 1:
+                        nc.sync.dma_start(out=dst, in_=rows[HP * e : HP * (e + 1), :])
+                    else:
+                        nc.scalar.copy(dst.bitcast(F32), rows[HP * e : HP * (e + 1), :].bitcast(F32))
         for s in range(2):
             add_skip(nc.vector, 3, planes[s][:, 3, :], SIDE * s, SIDE)
         for d in range(4):
             s, c0 = divmod(CHUNK * d, SIDE)
             add_skip(nc.vector, 2, planes[s][:, 2, c0 : c0 + CHUNK], CHUNK * d, CHUNK)
 
-        weave_on = ("scalar", "scalar", "vector", "vector")
-        result_on = ("scalar", "scalar", "scalar", "vector")
+        chunks = [
+            (0, CHUNK, "scalar", "scalar"),
+            (CHUNK, CHUNK, "scalar", "scalar"),
+            (2 * CHUNK, CHUNK, "vector", "scalar"),
+            (3 * CHUNK, P, "vector", "vector"),
+            (3 * CHUNK + P, P, "scalar", "vector"),
+        ]
         woven = []
-        for d in range(4):
-            s, c0 = divmod(CHUNK * d, SIDE)
-            woven.append(tile([P, CHUNK * PACK], BF16, "woven%d" % d))
-            copy_on[weave_on[d]](
+        for d, (v0, width, weaver, copier) in enumerate(chunks):
+            s, c0 = divmod(v0, SIDE)
+            woven.append(tile([P, width * PACK], BF16, "woven%d" % d))
+            copy_on[weaver](
                 woven[d][:].rearrange("p (c i t) -> p c t i", i=PACK, t=PACK),
-                planes[s][:, :, c0 : c0 + CHUNK].rearrange("p t (c i) -> p c t i", i=PACK),
+                planes[s][:, :, c0 : c0 + width].rearrange("p t (c i) -> p c t i", i=PACK),
             )
-        for d in range(4):
-            zc = tile([P, CHUNK], U32, "zc%d" % d)
-            zs = tile([P, CHUNK], U8, "planes1" if d == 0 else "zs%d" % d)
+        accs = []
+        for d, (v0, width, weaver, copier) in enumerate(chunks):
+            zc = tile([P, width], U32, "zc%d" % d)
+            zs = tile([P, width], U8, "zs%d" % d)
             nc.vector.quantize_mx(out=zc[:].bitcast(FP8X4), scales=zs[:], in_=woven[d][:])
-            acc = ps.tile([P, CHUNK], F32, name="b%d" % d)
+            accs.append(ps.tile([P, width], F32, name="b%d" % d))
             nc.tensor.matmul_mx(
-                out=acc[:], lhsT=w2w[:].bitcast(FP4X4), lhsT_scale=w2s[:],
+                out=accs[d][:], lhsT=w2w[:].bitcast(FP4X4), lhsT_scale=w2s[:],
                 rhs=zc[:].bitcast(FP8X4), rhs_scale=zs[:], start=True, stop=True,
             )
-            res = tile([P, CHUNK], F32, "res%d" % d)
-            copy_on[result_on[d]](res[:], acc[:])
-            nc.sync.dma_start(out=out[:, CHUNK * d : CHUNK * (d + 1)], in_=res[:])
+        for d, (v0, width, weaver, copier) in enumerate(chunks):
+            res = tile([P, width], F32, "res%d" % d)
+            copy_on[copier](res[:], accs[d][:])
+            nc.sync.dma_start(out=out[:, v0 : v0 + width], in_=res[:])

@@ -91,8 +91,7 @@ def tile_picked_unet_none_p_kernel(
 
         def round_pairs(a, g, engine):
             pairs[a, g] = tile([P, P * PACK], BF16, "pairs%d%d" % (a, g))
-            order = ("p (m e j) -> p m j e", "p (e m j) -> p m j e")[a]
-            copy_on[engine](pairs[a, g][:].rearrange(order, e=2, j=PACK), columns(a, g)[:, :, :, 0:2])
+            copy_on[engine](pairs[a, g][:].rearrange("p (m e j) -> p m j e", e=2, j=PACK), columns(a, g)[:, :, :, 0:2])
 
         def round_planes(a, g, engine):
             copy_on[engine](
@@ -132,11 +131,9 @@ def tile_picked_unet_none_p_kernel(
         skip_t = {}
         skip_t[0] = tile([P, U], F32, "w1raw0")
         nc.sync.dma_start(out=skip_t[0][:], in_=skip.rearrange("(q t) v -> q t v", t=PACK)[0:HP, 0:2, :])
-        skip_t[1] = tile([P, U], F32, "w1raw1")
-        for e in range(2):
-            nc.sync.dma_start(out=skip_t[1][HP * e : HP * (e + 1), :], in_=skip_rows[e, HP:P, :])
-        skip_t[3] = tile([P, U], F32, "xw0")
-        nc.sync.dma_start(out=skip_t[3][:], in_=skip_rows[3])
+        for t, name in ((2, "w1raw1"), (3, "xw0")):
+            skip_t[t] = tile([P, U], F32, name)
+            nc.sync.dma_start(out=skip_t[t][:], in_=skip_rows[t])
 
         bank = {}
         first = [slice(0, P), slice(P, HALF), slice(HALF, S)]
@@ -149,8 +146,8 @@ def tile_picked_unet_none_p_kernel(
             if b == 0:
                 h_first = tile([P, P], F32, "hs2")
                 nc.scalar.copy(h_first[:], bank[0, 0][:])
-        skip_t[2] = tile([P, U], F32, "xw1")
-        nc.sync.dma_start(out=skip_t[2][:], in_=skip_rows[2])
+        skip_t[1] = tile([P, U], F32, "xw1")
+        nc.sync.dma_start(out=skip_t[1][:], in_=skip.rearrange("(q t) v -> q t v", t=PACK)[HP:P, 0:2, :])
 
         for b in range(2):
             bank[1, b] = ps.tile([P, HALF], F32, name="b%d" % (3 + b))
@@ -192,13 +189,13 @@ def tile_picked_unet_none_p_kernel(
         h = tile([P, S], F32, "hv0")
         for b in range(2):
             nc.vector.tensor_copy(h[:, halves[b]], bank[1, b][:])
-        vector_scatter(1, slice(0, S - P), h[:, 0 : S - P])
+        vector_scatter(1, whole, h[:])
         late = tile([P, 2 * S], F32, "late")
         for i, t in enumerate((2, 3)):
             nc.scalar.copy(late[:, S * i : S * (i + 1)], bank[t][:])
         scalar_scatter(2, first[0], late[:, 0:P])
-        scalar_scatter(1, slice(S - P, S), h[:, S - P : S])
-        vector_scatter(3, whole, late[:, S : 2 * S])
+        scalar_scatter(3, first[0], late[:, S : S + P])
+        vector_scatter(3, slice(P, S), late[:, S + P : 2 * S])
         scalar_scatter(2, slice(P, S), late[:, P:S])
 
         planes = [tile([P, PACK, SIDE], BF16, "planes%d" % s) for s in range(2)]
@@ -207,29 +204,22 @@ def tile_picked_unet_none_p_kernel(
             engine.tensor_tensor(dst, up[t][:, v0 : v0 + width], skip_t[t][:, v0 : v0 + width], ADD)
 
         for a in range(2):
-            for s in (1, 0):
+            for s in range(2):
                 rows = tile([P, SIDE], BF16, "rows%d%d" % (a, s))
                 add_skip(nc.gpsimd, a, rows[:], SIDE * s, SIDE)
                 for e in range(2):
-                    dst = planes[s][HP * a : HP * (a + 1), e, :]
-                    if a == 0:
-                        nc.sync.dma_start(out=dst, in_=rows[e:P:2, :])
-                    elif s == 1:
-                        nc.sync.dma_start(out=dst, in_=rows[HP * e : HP * (e + 1), :])
-                    else:
-                        nc.scalar.copy(dst.bitcast(F32), rows[HP * e : HP * (e + 1), :].bitcast(F32))
-        for s in range(2):
-            add_skip(nc.vector, 3, planes[s][:, 3, :], SIDE * s, SIDE)
+                    nc.sync.dma_start(out=planes[s][HP * a : HP * (a + 1), e, :], in_=rows[e:P:2, :])
         for d in range(4):
             s, c0 = divmod(CHUNK * d, SIDE)
-            add_skip(nc.vector, 2, planes[s][:, 2, c0 : c0 + CHUNK], CHUNK * d, CHUNK)
+            for t in (3, 2):
+                add_skip(nc.vector, t, planes[s][:, t, c0 : c0 + CHUNK], CHUNK * d, CHUNK)
 
         chunks = [
             (0, CHUNK, "scalar", "scalar"),
             (CHUNK, CHUNK, "scalar", "scalar"),
-            (2 * CHUNK, CHUNK, "vector", "scalar"),
-            (3 * CHUNK, P, "vector", "vector"),
-            (3 * CHUNK + P, P, "scalar", "vector"),
+            (3 * CHUNK, CHUNK, "vector", "scalar"),
+            (2 * CHUNK, P, "scalar", "vector"),
+            (2 * CHUNK + P, P, "vector", "vector"),
         ]
         woven = []
         for d, (v0, width, weaver, copier) in enumerate(chunks):

@@ -81,32 +81,26 @@ def tile_picked_unet_none_p_kernel(
         for g in range(PASSES):
             load_w1(1, g, second[:, PACK * WIDE * g : PACK * WIDE * (g + 1)])
 
-        pairs = {}
-        rounded = [tile([P, 2 * P * PACK], BF16, "rounded%d" % g) for g in range(PASSES)]
-        codes = {}
-        scales = {}
+        rounded = {}
+        codes = {(t, g): tile([P, P], U32, "wc%d%d" % (t, g)) for t in range(PACK) for g in range(PASSES)}
+        scales = {(t, g): tile([P, P], U8, "ws%d%d" % (t, g)) for t in range(PACK) for g in range(PASSES)}
 
-        def columns(a, g):
-            return w1raw[a, g].rearrange("p j (m t) -> p m j t", t=PACK)
-
-        def round_pairs(a, g, engine):
-            pairs[a, g] = tile([P, P * PACK], BF16, "pairs%d%d" % (a, g))
-            copy_on[engine](pairs[a, g][:].rearrange("p (m e j) -> p m j e", e=2, j=PACK), columns(a, g)[:, :, :, 0:2])
-
-        def round_planes(a, g, engine):
+        def round_w1(a, g, engine):
+            rounded[a, g] = tile([P, PACK * WIDE], BF16, "rounded%d%d" % (a, g))
             copy_on[engine](
-                rounded[g][:].rearrange("p (e m j) -> p m j e", e=2, j=PACK)[:, HP * a : HP * (a + 1), :, :],
-                columns(a, g)[:, :, :, 2:PACK],
+                rounded[a, g][:].rearrange("p (t m j) -> p m j t", t=PACK, j=PACK),
+                w1raw[a, g].rearrange("p j (m t) -> p m j t", t=PACK),
             )
 
-        def quantise(src, t, g):
-            width = src.shape[1] // PACK
-            c = tile([P, width], U32, "wc%d%d" % (t, g))
-            s = tile([P, width], U8, "ws%d%d" % (t, g))
-            nc.vector.quantize_mx(out=c[:].bitcast(FP8X4), scales=s[:], in_=src[:])
-            for e in range(width // P):
-                codes[t + e, g] = c[:, P * e : P * (e + 1)]
-                scales[t + e, g] = s[:, P * e : P * (e + 1)]
+        def quantise(src, t, g, cols):
+            nc.vector.quantize_mx(out=codes[t, g][:, cols].bitcast(FP8X4), scales=scales[t, g][:, cols], in_=src)
+
+        def quantise_pair(a, g):
+            quantise(rounded[a, g][:, 0 : 2 * WIDE], a, g, slice(0, P))
+
+        def quantise_planes(a, g):
+            for t in (2, 3):
+                quantise(rounded[a, g][:, WIDE * t : WIDE * (t + 1)], t, g, slice(HP * a, HP * (a + 1)))
 
         xg = [tile([P, S], U32, "xg%d" % g) for g in range(PASSES)]
         whole = slice(0, S)
@@ -117,20 +111,21 @@ def tile_picked_unet_none_p_kernel(
 
         def product(bank, t, g, part):
             nc.tensor.matmul_mx(
-                out=bank[:], lhsT=codes[t, g].bitcast(FP8X4), lhsT_scale=scales[t, g],
+                out=bank[:], lhsT=codes[t, g][:].bitcast(FP8X4), lhsT_scale=scales[t, g][:],
                 rhs=xg[g][:, part].bitcast(FP8X4), rhs_scale=xsm[:, S * g + part.start : S * g + part.stop],
                 start=(g == 0), stop=(g == PASSES - 1),
             )
 
         for g in range(PASSES):
-            round_pairs(0, g, "scalar")
-            quantise(pairs[0, g], 0, g)
-            round_planes(0, g, "scalar")
+            round_w1(0, g, "scalar")
+            quantise_pair(0, g)
+            quantise_planes(0, g)
         nc.vector.tensor_copy(xg[0][:], xw[0][:].bitcast(U32).indirect(offs_t[:]))
         skip_rows = skip.rearrange("(q t) v -> t q v", t=PACK)
         skip_t = {}
         skip_t[0] = tile([P, U], F32, "w1raw0")
-        nc.sync.dma_start(out=skip_t[0][:], in_=skip.rearrange("(q t) v -> q t v", t=PACK)[0:HP, 0:2, :])
+        for e in range(2):
+            nc.sync.dma_start(out=skip_t[0][HP * e : HP * (e + 1), :], in_=skip_rows[e, 0:HP, :])
         for t, name in ((2, "w1raw1"), (3, "xw0")):
             skip_t[t] = tile([P, U], F32, name)
             nc.sync.dma_start(out=skip_t[t][:], in_=skip_rows[t])
@@ -147,30 +142,25 @@ def tile_picked_unet_none_p_kernel(
                 h_first = tile([P, P], F32, "hs2")
                 nc.scalar.copy(h_first[:], bank[0, 0][:])
         skip_t[1] = tile([P, U], F32, "xw1")
-        nc.sync.dma_start(out=skip_t[1][:], in_=skip.rearrange("(q t) v -> q t v", t=PACK)[HP:P, 0:2, :])
+        for e in range(2):
+            nc.sync.dma_start(out=skip_t[1][HP * e : HP * (e + 1), :], in_=skip_rows[e, HP:P, :])
 
         for b in range(2):
             bank[1, b] = ps.tile([P, HALF], F32, name="b%d" % (3 + b))
         for t in (2, 3):
             bank[t] = ps.tile([P, S], F32, name="b%d" % (3 + t))
-        round_pairs(1, 0, "vector")
-        round_planes(1, 0, "vector")
-        quantise(pairs[1, 0], 1, 0)
-        for b in range(2):
-            product(bank[1, b], 1, 0, halves[b])
-        round_pairs(1, 1, "vector")
-        quantise(rounded[0], 2, 0)
-        quantise(pairs[1, 1], 1, 1)
-        for b in range(2):
-            product(bank[1, b], 1, 1, halves[b])
-        round_planes(1, 1, "vector")
-        quantise(rounded[1], 2, 1)
+        for g in range(PASSES):
+            round_w1(1, g, "vector")
+            quantise_pair(1, g)
+            for b in range(2):
+                product(bank[1, b], 1, g, halves[b])
+            quantise_planes(1, g)
         for t in (2, 3):
             for g in range(PASSES):
                 product(bank[t], t, g, whole)
         w2w = tile([P, 2 * N], U8, "xsg")
         nc.sync.dma_start(out=w2w[:].bitcast(I32), in_=w2_words[0].bitcast(I32))
-        w2s = tile([P, N], U8, "rounded0")
+        w2s = tile([P, N], U8, "rounded10")
         nc.gpsimd.memset(w2s[:].bitcast(I32), 0)
         for q in range(4):
             nc.sync.dma_start(out=w2s[32 * q : 32 * q + 4, :].bitcast(I32), in_=w2_scales[0].bitcast(I32)[4 * q : 4 * q + 4, :])
@@ -208,7 +198,7 @@ def tile_picked_unet_none_p_kernel(
                 rows = tile([P, SIDE], BF16, "rows%d%d" % (a, s))
                 add_skip(nc.gpsimd, a, rows[:], SIDE * s, SIDE)
                 for e in range(2):
-                    nc.sync.dma_start(out=planes[s][HP * a : HP * (a + 1), e, :], in_=rows[e:P:2, :])
+                    nc.sync.dma_start(out=planes[s][HP * a : HP * (a + 1), e, :], in_=rows[HP * e : HP * (e + 1), :])
         for d in range(4):
             s, c0 = divmod(CHUNK * d, SIDE)
             for t in (3, 2):

@@ -92,6 +92,12 @@ def tile_picked_unet_none_p_kernel(
                 w1raw[a, g].rearrange("p j (m t) -> p m j t", t=PACK),
             )
 
+        def round_first(g):
+            rounded[0, g] = tile([P, PACK * WIDE], BF16, "rounded0%d" % g)
+            columns = w1raw[0, g].rearrange("p j (m t) -> p m j t", t=PACK)
+            nc.scalar.copy(rounded[0, g][:, 0 : 2 * WIDE].rearrange("p (m e j) -> p m j e", e=2, j=PACK), columns[:, :, :, 0:2])
+            nc.scalar.copy(rounded[0, g][:, 2 * WIDE : 4 * WIDE].rearrange("p (e m j) -> p m j e", e=2, j=PACK), columns[:, :, :, 2:PACK])
+
         def quantise(src, t, g, cols):
             nc.vector.quantize_mx(out=codes[t, g][:, cols].bitcast(FP8X4), scales=scales[t, g][:, cols], in_=src)
 
@@ -117,18 +123,21 @@ def tile_picked_unet_none_p_kernel(
             )
 
         for g in range(PASSES):
-            round_w1(0, g, "scalar")
+            round_first(g)
             quantise_pair(0, g)
             quantise_planes(0, g)
         nc.vector.tensor_copy(xg[0][:], xw[0][:].bitcast(U32).indirect(offs_t[:]))
         skip_rows = skip.rearrange("(q t) v -> t q v", t=PACK)
         skip_t = {}
         skip_t[0] = tile([P, U], F32, "w1raw0")
+        nc.sync.dma_start(out=skip_t[0][:], in_=skip.rearrange("(q t) v -> q t v", t=PACK)[0:HP, 0:2, :])
+        skip_t[1] = tile([P, U], F32, "w1raw1")
         for e in range(2):
-            nc.sync.dma_start(out=skip_t[0][HP * e : HP * (e + 1), :], in_=skip_rows[e, 0:HP, :])
-        for t, name in ((2, "w1raw1"), (3, "xw0")):
-            skip_t[t] = tile([P, U], F32, name)
-            nc.sync.dma_start(out=skip_t[t][:], in_=skip_rows[t])
+            nc.sync.dma_start(out=skip_t[1][HP * e : HP * (e + 1), :], in_=skip_rows[e, HP:P, :])
+        skip_late = tile([P, 2, U], F32, "xw0")
+        nc.sync.dma_start(out=skip_late[:], in_=skip.rearrange("(q t) v -> q t v", t=PACK)[:, 2:PACK, :])
+        for t in (2, 3):
+            skip_t[t] = skip_late[:, t - 2, :]
 
         bank = {}
         first = [slice(0, P), slice(P, HALF), slice(HALF, S)]
@@ -141,9 +150,6 @@ def tile_picked_unet_none_p_kernel(
             if b == 0:
                 h_first = tile([P, P], F32, "hs2")
                 nc.scalar.copy(h_first[:], bank[0, 0][:])
-        skip_t[1] = tile([P, U], F32, "xw1")
-        for e in range(2):
-            nc.sync.dma_start(out=skip_t[1][HP * e : HP * (e + 1), :], in_=skip_rows[e, HP:P, :])
 
         for b in range(2):
             bank[1, b] = ps.tile([P, HALF], F32, name="b%d" % (3 + b))
@@ -160,7 +166,7 @@ def tile_picked_unet_none_p_kernel(
                 product(bank[t], t, g, whole)
         w2w = tile([P, 2 * N], U8, "xsg")
         nc.sync.dma_start(out=w2w[:].bitcast(I32), in_=w2_words[0].bitcast(I32))
-        w2s = tile([P, N], U8, "rounded10")
+        w2s = tile([P, N], U8, "wc11")
         nc.gpsimd.memset(w2s[:].bitcast(I32), 0)
         for q in range(4):
             nc.sync.dma_start(out=w2s[32 * q : 32 * q + 4, :].bitcast(I32), in_=w2_scales[0].bitcast(I32)[4 * q : 4 * q + 4, :])
@@ -198,38 +204,48 @@ def tile_picked_unet_none_p_kernel(
                 rows = tile([P, SIDE], BF16, "rows%d%d" % (a, s))
                 add_skip(nc.gpsimd, a, rows[:], SIDE * s, SIDE)
                 for e in range(2):
-                    nc.sync.dma_start(out=planes[s][HP * a : HP * (a + 1), e, :], in_=rows[HP * e : HP * (e + 1), :])
+                    nc.sync.dma_start(out=planes[s][HP * a : HP * (a + 1), e, :], in_=(rows[e:P:2, :], rows[HP * e : HP * (e + 1), :])[a])
         for d in range(4):
             s, c0 = divmod(CHUNK * d, SIDE)
             for t in (3, 2):
                 add_skip(nc.vector, t, planes[s][:, t, c0 : c0 + CHUNK], CHUNK * d, CHUNK)
 
-        chunks = [
-            (0, CHUNK, "scalar", "scalar"),
-            (CHUNK, CHUNK, "scalar", "scalar"),
-            (3 * CHUNK, CHUNK, "vector", "scalar"),
-            (2 * CHUNK, P, "scalar", "vector"),
-            (2 * CHUNK + P, P, "vector", "vector"),
-        ]
-        woven = []
-        for d, (v0, width, weaver, copier) in enumerate(chunks):
+        chunks = [(0, CHUNK), (CHUNK, CHUNK), (2 * CHUNK, P), (2 * CHUNK + P, P), (3 * CHUNK, CHUNK)]
+        woven = {}
+        accs = {}
+
+        def weave(d, engine):
+            v0, width = chunks[d]
             s, c0 = divmod(v0, SIDE)
-            woven.append(tile([P, width * PACK], BF16, "woven%d" % d))
-            copy_on[weaver](
+            woven[d] = tile([P, width * PACK], BF16, "woven%d" % d)
+            copy_on[engine](
                 woven[d][:].rearrange("p (c i t) -> p c t i", i=PACK, t=PACK),
                 planes[s][:, :, c0 : c0 + width].rearrange("p t (c i) -> p c t i", i=PACK),
             )
-        accs = []
-        for d, (v0, width, weaver, copier) in enumerate(chunks):
+
+        def multiply(d):
+            width = chunks[d][1]
             zc = tile([P, width], U32, "zc%d" % d)
             zs = tile([P, width], U8, "zs%d" % d)
             nc.vector.quantize_mx(out=zc[:].bitcast(FP8X4), scales=zs[:], in_=woven[d][:])
-            accs.append(ps.tile([P, width], F32, name="b%d" % d))
+            accs[d] = ps.tile([P, width], F32, name="b%d" % d)
             nc.tensor.matmul_mx(
                 out=accs[d][:], lhsT=w2w[:].bitcast(FP4X4), lhsT_scale=w2s[:],
                 rhs=zc[:].bitcast(FP8X4), rhs_scale=zs[:], start=True, stop=True,
             )
-        for d, (v0, width, weaver, copier) in enumerate(chunks):
+
+        def store(d, engine):
+            v0, width = chunks[d]
             res = tile([P, width], F32, "res%d" % d)
-            copy_on[copier](res[:], accs[d][:])
+            copy_on[engine](res[:], accs[d][:])
             nc.sync.dma_start(out=out[:, v0 : v0 + width], in_=res[:])
+
+        for d in (0, 1, 2):
+            weave(d, "scalar")
+        weave(3, "vector")
+        multiply(0)
+        weave(4, "vector")
+        for d in (1, 3, 4, 2):
+            multiply(d)
+        for d, engine in ((0, "scalar"), (1, "scalar"), (3, "vector"), (4, "scalar"), (2, "vector")):
+            store(d, engine)

@@ -161,7 +161,7 @@ def tile_picked_unet_none_p_kernel(
             for b in range(2):
                 product(bank[1, b], 1, g, halves[b])
             quantise_planes(1, g)
-        for t in (2, 3):
+        for t in (3, 2):
             for g in range(PASSES):
                 product(bank[t], t, g, whole)
         w2w = tile([P, 2 * N], U8, "xsg")
@@ -187,12 +187,12 @@ def tile_picked_unet_none_p_kernel(
             nc.vector.tensor_copy(h[:, halves[b]], bank[1, b][:])
         vector_scatter(1, whole, h[:])
         late = tile([P, 2 * S], F32, "late")
-        for i, t in enumerate((2, 3)):
-            nc.scalar.copy(late[:, S * i : S * (i + 1)], bank[t][:])
-        scalar_scatter(2, first[0], late[:, 0:P])
+        for t in (3, 2):
+            nc.scalar.copy(late[:, S * (t - 2) : S * (t - 1)], bank[t][:])
         scalar_scatter(3, first[0], late[:, S : S + P])
         vector_scatter(3, slice(P, S), late[:, S + P : 2 * S])
-        scalar_scatter(2, slice(P, S), late[:, P:S])
+        for b in range(2):
+            scalar_scatter(2, halves[b], late[:, halves[b]])
 
         planes = [tile([P, PACK, SIDE], BF16, "planes%d" % s) for s in range(2)]
 
@@ -205,12 +205,13 @@ def tile_picked_unet_none_p_kernel(
                 add_skip(nc.gpsimd, a, rows[:], SIDE * s, SIDE)
                 for e in range(2):
                     nc.sync.dma_start(out=planes[s][HP * a : HP * (a + 1), e, :], in_=(rows[e:P:2, :], rows[HP * e : HP * (e + 1), :])[a])
-        for d in range(4):
-            s, c0 = divmod(CHUNK * d, SIDE)
-            for t in (3, 2):
-                add_skip(nc.vector, t, planes[s][:, t, c0 : c0 + CHUNK], CHUNK * d, CHUNK)
+        add_skip(nc.vector, 3, planes[0][:, 3, :], 0, SIDE)
+        for d in range(2):
+            add_skip(nc.vector, 2, planes[0][:, 2, CHUNK * d : CHUNK * (d + 1)], CHUNK * d, CHUNK)
+        for t in (3, 2):
+            add_skip(nc.vector, t, planes[1][:, t, :], SIDE, SIDE)
 
-        chunks = [(0, CHUNK), (CHUNK, CHUNK), (2 * CHUNK, P), (2 * CHUNK + P, P), (3 * CHUNK, CHUNK)]
+        chunks = [(CHUNK * d, CHUNK) for d in range(4)]
         woven = {}
         accs = {}
 
@@ -240,12 +241,12 @@ def tile_picked_unet_none_p_kernel(
             copy_on[engine](res[:], accs[d][:])
             nc.sync.dma_start(out=out[:, v0 : v0 + width], in_=res[:])
 
-        for d in (0, 1, 2):
+        for d in (0, 1):
             weave(d, "scalar")
-        weave(3, "vector")
+        weave(2, "vector")
         multiply(0)
-        weave(4, "vector")
-        for d in (1, 3, 4, 2):
+        weave(3, "vector")
+        for d in (1, 2, 3):
             multiply(d)
-        for d, engine in ((0, "scalar"), (1, "scalar"), (3, "vector"), (4, "scalar"), (2, "vector")):
+        for d, engine in ((0, "scalar"), (1, "scalar"), (2, "scalar"), (3, "vector")):
             store(d, engine)

@@ -66,9 +66,9 @@ def tile_picked_unet_none_p_kernel(
         nc.sync.dma_start(out=xs[0:P:4, :].bitcast(I32), in_=x_scales.rearrange("g q n -> (g q) n").bitcast(I32))
         nc.sync.dma_start(offs_t[:], offs)
         load_w1(0, 1, tile([P, PACK * WIDE], F32, "w1raw1")[:])
-        nc.sync.dma_start(cell_t[:], cell)
         load_x(0, "xw0")
         load_x(1, "xw1")
+        nc.sync.dma_start(cell_t[:], cell)
 
         xsg = tile([P, S], U8, "xsg")
         nc.vector.tensor_copy(xsg[:], xs[:].indirect(offs_t[:]))
@@ -141,15 +141,12 @@ def tile_picked_unet_none_p_kernel(
 
         bank = {}
         first = [slice(0, P), slice(P, HALF), slice(HALF, S)]
-        for part in (first[0], slice(P, S)):
+        for part in first:
             nc.vector.tensor_copy(xg[1][:, part], xw[1][:].bitcast(U32).indirect(offs_t[:, entries(part)]))
         for b, part in enumerate(first):
-            bank[0, b] = ps.tile([P, part.stop - part.start], F32, name="b%d" % (b // 2))
+            bank[0, b] = ps.tile([P, part.stop - part.start], F32, name="b%d" % b)
             for g in range(PASSES):
                 product(bank[0, b], 0, g, part)
-            if b == 0:
-                h_first = tile([P, P], F32, "hs2")
-                nc.scalar.copy(h_first[:], bank[0, 0][:])
 
         for b in range(2):
             bank[1, b] = ps.tile([P, HALF], F32, name="b%d" % (3 + b))
@@ -177,11 +174,12 @@ def tile_picked_unet_none_p_kernel(
         def vector_scatter(t, part, h):
             nc.vector.tensor_copy(up[t][:].indirect(cell_t[:, entries(part)]), h)
 
-        scalar_scatter(0, first[0], h_first[:])
-        h = tile([P, S - P], F32, "hs0")
-        nc.scalar.copy(h[:, 0:P], bank[0, 1][:])
-        nc.scalar.copy(h[:, P : S - P], bank[0, 2][:])
-        scalar_scatter(0, slice(P, S), h[:])
+        h = tile([P, S], F32, "hs0")
+        for b in range(2):
+            nc.scalar.copy(h[:, first[b]], bank[0, b][:])
+        scalar_scatter(0, first[0], h[:, first[0]])
+        nc.scalar.copy(h[:, first[2]], bank[0, 2][:])
+        scalar_scatter(0, slice(P, S), h[:, P:S])
         h = tile([P, S], F32, "hv0")
         for b in range(2):
             nc.vector.tensor_copy(h[:, halves[b]], bank[1, b][:])
@@ -219,9 +217,10 @@ def tile_picked_unet_none_p_kernel(
             v0, width = chunks[d]
             s, c0 = divmod(v0, SIDE)
             woven[d] = tile([P, width * PACK], BF16, "woven%d" % d)
+            run = {"scalar": 1, "vector": PACK}[engine]
             copy_on[engine](
-                woven[d][:].rearrange("p (c i t) -> p c t i", i=PACK, t=PACK),
-                planes[s][:, :, c0 : c0 + width].rearrange("p t (c i) -> p c t i", i=PACK),
+                woven[d][:].rearrange("p (c i t) -> p c t i", i=run, t=PACK),
+                planes[s][:, :, c0 : c0 + width].rearrange("p t (c i) -> p c t i", i=run),
             )
 
         def multiply(d):
@@ -246,7 +245,7 @@ def tile_picked_unet_none_p_kernel(
         weave(2, "vector")
         multiply(0)
         weave(3, "vector")
-        for d in (1, 2, 3):
+        for d in (2, 3, 1):
             multiply(d)
-        for d, engine in ((0, "scalar"), (1, "scalar"), (2, "scalar"), (3, "vector")):
+        for d, engine in ((0, "scalar"), (2, "scalar"), (3, "scalar"), (1, "vector")):
             store(d, engine)

@@ -1,6 +1,7 @@
 from contextlib import ExitStack
 
 import concourse.mybir as mybir
+from concourse.masks import make_identity
 
 K, T, S, H, N, U = 1024, 2048, 512, 512, 128, 1024
 FLOPS = 2 * K * H * S + 2 * H * N * U
@@ -21,9 +22,9 @@ P = 128
 PACK = 4
 PASSES = K // (P * PACK)
 HALF = S // 2
-SIDE = U // 2
 CHUNK = U // 4
 WIDE = H // 2
+TURNED = U - CHUNK
 HP = P // 2
 
 
@@ -49,6 +50,9 @@ def tile_picked_unet_none_p_kernel(
         up = [tile([P, U], F32, "up%d" % t) for t in range(PACK)]
         for t in range(PACK):
             nc.gpsimd.memset(up[t][:], 0.0)
+
+        ident = tile([P, P], F32, "ident")
+        make_identity(nc, ident[:])
 
         w1_rows = w1.rearrange("(g p j) c -> g p j c", p=P, j=PACK)
         w1raw = {}
@@ -158,7 +162,7 @@ def tile_picked_unet_none_p_kernel(
             for b in range(2):
                 product(bank[1, b], 1, g, halves[b])
             quantise_planes(1, g)
-        for t in (3, 2):
+        for t in (2, 3):
             for g in range(PASSES):
                 product(bank[t], t, g, whole)
         w2w = tile([P, 2 * N], U8, "xsg")
@@ -185,67 +189,88 @@ def tile_picked_unet_none_p_kernel(
             nc.vector.tensor_copy(h[:, halves[b]], bank[1, b][:])
         vector_scatter(1, whole, h[:])
         late = tile([P, 2 * S], F32, "late")
-        for t in (3, 2):
+        for t in (2, 3):
             nc.scalar.copy(late[:, S * (t - 2) : S * (t - 1)], bank[t][:])
-        scalar_scatter(3, first[0], late[:, S : S + P])
-        vector_scatter(3, slice(P, S), late[:, S + P : 2 * S])
+        scalar_scatter(2, first[0], late[:, 0:P])
+        vector_scatter(2, slice(P, S), late[:, P:S])
         for b in range(2):
-            scalar_scatter(2, halves[b], late[:, halves[b]])
+            scalar_scatter(3, halves[b], late[:, S + HALF * b : S + HALF * (b + 1)])
 
-        planes = [tile([P, PACK, SIDE], BF16, "planes%d" % s) for s in range(2)]
+        spans = [slice(0, CHUNK), slice(CHUNK, TURNED)]
+        planes = [tile([P, PACK, span.stop - span.start], BF16, "planes%d" % s) for s, span in enumerate(spans)]
 
-        def add_skip(engine, t, dst, v0, width):
-            engine.tensor_tensor(dst, up[t][:, v0 : v0 + width], skip_t[t][:, v0 : v0 + width], ADD)
+        def add_skip(engine, t, dst, span):
+            engine.tensor_tensor(dst, up[t][:, span], skip_t[t][:, span], ADD)
 
         for a in range(2):
-            for s in range(2):
-                rows = tile([P, SIDE], BF16, "rows%d%d" % (a, s))
-                add_skip(nc.gpsimd, a, rows[:], SIDE * s, SIDE)
+            for s, span in enumerate(spans):
+                rows = tile([P, span.stop - span.start], BF16, "rows%d%d" % (a, s))
+                add_skip(nc.gpsimd, a, rows[:], span)
                 for e in range(2):
                     nc.sync.dma_start(out=planes[s][HP * a : HP * (a + 1), e, :], in_=(rows[e:P:2, :], rows[HP * e : HP * (e + 1), :])[a])
-        add_skip(nc.vector, 3, planes[0][:, 3, :], 0, SIDE)
-        for d in range(2):
-            add_skip(nc.vector, 2, planes[0][:, 2, CHUNK * d : CHUNK * (d + 1)], CHUNK * d, CHUNK)
-        for t in (3, 2):
-            add_skip(nc.vector, t, planes[1][:, t, :], SIDE, SIDE)
 
-        chunks = [(CHUNK * d, CHUNK) for d in range(4)]
-        woven = {}
-        accs = {}
+        def turn(dst, src, start, stop):
+            nc.tensor.matmul(dst, lhsT=src, rhs=ident[:], is_transpose=True, start=start, stop=stop)
+
+        def block(src, i):
+            return src[:, TURNED + P * i : TURNED + P * (i + 1)]
+
+        low = tile([P, 2, P], F32, "low")
+        for a in range(2):
+            sums = ps.tile([P, 2, P], F32, name="b%d" % (4 + a))
+            for i in range(2):
+                turn(sums[:, i, :], block(skip_t[a], i), i == 0, False)
+            for i in range(2):
+                turn(sums[:, i, :], block(up[a], i), False, i == 1)
+            dst = low[:, :, HP * a : HP * (a + 1)].bitcast(BF16)
+            if a == 0:
+                nc.scalar.copy(dst, sums[:])
+            else:
+                nc.vector.tensor_copy(dst.rearrange("p i (q e) -> p i q e", e=2), sums[:].rearrange("p i (e q) -> p i q e", e=2))
+        sums = ps.tile([P, 2, 2, P], F32, name="b1")
+        for src, opens in ((skip_t, True), (up, False)):
+            for e in range(2):
+                for i in range(2):
+                    turn(sums[:, i, e, :], block(src[2 + e], i), opens and i + e == 0, not opens and i + e == 2)
+        high = tile([P, 2, P], F32, "high")
+        nc.scalar.copy(high[:].bitcast(BF16).rearrange("p i (q e) -> p i q e", e=2), sums[:].rearrange("p i e q -> p i q e"))
+        back = ps.tile([P, 2, CHUNK], F32, name="b1")
+        for u, words in enumerate((low, high)):
+            for i in range(2):
+                turn(back[:, u, P * i : P * (i + 1)], words[:, i, :], True, True)
+
+        for t in (2, 3):
+            for s, span in enumerate(spans):
+                add_skip(nc.vector, t, planes[s][:, t, :], span)
+
+        woven = [tile([P, CHUNK * PACK], BF16, "woven%d" % d) for d in range(3)]
 
         def weave(d, engine):
-            v0, width = chunks[d]
-            s, c0 = divmod(v0, SIDE)
-            woven[d] = tile([P, width * PACK], BF16, "woven%d" % d)
+            s = min(d, 1)
+            c0 = CHUNK * d - spans[s].start
             run = {"scalar": 1, "vector": PACK}[engine]
             copy_on[engine](
                 woven[d][:].rearrange("p (c i t) -> p c t i", i=run, t=PACK),
-                planes[s][:, :, c0 : c0 + width].rearrange("p t (c i) -> p c t i", i=run),
+                planes[s][:, :, c0 : c0 + CHUNK].rearrange("p t (c i) -> p c t i", i=run),
             )
 
-        def multiply(d):
-            width = chunks[d][1]
-            zc = tile([P, width], U32, "zc%d" % d)
-            zs = tile([P, width], U8, "zs%d" % d)
+        weave(0, "scalar")
+        woven.append(tile([P, CHUNK * PACK], BF16, "planes0"))
+        nc.scalar.copy(woven[3][:].bitcast(F32).rearrange("p (v u) -> p v u", u=2), back[:].rearrange("p u v -> p v u"))
+        for d in (1, 2):
+            weave(d, "vector")
+
+        accs = {}
+        for d in (1, 0, 2, 3):
+            zc = tile([P, CHUNK], U32, "zc%d" % d)
+            zs = tile([P, CHUNK], U8, ("planes1", "zs1", "zs2", "woven1")[d])
             nc.vector.quantize_mx(out=zc[:].bitcast(FP8X4), scales=zs[:], in_=woven[d][:])
-            accs[d] = ps.tile([P, width], F32, name="b%d" % d)
+            accs[d] = ps.tile([P, CHUNK], F32, name="b%d" % (5, 6, 4, 3)[d])
             nc.tensor.matmul_mx(
                 out=accs[d][:], lhsT=w2w[:].bitcast(FP4X4), lhsT_scale=w2s[:],
                 rhs=zc[:].bitcast(FP8X4), rhs_scale=zs[:], start=True, stop=True,
             )
-
-        def store(d, engine):
-            v0, width = chunks[d]
-            res = tile([P, width], F32, "res%d" % d)
+        for d, engine in ((1, "scalar"), (0, "scalar"), (2, "scalar"), (3, "vector")):
+            res = tile([P, CHUNK], F32, "res%d" % d)
             copy_on[engine](res[:], accs[d][:])
-            nc.sync.dma_start(out=out[:, v0 : v0 + width], in_=res[:])
-
-        for d in (0, 1):
-            weave(d, "scalar")
-        weave(2, "vector")
-        multiply(0)
-        weave(3, "vector")
-        for d in (2, 3, 1):
-            multiply(d)
-        for d, engine in ((0, "scalar"), (2, "scalar"), (3, "scalar"), (1, "vector")):
-            store(d, engine)
+            nc.sync.dma_start(out=out[:, CHUNK * d : CHUNK * (d + 1)], in_=res[:])

@@ -203,11 +203,16 @@ def tile_picked_unet_none_p_kernel(
             engine.tensor_tensor(dst, up[t][:, span], skip_t[t][:, span], ADD)
 
         for a in range(2):
-            for s, span in enumerate(spans):
-                rows = tile([P, span.stop - span.start], BF16, "rows%d%d" % (a, s))
-                add_skip(nc.gpsimd, a, rows[:], span)
+            for s in (1, 0):
+                rows = tile([P, spans[s].stop - spans[s].start], BF16, "rows%d%d" % (a, s))
+                add_skip(nc.gpsimd, a, rows[:], spans[s])
                 for e in range(2):
-                    nc.sync.dma_start(out=planes[s][HP * a : HP * (a + 1), e, :], in_=(rows[e:P:2, :], rows[HP * e : HP * (e + 1), :])[a])
+                    dst = planes[s][HP * a : HP * (a + 1), e, :]
+                    src = (rows[e:P:2, :], rows[HP * e : HP * (e + 1), :])[a]
+                    if a == 1 and s == 0:
+                        nc.scalar.copy(dst.bitcast(F32), src.bitcast(F32))
+                    else:
+                        nc.sync.dma_start(out=dst, in_=src)
 
         def turn(dst, src, start, stop):
             nc.tensor.matmul(dst, lhsT=src, rhs=ident[:], is_transpose=True, start=start, stop=stop)

@@ -187,14 +187,17 @@ def tile_picked_unet_none_p_kernel(
         h = tile([P, S], F32, "hv0")
         for b in range(2):
             nc.vector.tensor_copy(h[:, halves[b]], bank[1, b][:])
-        vector_scatter(1, whole, h[:])
-        late = tile([P, 2 * S], F32, "late")
-        for t in (2, 3):
-            nc.scalar.copy(late[:, S * (t - 2) : S * (t - 1)], bank[t][:])
+        late = tile([P, P + S], F32, "late")
+        nc.scalar.copy(late[:, 0:P], bank[2][:, 0:P])
+        nc.scalar.copy(late[:, P : P + S], bank[3][:])
+        vector_scatter(1, halves[0], h[:, halves[0]])
+        rest = tile([P, S - P], F32, "rest")
+        nc.vector.tensor_copy(rest[:], bank[2][:, P:S])
+        vector_scatter(1, halves[1], h[:, halves[1]])
         scalar_scatter(2, first[0], late[:, 0:P])
-        vector_scatter(2, slice(P, S), late[:, P:S])
+        vector_scatter(2, slice(P, S), rest[:])
         for b in range(2):
-            scalar_scatter(3, halves[b], late[:, S + HALF * b : S + HALF * (b + 1)])
+            scalar_scatter(3, halves[b], late[:, P + HALF * b : P + HALF * (b + 1)])
 
         spans = [slice(0, CHUNK), slice(CHUNK, TURNED)]
         planes = [tile([P, PACK, span.stop - span.start], BF16, "planes%d" % s) for s, span in enumerate(spans)]

@@ -235,21 +235,25 @@ def tile_picked_unet_none_p_kernel(
                 nc.scalar.copy(dst, sums[:])
             else:
                 nc.vector.tensor_copy(dst.rearrange("p i (q e) -> p i q e", e=2), sums[:].rearrange("p i (e q) -> p i q e", e=2))
-        sums = ps.tile([P, 2, 2, P], F32, name="b1")
+        sums = [ps.tile([P, 2, P], F32, name="b%d" % (1 + i)) for i in range(2)]
         for src, opens in ((skip_t, True), (up, False)):
             for e in range(2):
                 for i in range(2):
-                    turn(sums[:, i, e, :], block(src[2 + e], i), opens and i + e == 0, not opens and i + e == 2)
-        high = tile([P, 2, P], F32, "high")
-        nc.scalar.copy(high[:].bitcast(BF16).rearrange("p i (q e) -> p i q e", e=2), sums[:].rearrange("p i e q -> p i q e"))
-        back = ps.tile([P, 2, CHUNK], F32, name="b1")
-        for u, words in enumerate((low, high)):
-            for i in range(2):
-                turn(back[:, u, P * i : P * (i + 1)], words[:, i, :], True, True)
+                    turn(sums[i][:, e, :], block(src[2 + e], i), opens and e == 0, not opens and e == 1)
+        back = []
+        for i in range(2):
+            high = tile([P, P], F32, "high%d" % i)
+            nc.scalar.copy(high[:].bitcast(BF16).rearrange("p (q e) -> p q e", e=2), sums[i][:].rearrange("p e q -> p q e"))
+            back.append(ps.tile([P, 2, P], F32, name="b%d" % (1 + i)))
+            for u, words in enumerate((low[:, i, :], high[:])):
+                turn(back[i][:, u, :], words, True, True)
 
-        for t in (2, 3):
-            for s, span in enumerate(spans):
-                add_skip(nc.vector, t, planes[s][:, t, :], span)
+        for s, span in enumerate(spans):
+            add_skip(nc.vector, 2, planes[s][:, 2, :], span)
+        for d in range(3):
+            s = min(d, 1)
+            c0 = CHUNK * d - spans[s].start
+            add_skip(nc.vector, 3, planes[s][:, 3, c0 : c0 + CHUNK], slice(CHUNK * d, CHUNK * (d + 1)))
 
         woven = [tile([P, CHUNK * PACK], BF16, "woven%d" % d) for d in range(3)]
 
@@ -264,7 +268,9 @@ def tile_picked_unet_none_p_kernel(
 
         weave(0, "scalar")
         woven.append(tile([P, CHUNK * PACK], BF16, "planes0"))
-        nc.scalar.copy(woven[3][:].bitcast(F32).rearrange("p (v u) -> p v u", u=2), back[:].rearrange("p u v -> p v u"))
+        for i in range(2):
+            words = woven[3][:, P * PACK * i : P * PACK * (i + 1)].bitcast(F32)
+            nc.scalar.copy(words.rearrange("p (v u) -> p v u", u=2), back[i][:].rearrange("p u v -> p v u"))
         for d in (1, 2):
             weave(d, "vector")
 

@@ -22,10 +22,12 @@ P = 128
 PACK = 4
 PASSES = K // (P * PACK)
 HALF = S // 2
+SIDE = U // 2
 CHUNK = U // 4
-WIDE = H // 2
-TURNED = U - CHUNK
 HP = P // 2
+TURNED = U - CHUNK
+ROW = PACK * T
+SHARE = 96
 
 
 def tile_picked_unet_none_p_kernel(
@@ -34,140 +36,117 @@ def tile_picked_unet_none_p_kernel(
     nc = tc.nc
     with ExitStack() as ctx:
         sb = ctx.enter_context(tc.tile_pool(name="sb", bufs=1))
+        shared = ctx.enter_context(tc.tile_pool(name="shared", bufs=1))
         ps = ctx.enter_context(tc.psum_pool(name="ps", bufs=1))
 
         def tile(shape, dtype, name):
             return sb.tile(shape, dtype, name=name, align_bytes=64)
 
+        def placed(shape, dtype, name, offset):
+            return shared.tile(shape, dtype, name=name, align_bytes=64, offset=offset)
+
         copy_on = {"scalar": nc.scalar.copy, "vector": nc.vector.tensor_copy}
 
         offs_t = sb.tile([P, S // 16], U16, name="offs_t")
         cell_t = sb.tile([P, S // 16], U16, name="cell_t")
-        xs = tile([P, T], U8, "xs")
+        xs = placed([P, T], U8, "xs", ROW - T // 2)
         xsm = tile([P, PASSES * S], U8, "xsm")
-        nc.gpsimd.memset(xs[:].bitcast(I32), 0)
+        nc.gpsimd.memset(xs[32:HP, :].bitcast(I32), 0)
+        nc.gpsimd.memset(xs[HP:P, :].bitcast(I32), 0)
         nc.gpsimd.memset(xsm[:].bitcast(I32), 0)
         up = [tile([P, U], F32, "up%d" % t) for t in range(PACK)]
-        for t in range(PACK):
+        for t in range(2):
             nc.gpsimd.memset(up[t][:], 0.0)
-
+        for t in (2, 3):
+            nc.scalar.copy(up[t][:], up[0][:])
         ident = tile([P, P], F32, "ident")
         make_identity(nc, ident[:])
 
+        nc.sync.dma_start(out=xs[0:32, :].bitcast(I32), in_=x_scales.rearrange("g q n -> q g n").bitcast(I32))
+        nc.sync.dma_start(offs_t[:], offs)
         w1_rows = w1.rearrange("(g p j) c -> g p j c", p=P, j=PACK)
-        w1raw = {}
+        w1raw = [tile([P, PACK, H], F32, "w1raw0")]
+        xw = []
 
-        def load_w1(a, g, dst):
-            w1raw[a, g] = dst.rearrange("p (j c) -> p j c", j=PACK)
-            nc.sync.dma_start(out=w1raw[a, g], in_=w1_rows[g, :, :, WIDE * a : WIDE * (a + 1)])
-
-        def load_x(g, name):
-            xw.append(tile([P, T], I32, name))
+        def load_x(g, dst):
+            xw.append(dst)
             nc.sync.dma_start(out=xw[g][:], in_=x_words[g].rearrange("p n t -> p (n t)").bitcast(I32))
 
-        xw = []
-        load_w1(0, 0, tile([P, PACK * WIDE], F32, "w1raw0")[:])
-        nc.sync.dma_start(out=xs[0:P:4, :].bitcast(I32), in_=x_scales.rearrange("g q n -> (g q) n").bitcast(I32))
-        nc.sync.dma_start(offs_t[:], offs)
-        load_w1(0, 1, tile([P, PACK * WIDE], F32, "w1raw1")[:])
-        load_x(0, "xw0")
-        load_x(1, "xw1")
+        nc.sync.dma_start(out=w1raw[0][:], in_=w1_rows[0])
+        load_x(0, tile([P, T], I32, "xw0"))
         nc.sync.dma_start(cell_t[:], cell)
-
         xsg = tile([P, S], U8, "xsg")
         nc.vector.tensor_copy(xsg[:], xs[:].indirect(offs_t[:]))
-        xsp = tile([P, PASSES * S], U8, "xsp")
-        for g in range(PASSES):
-            nc.vector.tensor_copy(xsp[0:HP, S * g : S * (g + 1)].bitcast(I32), xsg[HP * g : HP * (g + 1), :].bitcast(I32))
-        for r in range(4):
-            nc.sync.dma_start(out=xsm[r:P:32, :].bitcast(I32), in_=xsp[4 * r : HP : 16, :].bitcast(I32))
-        second = tile([P, PASSES * PACK * WIDE], F32, "xsg")
-        for g in range(PASSES):
-            load_w1(1, g, second[:, PACK * WIDE * g : PACK * WIDE * (g + 1)])
-
-        rounded = {}
-        codes = {(t, g): tile([P, P], U32, "wc%d%d" % (t, g)) for t in range(PACK) for g in range(PASSES)}
-        scales = {(t, g): tile([P, P], U8, "ws%d%d" % (t, g)) for t in range(PACK) for g in range(PASSES)}
-
-        def round_w1(a, g, engine):
-            rounded[a, g] = tile([P, PACK * WIDE], BF16, "rounded%d%d" % (a, g))
-            copy_on[engine](
-                rounded[a, g][:].rearrange("p (t m j) -> p m j t", t=PACK, j=PACK),
-                w1raw[a, g].rearrange("p j (m t) -> p m j t", t=PACK),
-            )
-
-        def round_first(g):
-            rounded[0, g] = tile([P, PACK * WIDE], BF16, "rounded0%d" % g)
-            columns = w1raw[0, g].rearrange("p j (m t) -> p m j t", t=PACK)
-            nc.scalar.copy(rounded[0, g][:, 0 : 2 * WIDE].rearrange("p (m e j) -> p m j e", e=2, j=PACK), columns[:, :, :, 0:2])
-            nc.scalar.copy(rounded[0, g][:, 2 * WIDE : 4 * WIDE].rearrange("p (e m j) -> p m j e", e=2, j=PACK), columns[:, :, :, 2:PACK])
-
-        def quantise(src, t, g, cols):
-            nc.vector.quantize_mx(out=codes[t, g][:, cols].bitcast(FP8X4), scales=scales[t, g][:, cols], in_=src)
-
-        def quantise_pair(a, g):
-            quantise(rounded[a, g][:, 0 : 2 * WIDE], a, g, slice(0, P))
-
-        def quantise_planes(a, g):
-            for t in (2, 3):
-                quantise(rounded[a, g][:, WIDE * t : WIDE * (t + 1)], t, g, slice(HP * a, HP * (a + 1)))
+        for q in range(4):
+            rows = xsm[32 * q : 32 * q + 4, :].bitcast(I32).rearrange("r (g n) -> r g n", g=PASSES)
+            nc.sync.dma_start(out=rows, in_=xsg[8 * q : 8 * q + 8, :].bitcast(I32))
+        w1raw.append(placed([P, PACK, H], F32, "w1raw1", 0))
+        nc.sync.dma_start(out=w1raw[1][:], in_=w1_rows[1])
+        load_x(1, placed([P, T], I32, "xw1", ROW))
 
         xg = [tile([P, S], U32, "xg%d" % g) for g in range(PASSES)]
+        codes, scales = [], []
+        for g in range(PASSES):
+            rounded = tile([P, PACK * H], BF16, "rounded%d" % g)
+            dst = rounded[:].rearrange("p (t m j) -> p m j t", t=PACK, j=PACK)
+            src = w1raw[g][:].rearrange("p j (m t) -> p m j t", t=PACK)
+            if g == 0:
+                nc.vector.tensor_copy(dst, src)
+            else:
+                nc.vector.tensor_copy(xg[0][:], xw[0][:].bitcast(U32).indirect(offs_t[:]))
+                nc.vector.tensor_copy(dst[:, 0:SHARE], src[:, 0:SHARE])
+                nc.scalar.copy(dst[:, SHARE:P], src[:, SHARE:P])
+            codes.append(tile([P, H], U32, "wc%d" % g))
+            scales.append(tile([P, H], U8, "ws%d" % g))
+            nc.vector.quantize_mx(out=codes[g][:].bitcast(FP8X4), scales=scales[g][:], in_=rounded[:])
+
+        skip_rows = skip.rearrange("(q t) v -> q t v", t=PACK)
+        skip_t = []
+        for u in range(2):
+            both = tile([P, 2, U], F32, ("w1raw0", "xw0")[u])
+            nc.sync.dma_start(out=both[:], in_=skip_rows[:, 2 * u : 2 * u + 2, :])
+            skip_t.extend([both[:, 0, :], both[:, 1, :]])
+
         whole = slice(0, S)
         halves = [slice(0, HALF), slice(HALF, S)]
+        first = [slice(0, P), slice(P, HALF), slice(HALF, S)]
 
         def entries(part):
             return slice(part.start // 16, part.stop // 16)
 
-        def product(bank, t, g, part):
+        def product(dst, t, g, part, start, stop):
+            cols = slice(P * t, P * (t + 1))
             nc.tensor.matmul_mx(
-                out=bank[:], lhsT=codes[t, g][:].bitcast(FP8X4), lhsT_scale=scales[t, g][:],
+                out=dst, lhsT=codes[g][:, cols].bitcast(FP8X4), lhsT_scale=scales[g][:, cols],
                 rhs=xg[g][:, part].bitcast(FP8X4), rhs_scale=xsm[:, S * g + part.start : S * g + part.stop],
-                start=(g == 0), stop=(g == PASSES - 1),
+                start=start, stop=stop,
             )
 
-        for g in range(PASSES):
-            round_first(g)
-            quantise_pair(0, g)
-            quantise_planes(0, g)
-        nc.vector.tensor_copy(xg[0][:], xw[0][:].bitcast(U32).indirect(offs_t[:]))
-        skip_rows = skip.rearrange("(q t) v -> t q v", t=PACK)
-        skip_t = {}
-        skip_t[0] = tile([P, U], F32, "w1raw0")
-        nc.sync.dma_start(out=skip_t[0][:], in_=skip.rearrange("(q t) v -> q t v", t=PACK)[0:HP, 0:2, :])
-        skip_t[1] = tile([P, U], F32, "w1raw1")
-        for e in range(2):
-            nc.sync.dma_start(out=skip_t[1][HP * e : HP * (e + 1), :], in_=skip_rows[e, HP:P, :])
-        skip_late = tile([P, 2, U], F32, "xw0")
-        nc.sync.dma_start(out=skip_late[:], in_=skip.rearrange("(q t) v -> q t v", t=PACK)[:, 2:PACK, :])
-        for t in (2, 3):
-            skip_t[t] = skip_late[:, t - 2, :]
+        head = ps.tile([P, P], F32, name="b0")
+        body = ps.tile([P, S - P], F32, name="b1")
+        one = [ps.tile([P, HALF], F32, name="b%d" % (2 + b)) for b in range(2)]
+        late = {t: ps.tile([P, S], F32, name="b%d" % (2 + t)) for t in (2, 3)}
 
-        bank = {}
-        first = [slice(0, P), slice(P, HALF), slice(HALF, S)]
+        product(head[:], 0, 0, first[0], True, False)
+        product(one[0][:], 1, 0, halves[0], True, False)
+        product(body[:, 0:P], 0, 0, first[1], True, False)
+        product(body[:, P : S - P], 0, 0, first[2], False, False)
+        product(one[1][:], 1, 0, halves[1], True, False)
+        for t in (3, 2):
+            product(late[t][:], t, 0, whole, True, False)
         for part in first:
             nc.vector.tensor_copy(xg[1][:, part], xw[1][:].bitcast(U32).indirect(offs_t[:, entries(part)]))
-        for b, part in enumerate(first):
-            bank[0, b] = ps.tile([P, part.stop - part.start], F32, name="b%d" % b)
-            for g in range(PASSES):
-                product(bank[0, b], 0, g, part)
+        product(head[:], 0, 1, first[0], False, True)
+        product(one[0][:], 1, 1, halves[0], False, True)
+        product(body[:, 0:P], 0, 1, first[1], False, False)
+        product(body[:, P : S - P], 0, 1, first[2], False, True)
+        product(one[1][:], 1, 1, halves[1], False, True)
+        for t in (3, 2):
+            product(late[t][:], t, 1, whole, False, True)
 
-        for b in range(2):
-            bank[1, b] = ps.tile([P, HALF], F32, name="b%d" % (3 + b))
-        for t in (2, 3):
-            bank[t] = ps.tile([P, S], F32, name="b%d" % (3 + t))
-        for g in range(PASSES):
-            round_w1(1, g, "vector")
-            quantise_pair(1, g)
-            for b in range(2):
-                product(bank[1, b], 1, g, halves[b])
-            quantise_planes(1, g)
-        for t in (2, 3):
-            for g in range(PASSES):
-                product(bank[t], t, g, whole)
-        w2w = tile([P, 2 * N], U8, "xsg")
+        w2w = tile([P, 2 * N], U8, "rounded1")
         nc.sync.dma_start(out=w2w[:].bitcast(I32), in_=w2_words[0].bitcast(I32))
-        w2s = tile([P, N], U8, "wc11")
+        w2s = tile([P, N], U8, "wc1")
         nc.gpsimd.memset(w2s[:].bitcast(I32), 0)
         for q in range(4):
             nc.sync.dma_start(out=w2s[32 * q : 32 * q + 4, :].bitcast(I32), in_=w2_scales[0].bitcast(I32)[4 * q : 4 * q + 4, :])
@@ -178,113 +157,84 @@ def tile_picked_unet_none_p_kernel(
         def vector_scatter(t, part, h):
             nc.vector.tensor_copy(up[t][:].indirect(cell_t[:, entries(part)]), h)
 
-        h = tile([P, S], F32, "hs0")
+        h0 = tile([P, S], F32, "h0")
+        nc.scalar.copy(h0[:, 0:P], head[:])
+        scalar_scatter(0, first[0], h0[:, 0:P])
+        h3 = [tile([P, HALF], F32, "h3%d" % b) for b in range(2)]
+        nc.scalar.copy(h0[:, P:S], body[:])
+        nc.scalar.copy(h3[0][:], late[3][:, halves[0]])
+        scalar_scatter(0, slice(P, S), h0[:, P:S])
+        h1 = tile([P, S], F32, "h1")
         for b in range(2):
-            nc.scalar.copy(h[:, first[b]], bank[0, b][:])
-        scalar_scatter(0, first[0], h[:, first[0]])
-        nc.scalar.copy(h[:, first[2]], bank[0, 2][:])
-        scalar_scatter(0, slice(P, S), h[:, P:S])
-        h = tile([P, S], F32, "hv0")
-        for b in range(2):
-            nc.vector.tensor_copy(h[:, halves[b]], bank[1, b][:])
-        late = tile([P, P + S], F32, "late")
-        nc.scalar.copy(late[:, 0:P], bank[2][:, 0:P])
-        nc.scalar.copy(late[:, P : P + S], bank[3][:])
-        vector_scatter(1, halves[0], h[:, halves[0]])
-        rest = tile([P, S - P], F32, "rest")
-        nc.vector.tensor_copy(rest[:], bank[2][:, P:S])
-        vector_scatter(1, halves[1], h[:, halves[1]])
-        scalar_scatter(2, first[0], late[:, 0:P])
-        vector_scatter(2, slice(P, S), rest[:])
-        for b in range(2):
-            scalar_scatter(3, halves[b], late[:, P + HALF * b : P + HALF * (b + 1)])
-
-        spans = [slice(0, CHUNK), slice(CHUNK, TURNED)]
-        planes = [tile([P, PACK, span.stop - span.start], BF16, "planes%d" % s) for s, span in enumerate(spans)]
-
-        def add_skip(engine, t, dst, span):
-            engine.tensor_tensor(dst, up[t][:, span], skip_t[t][:, span], ADD)
-
-        for a in range(2):
-            for s in (1, 0):
-                rows = tile([P, spans[s].stop - spans[s].start], BF16, "rows%d%d" % (a, s))
-                add_skip(nc.gpsimd, a, rows[:], spans[s])
-                for e in range(2):
-                    dst = planes[s][HP * a : HP * (a + 1), e, :]
-                    src = (rows[e:P:2, :], rows[HP * e : HP * (e + 1), :])[a]
-                    if a == 1 and s == 0:
-                        nc.scalar.copy(dst.bitcast(F32), src.bitcast(F32))
-                    else:
-                        nc.sync.dma_start(out=dst, in_=src)
-
+            nc.vector.tensor_copy(h1[:, halves[b]], one[b][:])
+        h2 = tile([P, S], F32, "h2")
+        nc.vector.tensor_copy(h2[:], late[2][:])
+        vector_scatter(1, whole, h1[:])
         def turn(dst, src, start, stop):
             nc.tensor.matmul(dst, lhsT=src, rhs=ident[:], is_transpose=True, start=start, stop=stop)
 
-        def block(src, i):
-            return src[:, TURNED + P * i : TURNED + P * (i + 1)]
+        def turned_sums(u, name):
+            sums = ps.tile([P, 2, 2, P], F32, name=name)
+            for src, opens in ((skip_t, True), (up, False)):
+                for e in range(2):
+                    for i in range(2):
+                        block = src[2 * u + e][:, TURNED + P * i : TURNED + P * (i + 1)]
+                        turn(sums[:, i, e, :], block, opens and e + i == 0, not opens and e + i == 2)
+            words = tile([P, 2, P], F32, "turned%d" % u)
+            nc.scalar.copy(words[:].bitcast(BF16).rearrange("p i (q e) -> p i q e", e=2), sums[:].rearrange("p i e q -> p i q e"))
+            return words
 
-        low = tile([P, 2, P], F32, "low")
-        for a in range(2):
-            sums = ps.tile([P, 2, P], F32, name="b%d" % (4 + a))
-            for i in range(2):
-                turn(sums[:, i, :], block(skip_t[a], i), i == 0, False)
-            for i in range(2):
-                turn(sums[:, i, :], block(up[a], i), False, i == 1)
-            dst = low[:, :, HP * a : HP * (a + 1)].bitcast(BF16)
-            if a == 0:
-                nc.scalar.copy(dst, sums[:])
-            else:
-                nc.vector.tensor_copy(dst.rearrange("p i (q e) -> p i q e", e=2), sums[:].rearrange("p i (e q) -> p i q e", e=2))
-        sums = [ps.tile([P, 2, P], F32, name="b%d" % (1 + i)) for i in range(2)]
-        for src, opens in ((skip_t, True), (up, False)):
-            for e in range(2):
-                for i in range(2):
-                    turn(sums[i][:, e, :], block(src[2 + e], i), opens and e == 0, not opens and e == 1)
-        back = []
+        scalar_scatter(3, halves[0], h3[0][:])
+        nc.scalar.copy(h3[1][:], late[3][:, halves[1]])
+        turned = [turned_sums(0, "b6")]
+        scalar_scatter(3, halves[1], h3[1][:])
+        vector_scatter(2, whole, h2[:])
+        turned.append(turned_sums(1, "b7"))
+        back = ps.tile([P, 2, 2, P], F32, name="b7")
         for i in range(2):
-            high = tile([P, P], F32, "high%d" % i)
-            nc.scalar.copy(high[:].bitcast(BF16).rearrange("p (q e) -> p q e", e=2), sums[i][:].rearrange("p e q -> p q e"))
-            back.append(ps.tile([P, 2, P], F32, name="b%d" % (1 + i)))
-            for u, words in enumerate((low[:, i, :], high[:])):
-                turn(back[i][:, u, :], words, True, True)
+            for u in range(2):
+                turn(back[:, i, u, :], turned[u][:, i, :], True, True)
 
-        for s, span in enumerate(spans):
-            add_skip(nc.vector, 2, planes[s][:, 2, :], span)
-        for d in range(3):
-            s = min(d, 1)
-            c0 = CHUNK * d - spans[s].start
-            add_skip(nc.vector, 3, planes[s][:, 3, c0 : c0 + CHUNK], slice(CHUNK * d, CHUNK * (d + 1)))
+        spans = [slice(0, SIDE), slice(SIDE, TURNED)]
+        pairs = [tile([P, 2, span.stop - span.start, 2], BF16, "pairs%d" % s) for s, span in enumerate(spans)]
 
-        woven = [tile([P, CHUNK * PACK], BF16, "woven%d" % d) for d in range(3)]
+        def add_skip(engine, t, s):
+            engine.tensor_tensor(pairs[s][:, t // 2, :, t % 2], up[t][:, spans[s]], skip_t[t][:, spans[s]], ADD)
+
+        for t in range(2):
+            for s in range(2):
+                add_skip(nc.gpsimd, t, s)
+        for s in range(2):
+            for t in (2, 3):
+                add_skip(nc.vector, t, s)
+
+        woven = {}
 
         def weave(d, engine):
-            s = min(d, 1)
-            c0 = CHUNK * d - spans[s].start
-            run = {"scalar": 1, "vector": PACK}[engine]
+            woven[d] = tile([P, CHUNK * PACK], BF16, "woven%d" % d)
+            words = pairs[d // 2][:].rearrange("p u v e -> p u (v e)").bitcast(F32)
             copy_on[engine](
-                woven[d][:].rearrange("p (c i t) -> p c t i", i=run, t=PACK),
-                planes[s][:, :, c0 : c0 + CHUNK].rearrange("p t (c i) -> p c t i", i=run),
+                woven[d][:].bitcast(F32).rearrange("p (v u) -> p v u", u=2),
+                words[:, :, CHUNK * (d % 2) : CHUNK * (d % 2 + 1)].rearrange("p u v -> p v u"),
             )
 
         weave(0, "scalar")
-        woven.append(tile([P, CHUNK * PACK], BF16, "planes0"))
-        for i in range(2):
-            words = woven[3][:, P * PACK * i : P * PACK * (i + 1)].bitcast(F32)
-            nc.scalar.copy(words.rearrange("p (v u) -> p v u", u=2), back[i][:].rearrange("p u v -> p v u"))
-        for d in (1, 2):
-            weave(d, "vector")
+        woven[3] = tile([P, CHUNK * PACK], BF16, "woven3")
+        nc.scalar.copy(woven[3][:].bitcast(F32).rearrange("p (i v u) -> p i v u", i=2, u=2), back[:].rearrange("p i u v -> p i v u"))
+        weave(1, "scalar")
+        weave(2, "vector")
 
         accs = {}
-        for d in (1, 0, 2, 3):
+        for d in (3, 2, 0, 1):
             zc = tile([P, CHUNK], U32, "zc%d" % d)
-            zs = tile([P, CHUNK], U8, ("planes1", "zs1", "zs2", "woven1")[d])
+            zs = tile([P, CHUNK], U8, ("zs0", "zs1", "zs2", "pairs1")[d])
             nc.vector.quantize_mx(out=zc[:].bitcast(FP8X4), scales=zs[:], in_=woven[d][:])
-            accs[d] = ps.tile([P, CHUNK], F32, name="b%d" % (5, 6, 4, 3)[d])
+            accs[d] = ps.tile([P, CHUNK], F32, name="b%d" % d)
             nc.tensor.matmul_mx(
                 out=accs[d][:], lhsT=w2w[:].bitcast(FP4X4), lhsT_scale=w2s[:],
                 rhs=zc[:].bitcast(FP8X4), rhs_scale=zs[:], start=True, stop=True,
             )
-        for d, engine in ((1, "scalar"), (0, "scalar"), (2, "scalar"), (3, "vector")):
-            res = tile([P, CHUNK], F32, "res%d" % d)
+        for d, engine in ((3, "scalar"), (2, "scalar"), (0, "scalar"), (1, "vector")):
+            res = tile([P, CHUNK], F32, ("res0", "res1", "res2", "pairs0")[d])
             copy_on[engine](res[:], accs[d][:])
             nc.sync.dma_start(out=out[:, CHUNK * d : CHUNK * (d + 1)], in_=res[:])

@@ -22,7 +22,6 @@ P = 128
 PACK = 4
 PASSES = K // (P * PACK)
 HALF = S // 2
-SIDE = U // 2
 CHUNK = U // 4
 HP = P // 2
 TURNED = U - CHUNK
@@ -124,25 +123,26 @@ def tile_picked_unet_none_p_kernel(
 
         head = ps.tile([P, P], F32, name="b0")
         body = ps.tile([P, S - P], F32, name="b1")
-        one = [ps.tile([P, HALF], F32, name="b%d" % (2 + b)) for b in range(2)]
-        late = {t: ps.tile([P, S], F32, name="b%d" % (2 + t)) for t in (2, 3)}
-
-        product(head[:], 0, 0, first[0], True, False)
-        product(one[0][:], 1, 0, halves[0], True, False)
-        product(body[:, 0:P], 0, 0, first[1], True, False)
-        product(body[:, P : S - P], 0, 0, first[2], False, False)
-        product(one[1][:], 1, 0, halves[1], True, False)
-        for t in (3, 2):
-            product(late[t][:], t, 0, whole, True, False)
+        opening = ps.tile([P, HALF], F32, name="b2")
+        middle = ps.tile([P, S], F32, name="b3")
+        closing = ps.tile([P, HALF], F32, name="b4")
+        last = ps.tile([P, S], F32, name="b5")
+        pieces = [
+            (head[:], 0, first[0], True, True),
+            (opening[:], 1, halves[0], True, True),
+            (body[:, 0:P], 0, first[1], True, False),
+            (body[:, P : S - P], 0, first[2], False, True),
+            (last[:], 3, whole, True, True),
+            (middle[:, halves[0]], 1, halves[1], True, False),
+            (middle[:, halves[1]], 2, halves[0], False, True),
+            (closing[:], 2, halves[1], True, True),
+        ]
+        for dst, t, part, opens, closes in pieces:
+            product(dst, t, 0, part, opens, False)
         for part in first:
             nc.vector.tensor_copy(xg[1][:, part], xw[1][:].bitcast(U32).indirect(offs_t[:, entries(part)]))
-        product(head[:], 0, 1, first[0], False, True)
-        product(one[0][:], 1, 1, halves[0], False, True)
-        product(body[:, 0:P], 0, 1, first[1], False, False)
-        product(body[:, P : S - P], 0, 1, first[2], False, True)
-        product(one[1][:], 1, 1, halves[1], False, True)
-        for t in (3, 2):
-            product(late[t][:], t, 1, whole, False, True)
+        for dst, t, part, opens, closes in pieces:
+            product(dst, t, 1, part, False, closes)
 
         w2w = tile([P, 2 * N], U8, "rounded1")
         nc.sync.dma_start(out=w2w[:].bitcast(I32), in_=w2_words[0].bitcast(I32))
@@ -160,20 +160,25 @@ def tile_picked_unet_none_p_kernel(
         h0 = tile([P, S], F32, "h0")
         nc.scalar.copy(h0[:, 0:P], head[:])
         scalar_scatter(0, first[0], h0[:, 0:P])
-        h3 = [tile([P, HALF], F32, "h3%d" % b) for b in range(2)]
         nc.scalar.copy(h0[:, P:S], body[:])
-        nc.scalar.copy(h3[0][:], late[3][:, halves[0]])
+        h3 = [tile([P, HALF], F32, name) for name in ("h3", "h0")]
+        nc.scalar.copy(h3[0][:], last[:, halves[0]])
         scalar_scatter(0, slice(P, S), h0[:, P:S])
-        h1 = tile([P, S], F32, "h1")
-        for b in range(2):
-            nc.vector.tensor_copy(h1[:, halves[b]], one[b][:])
-        h2 = tile([P, S], F32, "h2")
-        nc.vector.tensor_copy(h2[:], late[2][:])
-        vector_scatter(1, whole, h1[:])
+        scalar_scatter(3, halves[0], h3[0][:])
+        nc.scalar.copy(h3[1][:], last[:, halves[1]])
+        h1 = tile([P, HALF], F32, "h1")
+        nc.vector.tensor_copy(h1[:], opening[:])
+        vector_scatter(1, halves[0], h1[:])
+        h2 = tile([P, HALF + S], F32, "h2")
+        nc.vector.tensor_copy(h2[:, 0:S], middle[:])
+        nc.vector.tensor_copy(h2[:, S : S + HALF], closing[:])
+        vector_scatter(1, halves[1], h2[:, 0:HALF])
+        vector_scatter(2, whole, h2[:, HALF : HALF + S])
+
         def turn(dst, src, start, stop):
             nc.tensor.matmul(dst, lhsT=src, rhs=ident[:], is_transpose=True, start=start, stop=stop)
 
-        def turned_sums(u, name):
+        def turned_sums(u, name, engine):
             sums = ps.tile([P, 2, 2, P], F32, name=name)
             for src, opens in ((skip_t, True), (up, False)):
                 for e in range(2):
@@ -181,60 +186,53 @@ def tile_picked_unet_none_p_kernel(
                         block = src[2 * u + e][:, TURNED + P * i : TURNED + P * (i + 1)]
                         turn(sums[:, i, e, :], block, opens and e + i == 0, not opens and e + i == 2)
             words = tile([P, 2, P], F32, "turned%d" % u)
-            nc.scalar.copy(words[:].bitcast(BF16).rearrange("p i (q e) -> p i q e", e=2), sums[:].rearrange("p i e q -> p i q e"))
+            copy_on[engine](words[:].bitcast(BF16).rearrange("p i (q e) -> p i q e", e=2), sums[:].rearrange("p i e q -> p i q e"))
             return words
 
-        scalar_scatter(3, halves[0], h3[0][:])
-        nc.scalar.copy(h3[1][:], late[3][:, halves[1]])
-        turned = [turned_sums(0, "b6")]
+        turned = [turned_sums(0, "b6", "scalar")]
         scalar_scatter(3, halves[1], h3[1][:])
-        vector_scatter(2, whole, h2[:])
-        turned.append(turned_sums(1, "b7"))
+        turned.append(turned_sums(1, "b7", "scalar"))
         back = ps.tile([P, 2, 2, P], F32, name="b7")
         for i in range(2):
             for u in range(2):
                 turn(back[:, i, u, :], turned[u][:, i, :], True, True)
 
-        spans = [slice(0, SIDE), slice(SIDE, TURNED)]
-        pairs = [tile([P, 2, span.stop - span.start, 2], BF16, "pairs%d" % s) for s, span in enumerate(spans)]
+        pairs = [tile([P, 2, CHUNK, 2], BF16, "pairs%d" % d) for d in range(3)]
 
-        def add_skip(engine, t, s):
-            engine.tensor_tensor(pairs[s][:, t // 2, :, t % 2], up[t][:, spans[s]], skip_t[t][:, spans[s]], ADD)
+        def add_skip(engine, t, d):
+            span = slice(CHUNK * d, CHUNK * (d + 1))
+            engine.tensor_tensor(pairs[d][:, t // 2, :, t % 2], up[t][:, span], skip_t[t][:, span], ADD)
 
         for t in range(2):
-            for s in range(2):
-                add_skip(nc.gpsimd, t, s)
-        for s in range(2):
-            for t in (2, 3):
-                add_skip(nc.vector, t, s)
+            for d in range(3):
+                add_skip(nc.gpsimd, t, d)
+        for t, d in ((2, 0), (2, 1), (3, 0), (2, 2), (3, 1), (3, 2)):
+            add_skip(nc.vector, t, d)
 
         woven = {}
 
         def weave(d, engine):
             woven[d] = tile([P, CHUNK * PACK], BF16, "woven%d" % d)
-            words = pairs[d // 2][:].rearrange("p u v e -> p u (v e)").bitcast(F32)
-            copy_on[engine](
-                woven[d][:].bitcast(F32).rearrange("p (v u) -> p v u", u=2),
-                words[:, :, CHUNK * (d % 2) : CHUNK * (d % 2 + 1)].rearrange("p u v -> p v u"),
-            )
+            words = pairs[d][:].rearrange("p u v e -> p u (v e)").bitcast(F32)
+            copy_on[engine](woven[d][:].bitcast(F32).rearrange("p (v u) -> p v u", u=2), words.rearrange("p u v -> p v u"))
 
         weave(0, "scalar")
-        woven[3] = tile([P, CHUNK * PACK], BF16, "woven3")
-        nc.scalar.copy(woven[3][:].bitcast(F32).rearrange("p (i v u) -> p i v u", i=2, u=2), back[:].rearrange("p i u v -> p i v u"))
         weave(1, "scalar")
+        woven[3] = tile([P, CHUNK * PACK], BF16, "pairs0")
+        nc.scalar.copy(woven[3][:].bitcast(F32).rearrange("p (i v u) -> p i v u", i=2, u=2), back[:].rearrange("p i u v -> p i v u"))
         weave(2, "vector")
 
         accs = {}
-        for d in (3, 2, 0, 1):
+        for d in range(4):
             zc = tile([P, CHUNK], U32, "zc%d" % d)
-            zs = tile([P, CHUNK], U8, ("zs0", "zs1", "zs2", "pairs1")[d])
+            zs = tile([P, CHUNK], U8, ("zs0", "zs1", "zs2", "woven0")[d])
             nc.vector.quantize_mx(out=zc[:].bitcast(FP8X4), scales=zs[:], in_=woven[d][:])
             accs[d] = ps.tile([P, CHUNK], F32, name="b%d" % d)
             nc.tensor.matmul_mx(
                 out=accs[d][:], lhsT=w2w[:].bitcast(FP4X4), lhsT_scale=w2s[:],
                 rhs=zc[:].bitcast(FP8X4), rhs_scale=zs[:], start=True, stop=True,
             )
-        for d, engine in ((3, "scalar"), (2, "scalar"), (0, "scalar"), (1, "vector")):
-            res = tile([P, CHUNK], F32, ("res0", "res1", "res2", "pairs0")[d])
+        for d, engine in ((0, "scalar"), (1, "scalar"), (2, "scalar"), (3, "vector")):
+            res = tile([P, CHUNK], F32, ("turned1", "res1", "res2", "res3")[d])
             copy_on[engine](res[:], accs[d][:])
             nc.sync.dma_start(out=out[:, CHUNK * d : CHUNK * (d + 1)], in_=res[:])

@@ -197,42 +197,48 @@ def tile_picked_unet_none_p_kernel(
             for u in range(2):
                 turn(back[:, i, u, :], turned[u][:, i, :], True, True)
 
-        pairs = [tile([P, 2, CHUNK, 2], BF16, "pairs%d" % d) for d in range(3)]
+        spans = [slice(0, CHUNK), slice(CHUNK, TURNED)]
+        planes = [tile([P, PACK, span.stop - span.start], BF16, "planes%d" % s) for s, span in enumerate(spans)]
 
-        def add_skip(engine, t, d):
-            span = slice(CHUNK * d, CHUNK * (d + 1))
-            engine.tensor_tensor(pairs[d][:, t // 2, :, t % 2], up[t][:, span], skip_t[t][:, span], ADD)
+        def add_skip(engine, t, s):
+            engine.tensor_tensor(planes[s][:, t, :], up[t][:, spans[s]], skip_t[t][:, spans[s]], ADD)
 
         for t in range(2):
-            for d in range(3):
-                add_skip(nc.gpsimd, t, d)
-        for t, d in ((2, 0), (2, 1), (3, 0), (2, 2), (3, 1), (3, 2)):
-            add_skip(nc.vector, t, d)
+            for s in range(2):
+                add_skip(nc.gpsimd, t, s)
+        for s in range(2):
+            for t in (2, 3):
+                add_skip(nc.vector, t, s)
 
         woven = {}
 
         def weave(d, engine):
             woven[d] = tile([P, CHUNK * PACK], BF16, "woven%d" % d)
-            words = pairs[d][:].rearrange("p u v e -> p u (v e)").bitcast(F32)
-            copy_on[engine](woven[d][:].bitcast(F32).rearrange("p (v u) -> p v u", u=2), words.rearrange("p u v -> p v u"))
+            s = min(d, 1)
+            c0 = CHUNK * d - spans[s].start
+            run = {"scalar": 1, "vector": PACK}[engine]
+            copy_on[engine](
+                woven[d][:].rearrange("p (c i t) -> p c t i", i=run, t=PACK),
+                planes[s][:, :, c0 : c0 + CHUNK].rearrange("p t (c i) -> p c t i", i=run),
+            )
 
         weave(0, "scalar")
-        weave(1, "scalar")
-        woven[3] = tile([P, CHUNK * PACK], BF16, "pairs0")
+        woven[3] = tile([P, CHUNK * PACK], BF16, "planes0")
         nc.scalar.copy(woven[3][:].bitcast(F32).rearrange("p (i v u) -> p i v u", i=2, u=2), back[:].rearrange("p i u v -> p i v u"))
-        weave(2, "vector")
+        for d in (1, 2):
+            weave(d, "vector")
 
         accs = {}
-        for d in range(4):
+        for d in (1, 0, 2, 3):
             zc = tile([P, CHUNK], U32, "zc%d" % d)
-            zs = tile([P, CHUNK], U8, ("zs0", "zs1", "zs2", "woven0")[d])
+            zs = tile([P, CHUNK], U8, ("planes1", "zs1", "zs2", "woven1")[d])
             nc.vector.quantize_mx(out=zc[:].bitcast(FP8X4), scales=zs[:], in_=woven[d][:])
             accs[d] = ps.tile([P, CHUNK], F32, name="b%d" % d)
             nc.tensor.matmul_mx(
                 out=accs[d][:], lhsT=w2w[:].bitcast(FP4X4), lhsT_scale=w2s[:],
                 rhs=zc[:].bitcast(FP8X4), rhs_scale=zs[:], start=True, stop=True,
             )
-        for d, engine in ((0, "scalar"), (1, "scalar"), (2, "scalar"), (3, "vector")):
-            res = tile([P, CHUNK], F32, ("turned1", "res1", "res2", "res3")[d])
+        for d, engine in ((1, "scalar"), (0, "scalar"), (2, "scalar"), (3, "vector")):
+            res = tile([P, CHUNK], F32, "res%d" % d)
             copy_on[engine](res[:], accs[d][:])
             nc.sync.dma_start(out=out[:, CHUNK * d : CHUNK * (d + 1)], in_=res[:])

@@ -189,8 +189,8 @@ def tile_picked_unet_none_p_kernel(
             copy_on[engine](words[:].bitcast(BF16).rearrange("p i (q e) -> p i q e", e=2), sums[:].rearrange("p i e q -> p i q e"))
             return words
 
-        turned = [turned_sums(0, "b6", "scalar")]
         scalar_scatter(3, halves[1], h3[1][:])
+        turned = [turned_sums(0, "b6", "scalar")]
         turned.append(turned_sums(1, "b7", "scalar"))
         back = ps.tile([P, 2, 2, P], F32, name="b7")
         for i in range(2):
@@ -203,12 +203,10 @@ def tile_picked_unet_none_p_kernel(
         def add_skip(engine, t, s):
             engine.tensor_tensor(planes[s][:, t, :], up[t][:, spans[s]], skip_t[t][:, spans[s]], ADD)
 
-        for t in range(2):
-            for s in range(2):
-                add_skip(nc.gpsimd, t, s)
-        for s in range(2):
-            for t in (2, 3):
-                add_skip(nc.vector, t, s)
+        for t, s in ((0, 0), (0, 1), (1, 1)):
+            add_skip(nc.gpsimd, t, s)
+        for t, s in ((1, 0), (2, 0), (2, 1), (3, 1), (3, 0)):
+            add_skip(nc.vector, t, s)
 
         woven = {}
 

@@ -23,9 +23,7 @@ PACK = 4
 PASSES = K // (P * PACK)
 HALF = S // 2
 CHUNK = U // 4
-HP = P // 2
 TURNED = U - CHUNK
-ROW = PACK * T
 SHARE = 96
 
 
@@ -35,23 +33,18 @@ def tile_picked_unet_none_p_kernel(
     nc = tc.nc
     with ExitStack() as ctx:
         sb = ctx.enter_context(tc.tile_pool(name="sb", bufs=1))
-        shared = ctx.enter_context(tc.tile_pool(name="shared", bufs=1))
         ps = ctx.enter_context(tc.psum_pool(name="ps", bufs=1))
 
         def tile(shape, dtype, name):
             return sb.tile(shape, dtype, name=name, align_bytes=64)
 
-        def placed(shape, dtype, name, offset):
-            return shared.tile(shape, dtype, name=name, align_bytes=64, offset=offset)
-
         copy_on = {"scalar": nc.scalar.copy, "vector": nc.vector.tensor_copy}
 
         offs_t = sb.tile([P, S // 16], U16, name="offs_t")
         cell_t = sb.tile([P, S // 16], U16, name="cell_t")
-        xs = placed([P, T], U8, "xs", ROW - T // 2)
+        xs = tile([P, T], U8, "xs")
         xsm = tile([P, PASSES * S], U8, "xsm")
-        nc.gpsimd.memset(xs[32:HP, :].bitcast(I32), 0)
-        nc.gpsimd.memset(xs[HP:P, :].bitcast(I32), 0)
+        nc.gpsimd.memset(xs[:].bitcast(I32), 0)
         nc.gpsimd.memset(xsm[:].bitcast(I32), 0)
         up = [tile([P, U], F32, "up%d" % t) for t in range(PACK)]
         for t in range(2):
@@ -61,27 +54,27 @@ def tile_picked_unet_none_p_kernel(
         ident = tile([P, P], F32, "ident")
         make_identity(nc, ident[:])
 
-        nc.sync.dma_start(out=xs[0:32, :].bitcast(I32), in_=x_scales.rearrange("g q n -> q g n").bitcast(I32))
-        nc.sync.dma_start(offs_t[:], offs)
         w1_rows = w1.rearrange("(g p j) c -> g p j c", p=P, j=PACK)
-        w1raw = [tile([P, PACK, H], F32, "w1raw0")]
+        w1raw = [tile([P, PACK, H], F32, "w1raw%d" % g) for g in range(PASSES)]
         xw = []
 
-        def load_x(g, dst):
-            xw.append(dst)
+        def load_x(g, name):
+            xw.append(tile([P, T], I32, name))
             nc.sync.dma_start(out=xw[g][:], in_=x_words[g].rearrange("p n t -> p (n t)").bitcast(I32))
 
-        nc.sync.dma_start(out=w1raw[0][:], in_=w1_rows[0])
-        load_x(0, tile([P, T], I32, "xw0"))
-        nc.sync.dma_start(cell_t[:], cell)
+        nc.sync.dma_start(out=w1raw[0][:, 0:2, :], in_=w1_rows[0, :, 0:2, :])
+        nc.sync.dma_start(out=xs[0:P:4, :].bitcast(I32), in_=x_scales.rearrange("g q n -> q g n").bitcast(I32))
+        nc.sync.dma_start(offs_t[:], offs)
+        nc.sync.dma_start(out=w1raw[0][:, 2:PACK, :], in_=w1_rows[0, :, 2:PACK, :])
+        load_x(0, "xw0")
+        nc.sync.dma_start(out=w1raw[1][:], in_=w1_rows[1])
         xsg = tile([P, S], U8, "xsg")
         nc.vector.tensor_copy(xsg[:], xs[:].indirect(offs_t[:]))
         for q in range(4):
             rows = xsm[32 * q : 32 * q + 4, :].bitcast(I32).rearrange("r (g n) -> r g n", g=PASSES)
-            nc.sync.dma_start(out=rows, in_=xsg[8 * q : 8 * q + 8, :].bitcast(I32))
-        w1raw.append(placed([P, PACK, H], F32, "w1raw1", 0))
-        nc.sync.dma_start(out=w1raw[1][:], in_=w1_rows[1])
-        load_x(1, placed([P, T], I32, "xw1", ROW))
+            nc.sync.dma_start(out=rows, in_=xsg[32 * q : 32 * (q + 1) : 4, :].bitcast(I32))
+        load_x(1, "xs")
+        nc.sync.dma_start(cell_t[:], cell)
 
         xg = [tile([P, S], U32, "xg%d" % g) for g in range(PASSES)]
         codes, scales = [], []
@@ -203,9 +196,9 @@ def tile_picked_unet_none_p_kernel(
         def add_skip(engine, t, s):
             engine.tensor_tensor(planes[s][:, t, :], up[t][:, spans[s]], skip_t[t][:, spans[s]], ADD)
 
-        for t, s in ((0, 0), (0, 1), (1, 1)):
+        for t, s in ((0, 0), (0, 1), (1, 1), (1, 0)):
             add_skip(nc.gpsimd, t, s)
-        for t, s in ((1, 0), (2, 0), (2, 1), (3, 1), (3, 0)):
+        for t, s in ((2, 1), (2, 0), (3, 1), (3, 0)):
             add_skip(nc.vector, t, s)
 
         woven = {}

@@ -24,6 +24,7 @@ PASSES = K // (P * PACK)
 HALF = S // 2
 CHUNK = U // 4
 TURNED = U - CHUNK
+MOST = S - P
 SHARE = 96
 
 
@@ -99,7 +100,6 @@ def tile_picked_unet_none_p_kernel(
             nc.sync.dma_start(out=both[:], in_=skip_rows[:, 2 * u : 2 * u + 2, :])
             skip_t.extend([both[:, 0, :], both[:, 1, :]])
 
-        whole = slice(0, S)
         halves = [slice(0, HALF), slice(HALF, S)]
         first = [slice(0, P), slice(P, HALF), slice(HALF, S)]
 
@@ -120,15 +120,19 @@ def tile_picked_unet_none_p_kernel(
         middle = ps.tile([P, S], F32, name="b3")
         closing = ps.tile([P, HALF], F32, name="b4")
         last = ps.tile([P, S], F32, name="b5")
+        third, fourth = slice(HALF, MOST), slice(MOST, S)
         pieces = [
             (head[:], 0, first[0], True, True),
             (opening[:], 1, halves[0], True, True),
             (body[:, 0:P], 0, first[1], True, False),
             (body[:, P : S - P], 0, first[2], False, True),
-            (last[:], 3, whole, True, True),
+            (last[:, halves[0]], 3, halves[0], True, False),
+            (last[:, third], 3, third, False, False),
+            (last[:, fourth], 2, fourth, False, True),
             (middle[:, halves[0]], 1, halves[1], True, False),
             (middle[:, halves[1]], 2, halves[0], False, True),
-            (closing[:], 2, halves[1], True, True),
+            (closing[:, 0:P], 2, third, True, False),
+            (closing[:, P:HALF], 3, fourth, False, True),
         ]
         for dst, t, part, opens, closes in pieces:
             product(dst, t, 0, part, opens, False)
@@ -154,11 +158,12 @@ def tile_picked_unet_none_p_kernel(
         nc.scalar.copy(h0[:, 0:P], head[:])
         scalar_scatter(0, first[0], h0[:, 0:P])
         nc.scalar.copy(h0[:, P:S], body[:])
-        h3 = [tile([P, HALF], F32, name) for name in ("h3", "h0")]
-        nc.scalar.copy(h3[0][:], last[:, halves[0]])
+        h3 = tile([P, MOST], F32, "h3")
+        nc.scalar.copy(h3[:], last[:, 0:MOST])
         scalar_scatter(0, slice(P, S), h0[:, P:S])
-        scalar_scatter(3, halves[0], h3[0][:])
-        nc.scalar.copy(h3[1][:], last[:, halves[1]])
+        scalar_scatter(3, slice(0, MOST), h3[:])
+        tail = tile([P, P], F32, "h0")
+        nc.scalar.copy(tail[:], last[:, fourth])
         h1 = tile([P, HALF], F32, "h1")
         nc.vector.tensor_copy(h1[:], opening[:])
         vector_scatter(1, halves[0], h1[:])
@@ -166,7 +171,8 @@ def tile_picked_unet_none_p_kernel(
         nc.vector.tensor_copy(h2[:, 0:S], middle[:])
         nc.vector.tensor_copy(h2[:, S : S + HALF], closing[:])
         vector_scatter(1, halves[1], h2[:, 0:HALF])
-        vector_scatter(2, whole, h2[:, HALF : HALF + S])
+        vector_scatter(2, slice(0, MOST), h2[:, HALF : HALF + MOST])
+        vector_scatter(3, fourth, h2[:, HALF + MOST : HALF + S])
 
         def turn(dst, src, start, stop):
             nc.tensor.matmul(dst, lhsT=src, rhs=ident[:], is_transpose=True, start=start, stop=stop)
@@ -182,39 +188,37 @@ def tile_picked_unet_none_p_kernel(
             copy_on[engine](words[:].bitcast(BF16).rearrange("p i (q e) -> p i q e", e=2), sums[:].rearrange("p i e q -> p i q e"))
             return words
 
-        scalar_scatter(3, halves[1], h3[1][:])
         turned = [turned_sums(0, "b6", "scalar")]
+        scalar_scatter(2, fourth, tail[:])
         turned.append(turned_sums(1, "b7", "scalar"))
         back = ps.tile([P, 2, 2, P], F32, name="b7")
         for i in range(2):
             for u in range(2):
                 turn(back[:, i, u, :], turned[u][:, i, :], True, True)
 
-        spans = [slice(0, CHUNK), slice(CHUNK, TURNED)]
-        planes = [tile([P, PACK, span.stop - span.start], BF16, "planes%d" % s) for s, span in enumerate(spans)]
+        planes = tile([P, PACK, TURNED], BF16, "planes")
 
-        def add_skip(engine, t, s):
-            engine.tensor_tensor(planes[s][:, t, :], up[t][:, spans[s]], skip_t[t][:, spans[s]], ADD)
+        def add_skip(engine, t, span):
+            engine.tensor_tensor(planes[:, t, span], up[t][:, span], skip_t[t][:, span], ADD)
 
-        for t, s in ((0, 0), (0, 1), (1, 1), (1, 0)):
-            add_skip(nc.gpsimd, t, s)
-        for t, s in ((2, 1), (2, 0), (3, 1), (3, 0)):
-            add_skip(nc.vector, t, s)
+        for t in range(2):
+            add_skip(nc.gpsimd, t, slice(0, TURNED))
+        add_skip(nc.vector, 3, slice(0, TURNED))
+        add_skip(nc.vector, 2, slice(CHUNK, TURNED))
+        add_skip(nc.vector, 2, slice(0, CHUNK))
 
         woven = {}
 
         def weave(d, engine):
             woven[d] = tile([P, CHUNK * PACK], BF16, "woven%d" % d)
-            s = min(d, 1)
-            c0 = CHUNK * d - spans[s].start
             run = {"scalar": 1, "vector": PACK}[engine]
             copy_on[engine](
                 woven[d][:].rearrange("p (c i t) -> p c t i", i=run, t=PACK),
-                planes[s][:, :, c0 : c0 + CHUNK].rearrange("p t (c i) -> p c t i", i=run),
+                planes[:, :, CHUNK * d : CHUNK * (d + 1)].rearrange("p t (c i) -> p c t i", i=run),
             )
 
         weave(0, "scalar")
-        woven[3] = tile([P, CHUNK * PACK], BF16, "planes0")
+        woven[3] = tile([P, CHUNK * PACK], BF16, "up2")
         nc.scalar.copy(woven[3][:].bitcast(F32).rearrange("p (i v u) -> p i v u", i=2, u=2), back[:].rearrange("p i u v -> p i v u"))
         for d in (1, 2):
             weave(d, "vector")
@@ -222,7 +226,7 @@ def tile_picked_unet_none_p_kernel(
         accs = {}
         for d in (1, 0, 2, 3):
             zc = tile([P, CHUNK], U32, "zc%d" % d)
-            zs = tile([P, CHUNK], U8, ("planes1", "zs1", "zs2", "woven1")[d])
+            zs = tile([P, CHUNK], U8, ("planes", "zs1", "zs2", "woven1")[d])
             nc.vector.quantize_mx(out=zc[:].bitcast(FP8X4), scales=zs[:], in_=woven[d][:])
             accs[d] = ps.tile([P, CHUNK], F32, name="b%d" % d)
             nc.tensor.matmul_mx(

@@ -223,17 +223,31 @@ def tile_picked_unet_none_p_kernel(
         for d in (1, 2):
             weave(d, "vector")
 
+        def product_w2(dst, words, plane):
+            nc.tensor.matmul_mx(
+                out=dst, lhsT=w2w[:].bitcast(FP4X4), lhsT_scale=w2s[:],
+                rhs=words.bitcast(FP8X4), rhs_scale=plane, start=True, stop=True,
+            )
+
         accs = {}
-        for d in (1, 0, 2, 3):
+        for d in (1, 0, 2):
             zc = tile([P, CHUNK], U32, "zc%d" % d)
-            zs = tile([P, CHUNK], U8, ("planes", "zs1", "zs2", "woven1")[d])
+            zs = tile([P, CHUNK], U8, ("planes", "zs1", "zs2")[d])
             nc.vector.quantize_mx(out=zc[:].bitcast(FP8X4), scales=zs[:], in_=woven[d][:])
             accs[d] = ps.tile([P, CHUNK], F32, name="b%d" % d)
-            nc.tensor.matmul_mx(
-                out=accs[d][:], lhsT=w2w[:].bitcast(FP4X4), lhsT_scale=w2s[:],
-                rhs=zc[:].bitcast(FP8X4), rhs_scale=zs[:], start=True, stop=True,
-            )
-        for d, engine in ((1, "scalar"), (0, "scalar"), (2, "scalar"), (3, "vector")):
+            product_w2(accs[d][:], zc[:], zs[:])
+        ends = []
+        for i in range(2):
+            zc = tile([P, P], U32, "zc3%d" % i)
+            zs = tile([P, P], U8, ("woven1", "zs31")[i])
+            nc.vector.quantize_mx(out=zc[:].bitcast(FP8X4), scales=zs[:], in_=woven[3][:, P * PACK * i : P * PACK * (i + 1)])
+            ends.append(ps.tile([P, P], F32, name="b%d" % (3 + i)))
+            product_w2(ends[i][:], zc[:], zs[:])
+        for d in (1, 0, 2):
             res = tile([P, CHUNK], F32, "res%d" % d)
-            copy_on[engine](res[:], accs[d][:])
+            nc.scalar.copy(res[:], accs[d][:])
             nc.sync.dma_start(out=out[:, CHUNK * d : CHUNK * (d + 1)], in_=res[:])
+        res = tile([P, CHUNK], F32, "res3")
+        for i in range(2):
+            nc.vector.tensor_copy(res[:, P * i : P * (i + 1)], ends[i][:])
+        nc.sync.dma_start(out=out[:, TURNED:U], in_=res[:])

from contextlib import ExitStack

import concourse.mybir as mybir
from concourse.masks import make_identity

K, T, S, H, N, U = 1024, 2048, 512, 512, 128, 1024
FLOPS = 2 * K * H * S + 2 * H * N * U

F32 = mybir.dt.float32
BF16 = mybir.dt.bfloat16
I32 = mybir.dt.int32
U32 = mybir.dt.uint32
U16 = mybir.dt.uint16
U8 = mybir.dt.uint8
FP8X4 = mybir.dt.float8_e4m3fn_x4
FP4X4 = mybir.dt.float4_e2m1fn_x4

COPY = mybir.ActivationFunctionType.Copy
ADD = mybir.AluOpType.add

P = 128
PACK = 4
PASSES = K // (P * PACK)
HALF = S // 2
CHUNK = U // 4
TURNED = U - CHUNK
MOST = S - P
SHARE = 96


def tile_picked_unet_none_p_kernel(
    tc, x_words, x_scales, w1, w2_words, w2_scales, skip, offs, cell, out
):
    nc = tc.nc
    with ExitStack() as ctx:
        sb = ctx.enter_context(tc.tile_pool(name="sb", bufs=1))
        ps = ctx.enter_context(tc.psum_pool(name="ps", bufs=1))

        def tile(shape, dtype, name):
            return sb.tile(shape, dtype, name=name, align_bytes=64)

        copy_on = {"scalar": nc.scalar.copy, "vector": nc.vector.tensor_copy}

        offs_t = sb.tile([P, S // 16], U16, name="offs_t")
        cell_t = sb.tile([P, S // 16], U16, name="cell_t")
        xs = tile([P, T], U8, "xs")
        xsm = tile([P, PASSES * S], U8, "xsm")
        nc.gpsimd.memset(xs[:].bitcast(I32), 0)
        nc.gpsimd.memset(xsm[:].bitcast(I32), 0)
        up = [tile([P, U], F32, "up%d" % t) for t in range(PACK)]
        for t in range(2):
            nc.gpsimd.memset(up[t][:], 0.0)
        for t in (2, 3):
            nc.scalar.copy(up[t][:], up[0][:])
        ident = tile([P, P], F32, "ident")
        make_identity(nc, ident[:])

        w1_rows = w1.rearrange("(g p j) c -> g p j c", p=P, j=PACK)
        w1raw = [tile([P, PACK, H], F32, "w1raw%d" % g) for g in range(PASSES)]
        xw = []

        def load_x(g, name):
            xw.append(tile([P, T], I32, name))
            nc.sync.dma_start(out=xw[g][:], in_=x_words[g].rearrange("p n t -> p (n t)").bitcast(I32))

        nc.sync.dma_start(out=w1raw[0][:, 0:2, :], in_=w1_rows[0, :, 0:2, :])
        nc.sync.dma_start(out=xs[0:P:4, :].bitcast(I32), in_=x_scales.rearrange("g q n -> q g n").bitcast(I32))
        nc.sync.dma_start(offs_t[:], offs)
        nc.sync.dma_start(out=w1raw[0][:, 2:PACK, :], in_=w1_rows[0, :, 2:PACK, :])
        load_x(0, "xw0")
        nc.sync.dma_start(out=w1raw[1][:], in_=w1_rows[1])
        xsg = tile([P, S], U8, "xsg")
        nc.vector.tensor_copy(xsg[:], xs[:].indirect(offs_t[:]))
        for q in range(4):
            rows = xsm[32 * q : 32 * q + 4, :].bitcast(I32).rearrange("r (g n) -> r g n", g=PASSES)
            nc.sync.dma_start(out=rows, in_=xsg[32 * q : 32 * (q + 1) : 4, :].bitcast(I32))
        load_x(1, "xs")
        nc.sync.dma_start(cell_t[:], cell)

        xg = [tile([P, S], U32, "xg%d" % g) for g in range(PASSES)]
        codes, scales = [], []
        for g in range(PASSES):
            rounded = tile([P, PACK * H], BF16, "rounded%d" % g)
            dst = rounded[:].rearrange("p (t m j) -> p m j t", t=PACK, j=PACK)
            src = w1raw[g][:].rearrange("p j (m t) -> p m j t", t=PACK)
            if g == 0:
                nc.vector.tensor_copy(dst, src)
            else:
                nc.vector.tensor_copy(xg[0][:], xw[0][:].bitcast(U32).indirect(offs_t[:]))
                nc.vector.tensor_copy(dst[:, 0:SHARE], src[:, 0:SHARE])
                nc.scalar.copy(dst[:, SHARE:P], src[:, SHARE:P])
            codes.append(tile([P, H], U32, "wc%d" % g))
            scales.append(tile([P, H], U8, "ws%d" % g))
            nc.vector.quantize_mx(out=codes[g][:].bitcast(FP8X4), scales=scales[g][:], in_=rounded[:])

        skip_rows = skip.rearrange("(q t) v -> q t v", t=PACK)
        skip_t = []
        for u in range(2):
            both = tile([P, 2, U], F32, ("w1raw0", "xw0")[u])
            nc.sync.dma_start(out=both[:], in_=skip_rows[:, 2 * u : 2 * u + 2, :])
            skip_t.extend([both[:, 0, :], both[:, 1, :]])

        halves = [slice(0, HALF), slice(HALF, S)]
        first = [slice(0, P), slice(P, HALF), slice(HALF, S)]

        def entries(part):
            return slice(part.start // 16, part.stop // 16)

        def product(dst, t, g, part, start, stop):
            cols = slice(P * t, P * (t + 1))
            nc.tensor.matmul_mx(
                out=dst, lhsT=codes[g][:, cols].bitcast(FP8X4), lhsT_scale=scales[g][:, cols],
                rhs=xg[g][:, part].bitcast(FP8X4), rhs_scale=xsm[:, S * g + part.start : S * g + part.stop],
                start=start, stop=stop,
            )

        head = ps.tile([P, P], F32, name="b0")
        body = ps.tile([P, S - P], F32, name="b1")
        opening = ps.tile([P, HALF], F32, name="b2")
        middle = ps.tile([P, S], F32, name="b3")
        closing = ps.tile([P, HALF], F32, name="b4")
        last = ps.tile([P, S], F32, name="b5")
        third, fourth = slice(HALF, MOST), slice(MOST, S)
        pieces = [
            (head[:], 0, first[0], True, True),
            (opening[:], 1, halves[0], True, True),
            (body[:, 0:P], 0, first[1], True, False),
            (body[:, P : S - P], 0, first[2], False, True),
            (last[:, halves[0]], 3, halves[0], True, False),
            (last[:, third], 3, third, False, False),
            (last[:, fourth], 2, fourth, False, True),
            (middle[:, halves[0]], 1, halves[1], True, False),
            (middle[:, halves[1]], 2, halves[0], False, True),
            (closing[:, 0:P], 2, third, True, False),
            (closing[:, P:HALF], 3, fourth, False, True),
        ]
        for dst, t, part, opens, closes in pieces:
            product(dst, t, 0, part, opens, False)
        for part in first:
            nc.vector.tensor_copy(xg[1][:, part], xw[1][:].bitcast(U32).indirect(offs_t[:, entries(part)]))
        for dst, t, part, opens, closes in pieces:
            product(dst, t, 1, part, False, closes)

        w2w = tile([P, 2 * N], U8, "rounded1")
        nc.sync.dma_start(out=w2w[:].bitcast(I32), in_=w2_words[0].bitcast(I32))
        w2s = tile([P, N], U8, "wc1")
        nc.gpsimd.memset(w2s[:].bitcast(I32), 0)
        for q in range(4):
            nc.sync.dma_start(out=w2s[32 * q : 32 * q + 4, :].bitcast(I32), in_=w2_scales[0].bitcast(I32)[4 * q : 4 * q + 4, :])

        def scalar_scatter(t, part, h):
            nc.scalar.activation(out=up[t][:].indirect(cell_t[:, entries(part)]), in_=h, func=COPY)

        def vector_scatter(t, part, h):
            nc.vector.tensor_copy(up[t][:].indirect(cell_t[:, entries(part)]), h)

        h0 = tile([P, S], F32, "h0")
        nc.scalar.copy(h0[:, 0:P], head[:])
        scalar_scatter(0, first[0], h0[:, 0:P])
        nc.scalar.copy(h0[:, P:S], body[:])
        h3 = tile([P, MOST], F32, "h3")
        nc.scalar.copy(h3[:], last[:, 0:MOST])
        scalar_scatter(0, slice(P, S), h0[:, P:S])
        scalar_scatter(3, slice(0, MOST), h3[:])
        tail = tile([P, P], F32, "h0")
        nc.scalar.copy(tail[:], last[:, fourth])
        h1 = tile([P, HALF], F32, "h1")
        nc.vector.tensor_copy(h1[:], opening[:])
        vector_scatter(1, halves[0], h1[:])
        h2 = tile([P, HALF + S], F32, "h2")
        nc.vector.tensor_copy(h2[:, 0:S], middle[:])
        nc.vector.tensor_copy(h2[:, S : S + HALF], closing[:])
        vector_scatter(1, halves[1], h2[:, 0:HALF])
        vector_scatter(2, slice(0, MOST), h2[:, HALF : HALF + MOST])
        vector_scatter(3, fourth, h2[:, HALF + MOST : HALF + S])

        def turn(dst, src, start, stop):
            nc.tensor.matmul(dst, lhsT=src, rhs=ident[:], is_transpose=True, start=start, stop=stop)

        def turned_sums(u, name, engine):
            sums = ps.tile([P, 2, 2, P], F32, name=name)
            for src, opens in ((skip_t, True), (up, False)):
                for e in range(2):
                    for i in range(2):
                        block = src[2 * u + e][:, TURNED + P * i : TURNED + P * (i + 1)]
                        turn(sums[:, i, e, :], block, opens and e + i == 0, not opens and e + i == 2)
            words = tile([P, 2, P], F32, "turned%d" % u)
            copy_on[engine](words[:].bitcast(BF16).rearrange("p i (q e) -> p i q e", e=2), sums[:].rearrange("p i e q -> p i q e"))
            return words

        turned = [turned_sums(0, "b6", "scalar")]
        scalar_scatter(2, fourth, tail[:])
        turned.append(turned_sums(1, "b7", "scalar"))
        back = ps.tile([P, 2, 2, P], F32, name="b7")
        for i in range(2):
            for u in range(2):
                turn(back[:, i, u, :], turned[u][:, i, :], True, True)

        planes = tile([P, PACK, TURNED], BF16, "planes")

        def add_skip(engine, t, span):
            engine.tensor_tensor(planes[:, t, span], up[t][:, span], skip_t[t][:, span], ADD)

        for t in range(2):
            add_skip(nc.gpsimd, t, slice(0, TURNED))
        add_skip(nc.vector, 3, slice(0, TURNED))
        add_skip(nc.vector, 2, slice(CHUNK, TURNED))
        add_skip(nc.vector, 2, slice(0, CHUNK))

        woven = {}

        def weave(d, engine):
            woven[d] = tile([P, CHUNK * PACK], BF16, "woven%d" % d)
            run = {"scalar": 1, "vector": PACK}[engine]
            copy_on[engine](
                woven[d][:].rearrange("p (c i t) -> p c t i", i=run, t=PACK),
                planes[:, :, CHUNK * d : CHUNK * (d + 1)].rearrange("p t (c i) -> p c t i", i=run),
            )

        weave(0, "scalar")
        woven[3] = tile([P, CHUNK * PACK], BF16, "up2")
        nc.scalar.copy(woven[3][:].bitcast(F32).rearrange("p (i v u) -> p i v u", i=2, u=2), back[:].rearrange("p i u v -> p i v u"))
        for d in (1, 2):
            weave(d, "vector")

        def product_w2(dst, words, plane):
            nc.tensor.matmul_mx(
                out=dst, lhsT=w2w[:].bitcast(FP4X4), lhsT_scale=w2s[:],
                rhs=words.bitcast(FP8X4), rhs_scale=plane, start=True, stop=True,
            )

        accs = {}
        for d in (1, 0, 2):
            zc = tile([P, CHUNK], U32, "zc%d" % d)
            zs = tile([P, CHUNK], U8, ("planes", "zs1", "zs2")[d])
            nc.vector.quantize_mx(out=zc[:].bitcast(FP8X4), scales=zs[:], in_=woven[d][:])
            accs[d] = ps.tile([P, CHUNK], F32, name="b%d" % d)
            product_w2(accs[d][:], zc[:], zs[:])
        ends = []
        for i in range(2):
            zc = tile([P, P], U32, "zc3%d" % i)
            zs = tile([P, P], U8, ("woven1", "zs31")[i])
            nc.vector.quantize_mx(out=zc[:].bitcast(FP8X4), scales=zs[:], in_=woven[3][:, P * PACK * i : P * PACK * (i + 1)])
            ends.append(ps.tile([P, P], F32, name="b%d" % (3 + i)))
            product_w2(ends[i][:], zc[:], zs[:])
        for d in (1, 0, 2):
            res = tile([P, CHUNK], F32, "res%d" % d)
            nc.scalar.copy(res[:], accs[d][:])
            nc.sync.dma_start(out=out[:, CHUNK * d : CHUNK * (d + 1)], in_=res[:])
        res = tile([P, CHUNK], F32, "res3")
        for i in range(2):
            nc.vector.tensor_copy(res[:, P * i : P * (i + 1)], ends[i][:])
        nc.sync.dma_start(out=out[:, TURNED:U], in_=res[:])
